import numpy as np
import ml_dtypes


def mxq(x, axis, fmt="e4m3"):
    dtype, down = {"e4m3": (ml_dtypes.float8_e4m3fn, 7), "e5m2": (ml_dtypes.float8_e5m2, 14)}[fmt]
    v = np.moveaxis(np.asarray(x, np.float32).astype(ml_dtypes.bfloat16).astype(np.float64), axis, -1)
    blocks = v.reshape(v.shape[:-1] + (-1, 32))
    amax = np.abs(blocks).max(-1, keepdims=True)
    byte = np.maximum(np.where(amax > 0, np.frexp(amax)[1] - 1 + 127, 0) - down, 1)
    scale = np.exp2(byte - 127.0)
    codes = (blocks / scale).astype(np.float32).astype(dtype).astype(np.float64)
    return np.moveaxis((codes * scale).reshape(v.shape), -1, axis)


WIDE = False


def mx_kscale(k):
    if not WIDE:
        return np.ones(k)
    levels = np.array([10, -10, 5, -5, 0])
    if k % 512:
        return np.exp2(np.random.permutation(np.resize(levels, k // 32))).repeat(32)
    a = np.empty((k // 512, 16))
    for p in range(k // 512):
        a[p, :8] = np.random.permutation(np.resize(levels, 8))
        for g in range(8):
            far = levels[np.abs(levels - a[p, g]) >= 10]
            a[p, g + 8] = far[np.random.randint(len(far))]
    return np.exp2(a.ravel()).repeat(32)


BF16 = ml_dtypes.bfloat16


def bf(x):
    return np.asarray(x, np.float32).astype(BF16)


def f64(x):
    return np.asarray(x).astype(np.float64)


B, C, G, J = 1024, 1536, 3, 512

SHARE = 0.35


def setup_inputs():
    s = mx_kscale(C)
    u = mx_kscale(B)
    v = mx_kscale(C)
    return {"student": bf(np.random.standard_normal((B, C)) * u[:, None] * v),
            "teacher": bf(np.random.standard_normal((B, C)) * u[:, None] * s),
            "confusion": bf(SHARE * np.random.standard_normal((C, C)) / np.sqrt(C) / s[:, None] * v),
            "affinity": bf(SHARE * np.random.standard_normal((B, B)) / np.sqrt(B) / u),
            "keep": bf((1 + 0.1 * np.random.standard_normal(B)) / u),
            "within": bf(SHARE * np.random.standard_normal((C, J)) / np.sqrt(J) / v[:, None]),
            "gain": bf((1 + 0.1 * np.random.standard_normal(C)) / v)}


def reference(student, teacher, confusion, affinity, keep, within, gain):
    d1 = mxq(f64(teacher), 1, "e4m3") @ mxq(f64(confusion), 0, "e4m3")
    z1 = f64(student) + d1
    d2 = mxq(f64(affinity), 1, "e4m3") @ mxq(z1, 0, "e4m3")
    z2 = f64(keep)[:, None] * z1 + d2
    zq = mxq(z2, 1, "e4m3").reshape(B, G, J).swapaxes(0, 1)
    wq = mxq(f64(within), 0, "e4m3").reshape(G, J, J)
    d3 = zq @ wq
    return f64(gain) * z2 + d3.swapaxes(0, 1).reshape(B, C)

@@ -1,0 +1,462 @@
+from contextlib import ExitStack
+
+import concourse.mybir as mybir
+from concourse.masks import make_identity
+
+B, C, G, J = 1024, 1536, 3, 512
+P = 128
+K_PASS = 512
+FLOPS = 2 * B * C * C + 2 * B * B * C + 2 * B * C * J
+
+F32 = mybir.dt.float32
+BF16 = mybir.dt.bfloat16
+U32 = mybir.dt.uint32
+U8 = mybir.dt.uint8
+FP8X4 = mybir.dt.float8_e4m3fn_x4
+MULT = mybir.AluOpType.mult
+ADD = mybir.AluOpType.add
+
+LEAD = 1
+
+
+def tile_teacher_student_logits_t1_kernel(
+    tc, student, teacher, confusion, affinity, keep, within, gain, out
+):
+    nc = tc.nc
+    with ExitStack() as ctx:
+        raw = ctx.enter_context(tc.tile_pool(name="raw", bufs=13))
+        trow = ctx.enter_context(tc.tile_pool(name="trow", bufs=4))
+        const = ctx.enter_context(tc.tile_pool(name="const", bufs=1))
+        grp = ctx.enter_context(tc.tile_pool(name="grp", bufs=5))
+        zgrp = ctx.enter_context(tc.tile_pool(name="zgrp", bufs=2))
+        z2grp = ctx.enter_context(tc.tile_pool(name="z2grp", bufs=4))
+        z1pool = ctx.enter_context(tc.tile_pool(name="z1pool", bufs=4))
+        z2pool = ctx.enter_context(tc.tile_pool(name="z2pool", bufs=6))
+        gzpool = ctx.enter_context(tc.tile_pool(name="gzpool", bufs=6))
+        outpool = ctx.enter_context(tc.tile_pool(name="outpool", bufs=3))
+        cpool = ctx.enter_context(tc.tile_pool(name="cpool", bufs=2))
+        z2codes = ctx.enter_context(tc.tile_pool(name="z2codes", bufs=6))
+        keepc = ctx.enter_context(tc.tile_pool(name="keepc", bufs=1))
+        psum = ctx.enter_context(tc.psum_pool(name="psum", bufs=8))
+
+        teacher_v = teacher.rearrange("(g p t) k -> g p t k", p=P, t=4)
+        affinity_v = affinity.rearrange("(g p t) k -> g p t k", p=P, t=4)
+        student_v = student.rearrange("(g p t) c -> g p t c", p=P, t=4)
+        confusion_v = confusion.rearrange("(c p j) n -> c p j n", p=P, j=4)
+        within_v = within.rearrange("(h p j) n -> h p j n", p=P, j=4)
+        out_v = out.rearrange("(g p t) c -> g p t c", p=P, t=4)
+
+        ident = const.tile([P, P], F32, name="ident", tag="ident")
+        make_identity(nc, ident[:])
+        keep16 = const.tile([P, 2, 4], BF16, name="keep16", tag="keep16")
+        keep32 = const.tile([P, 2, 4], F32, name="keep32", tag="keep32")
+        gain_sb = const.tile([P, C], BF16, name="gain_sb", tag="gain_sb")
+
+        conf_raw = {}
+        stu_raw = {}
+        tea_raw = {}
+        aff_raw = {}
+        win_raw = {}
+
+        def raw_tile():
+            return raw.tile([P, 4, 512], BF16, name="rawt", tag="rawt", align_bytes=64)
+
+        def load_conf(h, c):
+            t = raw_tile()
+            nc.sync.dma_start(out=t[:], in_=confusion_v[c, :, :, h * 512 : (h + 1) * 512])
+            conf_raw[h, c] = t
+
+        def load_student(h, g):
+            t = raw_tile()
+            nc.sync.dma_start(out=t[:], in_=student_v[g, :, :, h * 512 : (h + 1) * 512])
+            stu_raw[h, g] = t
+
+        def load_teacher(g, q):
+            t = trow.tile([P, 2, C], BF16, name="teat", tag="teat", align_bytes=64)
+            nc.sync.dma_start(out=t[:], in_=teacher_v[g, :, 2 * q : 2 * q + 2, :])
+            tea_raw[g, q] = t
+
+        def load_affinity(g, q):
+            t = raw.tile([P, 2, B], BF16, name="rawt", tag="rawt", align_bytes=64)
+            nc.sync.dma_start(out=t[:], in_=affinity_v[g, :, 2 * q : 2 * q + 2, :])
+            aff_raw[g, q] = t
+
+        def load_within(h):
+            t = raw_tile()
+            nc.sync.dma_start(out=t[:], in_=within_v[h])
+            win_raw[h] = t
+
+        load_teacher(0, 0)
+        load_teacher(0, 1)
+        for c in range(3):
+            load_conf(0, c)
+        load_teacher(1, 0)
+        load_student(0, 0)
+        load_teacher(1, 1)
+        load_affinity(0, 0)
+        load_affinity(0, 1)
+        load_student(0, 1)
+        nc.sync.dma_start(out=keep16[:], in_=keep.rearrange("(g p t) -> p g t", p=P, t=4))
+        load_affinity(1, 0)
+        load_affinity(1, 1)
+        for c in range(3):
+            load_conf(1, c)
+        load_student(1, 0)
+        nc.sync.dma_start(out=gain_sb[:], in_=gain.partition_broadcast(P))
+        load_within(0)
+        load_student(1, 1)
+        for c in range(3):
+            load_conf(2, c)
+        load_student(2, 0)
+        load_within(1)
+        load_student(2, 1)
+        load_within(2)
+
+        conf_codes = {}
+        conf_scales = {}
+        tea_codes = {}
+        tea_scales = {}
+        aff_codes = {}
+        aff_scales = {}
+        win_codes = {}
+        win_scales = {}
+        z1_codes = {}
+        z1_scales = {}
+        z1_f32 = {}
+        z1_grp = {}
+        grouped_t = {}
+
+        def interleave(engine, key, src, parts=((0, 512),)):
+            if key not in grouped_t:
+                grouped_t[key] = grp.tile([P, 512, 4], BF16, name="grouped", tag="grouped", align_bytes=64)
+            dst = grouped_t[key]
+            for lo, hi in parts:
+                o = dst[:, lo:hi, :].rearrange("p (n i) t -> p n t i", i=4)
+                s = src[:, :, lo:hi].rearrange("p t (n i) -> p n t i", i=4)
+                if engine == "v":
+                    nc.vector.tensor_copy(out=o, in_=s)
+                elif engine == "s":
+                    nc.scalar.copy(out=o, in_=s)
+                else:
+                    nc.gpsimd.tensor_scalar(out=o, in0=s, scalar1=1.0, scalar2=0.0, op0=MULT, op1=ADD)
+
+        def quant_conf(h, c):
+            if h not in conf_codes:
+                conf_codes[h] = cpool.tile([P, 3, 512], U32, name="ccodes", tag="ccodes", align_bytes=64)
+                conf_scales[h] = cpool.tile([P, 3, 512], U8, name="cscales", tag="cscales", align_bytes=64)
+            nc.vector.quantize_mx(
+                out=conf_codes[h][:, c, :].bitcast(FP8X4),
+                scales=conf_scales[h][:, c, :],
+                in_=grouped_t["c", h, c][:].rearrange("p n t -> p (n t)"),
+            )
+
+        def quant_within(h):
+            win_codes[h] = cpool.tile([P, 512], U32, name="wcodes", tag="wcodes", align_bytes=64)
+            win_scales[h] = cpool.tile([P, 512], U8, name="wscales", tag="wscales", align_bytes=64)
+            nc.vector.quantize_mx(
+                out=win_codes[h][:].bitcast(FP8X4),
+                scales=win_scales[h][:],
+                in_=grouped_t["w", h][:].rearrange("p n t -> p (n t)"),
+            )
+
+        banks = {}
+
+        def turn(kind, g, q, c):
+            src = (tea_raw if kind == "t" else aff_raw)[g, q]
+            words = src[:].bitcast(F32)
+            bank = psum.tile([P, 2, 2, P], F32, name="bank", tag="bank")
+            for a in range(2):
+                for u in range(2):
+                    nc.tensor.transpose(bank[:, a, u, :], words[:, a, 256 * c + u : 256 * (c + 1) : 2], ident[:])
+            banks[kind, g, q, c] = bank
+
+        def turn_copy(kind, g, q, c):
+            dst = grp.tile([P, 256, 4], BF16, name="grouped", tag="grouped", align_bytes=64)
+            nc.scalar.copy(
+                out=dst[:].bitcast(F32).rearrange("p (a r) u -> p a r u", a=2),
+                in_=banks[kind, g, q, c][:].rearrange("p a u r -> p a r u"),
+            )
+            grouped_t[kind, g, q, c] = dst
+
+        def turn_quant(kind, g, q, c):
+            codes, scales, n = (tea_codes, tea_scales, 3) if kind == "t" else (aff_codes, aff_scales, 2)
+            if (g, q) not in codes:
+                codes[g, q] = keepc.tile([P, n, 256], U32, name=f"{kind}codes{g}{q}", tag=f"{kind}codes{g}{q}", align_bytes=64)
+                scales[g, q] = keepc.tile([P, n, 256], U8, name=f"{kind}scales{g}{q}", tag=f"{kind}scales{g}{q}", align_bytes=64)
+            nc.vector.quantize_mx(
+                out=codes[g, q][:, c, :].bitcast(FP8X4),
+                scales=scales[g, q][:, c, :],
+                in_=grouped_t[kind, g, q, c][:].rearrange("p n t -> p (n t)"),
+            )
+
+        def mm1(k, passes=(0, 1, 2)):
+            h, g, q = k // 4, k // 2 % 2, k % 2
+            for a in range(2):
+                if passes[0] == 0:
+                    banks["s1", k, a] = psum.tile([P, 512], F32, name="bank", tag="bank")
+            if len(passes) == 3:
+                order = [(a, c) for a in range(2) for c in passes]
+            else:
+                order = [(a, c) for c in passes for a in range(2)]
+            for a, c in order:
+                cols = slice(a * P, (a + 1) * P)
+                nc.tensor.matmul_mx(
+                    out=banks["s1", k, a][:],
+                    lhsT=tea_codes[g, q][:, c, cols].bitcast(FP8X4),
+                    lhsT_scale=tea_scales[g, q][:, c, cols],
+                    rhs=conf_codes[h][:, c, :].bitcast(FP8X4),
+                    rhs_scale=conf_scales[h][:, c, :],
+                    start=(c == 0),
+                    stop=(c == 2),
+                )
+
+        def add1(k):
+            h, g, q = k // 4, k // 2 % 2, k % 2
+            if (h, g) not in z1_f32:
+                z1_f32[h, g] = z1pool.tile([P, 4, 512], F32, name="z1", tag="z1", align_bytes=64)
+            for a in range(2):
+                t = 2 * q + a
+                nc.vector.tensor_tensor(
+                    out=z1_f32[h, g][:, t, :].rearrange("p (u m) -> p u m", u=4),
+                    in0=banks["s1", k, a][:].rearrange("p (m u) -> p u m", u=4),
+                    in1=stu_raw[h, g][:, t, :].rearrange("p (m u) -> p u m", u=4),
+                    op=ADD,
+                )
+
+        def z1_round(h, g, half):
+            if half == 0:
+                z1_grp[h, g] = zgrp.tile([P, 512, 4], BF16, name="zgrouped", tag="zgrouped", align_bytes=64)
+            cols = slice(half * 256, half * 256 + 256)
+            nc.scalar.copy(
+                out=z1_grp[h, g][:, cols, :].rearrange("p (n i) t -> p n t i", i=4),
+                in_=z1_f32[h, g][:, :, cols].rearrange("p t (n i) -> p n t i", i=4),
+            )
+
+        def z1_quant(h, g, half):
+            if half == 0:
+                z1_codes[h, g] = cpool.tile([P, 512], U32, name=f"zcodes{g}", tag=f"zcodes{g}", align_bytes=64)
+                z1_scales[h, g] = cpool.tile([P, 512], U8, name=f"zscales{g}", tag=f"zscales{g}", align_bytes=64)
+            cols = slice(half * 256, half * 256 + 256)
+            nc.vector.quantize_mx(
+                out=z1_codes[h, g][:, cols].bitcast(FP8X4),
+                scales=z1_scales[h, g][:, cols],
+                in_=z1_grp[h, g][:, cols, :].rearrange("p n t -> p (n t)"),
+            )
+
+        z2_f32 = {}
+        gz_f32 = {}
+        z2_grp = {}
+        z2_codes = {}
+        z2_scales = {}
+        outs = {}
+
+        def mm2(s):
+            h, g, q = s // 4, s // 2 % 2, s % 2
+            for a in range(2):
+                bank = psum.tile([P, 512], F32, name="bank", tag="bank")
+                banks["s2", s, a] = bank
+                cols = slice(a * P, (a + 1) * P)
+                for c in range(2):
+                    nc.tensor.matmul_mx(
+                        out=bank[:],
+                        lhsT=aff_codes[g, q][:, c, cols].bitcast(FP8X4),
+                        lhsT_scale=aff_scales[g, q][:, c, cols],
+                        rhs=z1_codes[h, c][:].bitcast(FP8X4),
+                        rhs_scale=z1_scales[h, c][:],
+                        start=(c == 0),
+                        stop=(c == 1),
+                    )
+
+        def add2(s):
+            h, g, q = s // 4, s // 2 % 2, s % 2
+            for a in range(2):
+                t = 2 * q + a
+                z2 = z2pool.tile([P, 512], F32, name="z2", tag="z2", align_bytes=64)
+                nc.vector.scalar_tensor_tensor(
+                    out=z2[:],
+                    in0=z1_f32[h, g][:, t, :],
+                    scalar=keep32[:, g, t : t + 1],
+                    in1=banks["s2", s, a][:],
+                    op0=MULT,
+                    op1=ADD,
+                )
+                z2_f32[s, a] = z2
+
+        def gain_mul(s):
+            h = s // 4
+            for a in range(2):
+                gz = gzpool.tile([P, 512], F32, name="gz", tag="gz", align_bytes=64)
+                nc.gpsimd.tensor_tensor(
+                    out=gz[:].rearrange("p (m u) -> p m u", u=4),
+                    in0=z2_f32[s, a][:].rearrange("p (u m) -> p m u", u=4),
+                    in1=gain_sb[:, h * 512 : (h + 1) * 512].rearrange("p (m u) -> p m u", u=4),
+                    op=MULT,
+                )
+                gz_f32[s, a] = gz
+
+        def turn2(s):
+            for a in range(2):
+                bank = psum.tile([P, 4, P], F32, name="bank", tag="bank")
+                banks["t2", s, a] = bank
+                for u in range(4):
+                    nc.tensor.transpose(bank[:, u, :], z2_f32[s, a][:, u * P : (u + 1) * P], ident[:])
+
+        def round2(s):
+            for a in range(2):
+                dst = z2grp.tile([P, P, 4], BF16, name="z2g", tag="z2g", align_bytes=64)
+                nc.scalar.copy(out=dst[:], in_=banks["t2", s, a][:].rearrange("p u n -> p n u"))
+                z2_grp[s, a] = dst
+
+        def quant2(s):
+            for a in range(2):
+                codes = z2codes.tile([P, P], U32, name="z2c", tag="z2c", align_bytes=64)
+                scales = z2codes.tile([P, P], U8, name="z2s", tag="z2s", align_bytes=64)
+                nc.vector.quantize_mx(
+                    out=codes[:].bitcast(FP8X4),
+                    scales=scales[:],
+                    in_=z2_grp[s, a][:].rearrange("p n t -> p (n t)"),
+                )
+                z2_codes[s, a] = codes
+                z2_scales[s, a] = scales
+
+        def mm3(s):
+            h = s // 4
+            for a in range(2):
+                bank = psum.tile([P, 512], F32, name="bank", tag="bank")
+                banks["s3", s, a] = bank
+                nc.tensor.matmul_mx(
+                    out=bank[:],
+                    lhsT=z2_codes[s, a][:].bitcast(FP8X4),
+                    lhsT_scale=z2_scales[s, a][:],
+                    rhs=win_codes[h][:].bitcast(FP8X4),
+                    rhs_scale=win_scales[h][:],
+                    start=True,
+                    stop=True,
+                )
+
+        def add3(s):
+            outs[s] = outpool.tile([P, 2, 512], F32, name="outt", tag="outt", align_bytes=64)
+            for a in range(2):
+                nc.vector.tensor_tensor(out=outs[s][:, a, :], in0=banks["s3", s, a][:], in1=gz_f32[s, a][:], op=ADD)
+
+        def store(s):
+            h, g, q = s // 4, s // 2 % 2, s % 2
+            nc.sync.dma_start(out=out_v[g, :, 2 * q : 2 * q + 2, h * 512 : (h + 1) * 512], in_=outs[s][:])
+
+        HB = ((0, 256), (256, 512))
+        HA = ((0, 256),)
+        HC = ((256, 512),)
+
+        def turns(kind, g, q):
+            for c in range(3 if kind == "t" else 2):
+                turn(kind, g, q, c)
+                turn_copy(kind, g, q, c)
+
+        def turn_quants(kind, g, q):
+            for c in range(3 if kind == "t" else 2):
+                turn_quant(kind, g, q, c)
+
+        turns("t", 0, 0)
+        turn_quants("t", 0, 0)
+        turns("t", 0, 1)
+        interleave("v", ("c", 0, 0), conf_raw[0, 0])
+        turn_quants("t", 0, 1)
+        quant_conf(0, 0)
+        mm1(0, (0,))
+        mm1(1, (0,))
+        interleave("v", ("c", 0, 1), conf_raw[0, 1], HA)
+        interleave("s", ("c", 0, 1), conf_raw[0, 1], HC)
+        interleave("v", ("c", 0, 2), conf_raw[0, 2], HA)
+        interleave("s", ("c", 0, 2), conf_raw[0, 2], HC)
+        quant_conf(0, 1)
+        mm1(0, (1,))
+        mm1(1, (1,))
+        quant_conf(0, 2)
+        turns("t", 1, 0)
+        mm1(0, (2,))
+        mm1(1, (2,))
+        turn_quants("t", 1, 0)
+        add1(0)
+        turns("t", 1, 1)
+        add1(1)
+        mm1(2)
+        turn_quants("t", 1, 1)
+        z1_round(0, 0, 0)
+        z1_round(0, 0, 1)
+        mm1(3)
+        add1(2)
+        z1_quant(0, 0, 0)
+        z1_quant(0, 0, 1)
+        turns("a", 0, 0)
+        turns("a", 0, 1)
+        turns("a", 1, 0)
+        add1(3)
+        z1_round(0, 1, 0)
+        z1_round(0, 1, 1)
+        turns("a", 1, 1)
+        turn_quants("a", 0, 0)
+        turn_quants("a", 0, 1)
+        nc.vector.tensor_copy(out=keep32[:], in_=keep16[:])
+        turn_quants("a", 1, 0)
+        z1_quant(0, 1, 0)
+        z1_quant(0, 1, 1)
+        interleave("v", ("c", 1, 0), conf_raw[1, 0])
+        interleave("s", ("c", 1, 1), conf_raw[1, 1], HB)
+        turn_quants("a", 1, 1)
+        quant_conf(1, 0)
+
+        s1_at = {0: [4], 1: [5], 2: [6, 7], 4: [8], 5: [9], 6: [10, 11]}
+        pre_s = {2: [("z1", 1, 0)], 3: [("z1", 1, 1)], 6: [("z1", 2, 0)], 7: [("z1", 2, 1)]}
+        side_s = {
+            0: [("c", 1, 2)],
+            1: [("w", 0), ("c", 2, 0)],
+            2: [("c", 2, 1)],
+            3: [("c", 2, 2)],
+            5: [("w", 1)],
+            7: [("w", 2)],
+        }
+        for s in range(14):
+            if s == 0:
+                interleave("s", ("c", 1, 2), conf_raw[1, 2], HC)
+                interleave("v", ("c", 1, 2), conf_raw[1, 2], HA)
+                quant_conf(1, 1)
+                quant_conf(1, 2)
+            ks = s1_at.get(s, [])
+            for item in pre_s.get(s, ()):
+                for half in range(2):
+                    z1_round(item[1], item[2], half)
+            if s < 12:
+                mm2(s)
+            if 1 <= s < 13:
+                turn2(s - 1)
+            if s >= 2:
+                mm3(s - 2)
+            for k in ks:
+                mm1(k)
+            if s < 12:
+                add2(s)
+                gain_mul(s)
+            if 1 <= s < 13:
+                round2(s - 1)
+            if s >= 2:
+                add3(s - 2)
+                store(s - 2)
+            for k in ks:
+                add1(k)
+            for item in pre_s.get(s, ()):
+                for half in range(2):
+                    z1_quant(item[1], item[2], half)
+            if s > 0:
+                for item in side_s.get(s, ()):
+                    if item[0] == "c":
+                        interleave("s", item, conf_raw[item[1], item[2]], HB)
+                    else:
+                        interleave("s", item, win_raw[item[1]], HB)
+            if 1 <= s < 13:
+                quant2(s - 1)
+            if s > 0:
+                for item in side_s.get(s, ()):
+                    if item[0] == "c":
+                        quant_conf(item[1], item[2])
+                    else:
+                        quant_within(item[1])

@@ -5,7 +5,6 @@ from concourse.masks import make_identity
 
 B, C, G, J = 1024, 1536, 3, 512
 P = 128
-K_PASS = 512
 FLOPS = 2 * B * C * C + 2 * B * B * C + 2 * B * C * J
 
 F32 = mybir.dt.float32
@@ -16,7 +15,11 @@ FP8X4 = mybir.dt.float8_e4m3fn_x4
 MULT = mybir.AluOpType.mult
 ADD = mybir.AluOpType.add
 
-LEAD = 1
+BLOCK_BYTES = 4 * 512 * 2
+TEACHER_BYTES = 2 * C * 2
+HALVES = (slice(0, 256), slice(256, 512))
+TURN_BANKS = 3
+SUM_BANKS = 5
 
 
 def tile_teacher_student_logits_t1_kernel(
@@ -24,439 +27,392 @@ def tile_teacher_student_logits_t1_kernel(
 ):
     nc = tc.nc
     with ExitStack() as ctx:
-        raw = ctx.enter_context(tc.tile_pool(name="raw", bufs=13))
-        trow = ctx.enter_context(tc.tile_pool(name="trow", bufs=4))
-        const = ctx.enter_context(tc.tile_pool(name="const", bufs=1))
-        grp = ctx.enter_context(tc.tile_pool(name="grp", bufs=5))
-        zgrp = ctx.enter_context(tc.tile_pool(name="zgrp", bufs=2))
-        z2grp = ctx.enter_context(tc.tile_pool(name="z2grp", bufs=4))
-        z1pool = ctx.enter_context(tc.tile_pool(name="z1pool", bufs=4))
-        z2pool = ctx.enter_context(tc.tile_pool(name="z2pool", bufs=6))
-        gzpool = ctx.enter_context(tc.tile_pool(name="gzpool", bufs=6))
-        outpool = ctx.enter_context(tc.tile_pool(name="outpool", bufs=3))
-        cpool = ctx.enter_context(tc.tile_pool(name="cpool", bufs=2))
-        z2codes = ctx.enter_context(tc.tile_pool(name="z2codes", bufs=6))
-        keepc = ctx.enter_context(tc.tile_pool(name="keepc", bufs=1))
-        psum = ctx.enter_context(tc.psum_pool(name="psum", bufs=8))
+        raw = ctx.enter_context(tc.tile_pool(name="raw", bufs=1))
+        sbuf = ctx.enter_context(tc.tile_pool(name="sbuf", bufs=1))
+        psum = ctx.enter_context(tc.psum_pool(name="psum", bufs=1))
+        ctx.enter_context(tc.manual_schedule())
+
+        counts = {}
+
+        def ring(pool, name, depth, shape, dtype):
+            n = counts.get(name, 0)
+            counts[name] = n + 1
+            tag = name + str(n % depth)
+            if pool is psum:
+                return pool.tile(shape, dtype, name=tag, tag=tag)
+            return pool.tile(shape, dtype, name=tag, tag=tag, align_bytes=64)
+
+        def turn_bank(shape):
+            return ring(psum, "turn", TURN_BANKS, shape, F32)
+
+        def sum_bank():
+            return ring(psum, "sum", SUM_BANKS, [P, 512], F32)
 
         teacher_v = teacher.rearrange("(g p t) k -> g p t k", p=P, t=4)
         affinity_v = affinity.rearrange("(g p t) k -> g p t k", p=P, t=4)
         student_v = student.rearrange("(g p t) c -> g p t c", p=P, t=4)
         confusion_v = confusion.rearrange("(c p j) n -> c p j n", p=P, j=4)
-        within_v = within.rearrange("(h p j) n -> h p j n", p=P, j=4)
+        within_v = within.rearrange("(h b t r) n -> h r b t n", b=64, t=4, r=2)
         out_v = out.rearrange("(g p t) c -> g p t c", p=P, t=4)
 
-        ident = const.tile([P, P], F32, name="ident", tag="ident")
-        make_identity(nc, ident[:])
-        keep16 = const.tile([P, 2, 4], BF16, name="keep16", tag="keep16")
-        keep32 = const.tile([P, 2, 4], F32, name="keep32", tag="keep32")
-        gain_sb = const.tile([P, C], BF16, name="gain_sb", tag="gain_sb")
+        loaded = {}
+        words = {}
+        grouped = {}
+        codes = {}
+        scales = {}
+        banks = {}
+        z1 = {}
+        z2 = {}
+        gained = {}
+        outs = {}
 
-        conf_raw = {}
-        stu_raw = {}
-        tea_raw = {}
-        aff_raw = {}
-        win_raw = {}
+        def raw_tile(key, shape, offset):
+            name = "raw_" + "_".join(str(x) for x in key)
+            loaded[key] = raw.tile(shape, BF16, name=name, tag=name, align_bytes=64, offset=offset)
+            return loaded[key]
 
-        def raw_tile():
-            return raw.tile([P, 4, 512], BF16, name="rawt", tag="rawt", align_bytes=64)
+        teacher_at = 0
+        first_at = 4 * TEACHER_BYTES
+        rest_at = first_at + 3 * BLOCK_BYTES
+        place = {
+            ("c", 0, 0): first_at,
+            ("c", 0, 1): first_at + BLOCK_BYTES,
+            ("c", 0, 2): first_at + 2 * BLOCK_BYTES,
+            ("s", 1, 0): first_at,
+            ("s", 1, 1): first_at + BLOCK_BYTES,
+            ("w", 1): first_at + 2 * BLOCK_BYTES,
+            ("c", 2, 0): teacher_at,
+            ("c", 2, 1): teacher_at + BLOCK_BYTES,
+            ("c", 2, 2): teacher_at + 2 * BLOCK_BYTES,
+            ("s", 2, 0): teacher_at + 3 * BLOCK_BYTES,
+            ("s", 2, 1): teacher_at + 4 * BLOCK_BYTES,
+            ("w", 2): teacher_at + 5 * BLOCK_BYTES,
+        }
+        own = [("s", 0, 0), ("s", 0, 1), ("w", 0), ("c", 1, 0), ("c", 1, 1), ("c", 1, 2)]
+        own.extend(("a", g, q) for g in range(2) for q in range(2))
+        for n, key in enumerate(own):
+            place[key] = rest_at + n * BLOCK_BYTES
 
-        def load_conf(h, c):
-            t = raw_tile()
+        def load_confusion(h, c):
+            t = raw_tile(("c", h, c), [P, 4, 512], place["c", h, c])
             nc.sync.dma_start(out=t[:], in_=confusion_v[c, :, :, h * 512 : (h + 1) * 512])
-            conf_raw[h, c] = t
 
         def load_student(h, g):
-            t = raw_tile()
+            t = raw_tile(("s", h, g), [P, 4, 512], place["s", h, g])
             nc.sync.dma_start(out=t[:], in_=student_v[g, :, :, h * 512 : (h + 1) * 512])
-            stu_raw[h, g] = t
 
-        def load_teacher(g, q):
-            t = trow.tile([P, 2, C], BF16, name="teat", tag="teat", align_bytes=64)
-            nc.sync.dma_start(out=t[:], in_=teacher_v[g, :, 2 * q : 2 * q + 2, :])
-            tea_raw[g, q] = t
+        def load_teacher(g, q, passes=(0, 1, 2)):
+            width = 512 * len(passes)
+            at = teacher_at + (2 * g + q) * TEACHER_BYTES + passes[0] * TEACHER_BYTES // 3
+            t = raw_tile(("t", g, q, passes[0]), [P, 2, width], at)
+            k0 = 512 * passes[0]
+            nc.sync.dma_start(out=t[:], in_=teacher_v[g, :, 2 * q : 2 * q + 2, k0 : k0 + width])
+            for c in passes:
+                words["t", g, q, c] = t[:].bitcast(F32)[:, :, 256 * (c - passes[0]) : 256 * (c - passes[0] + 1)]
 
         def load_affinity(g, q):
-            t = raw.tile([P, 2, B], BF16, name="rawt", tag="rawt", align_bytes=64)
+            t = raw_tile(("a", g, q), [P, 2, B], place["a", g, q])
             nc.sync.dma_start(out=t[:], in_=affinity_v[g, :, 2 * q : 2 * q + 2, :])
-            aff_raw[g, q] = t
+            for c in range(2):
+                words["a", g, q, c] = t[:].bitcast(F32)[:, :, 256 * c : 256 * (c + 1)]
 
         def load_within(h):
-            t = raw_tile()
-            nc.sync.dma_start(out=t[:], in_=within_v[h])
-            win_raw[h] = t
+            t = raw_tile(("w", h), [P, 4, 512], place["w", h])
+            for r in range(2):
+                nc.sync.dma_start(out=t[r:P:2], in_=within_v[h, r])
 
-        load_teacher(0, 0)
-        load_teacher(0, 1)
-        for c in range(3):
-            load_conf(0, c)
-        load_teacher(1, 0)
-        load_student(0, 0)
-        load_teacher(1, 1)
-        load_affinity(0, 0)
-        load_affinity(0, 1)
-        load_student(0, 1)
-        nc.sync.dma_start(out=keep16[:], in_=keep.rearrange("(g p t) -> p g t", p=P, t=4))
-        load_affinity(1, 0)
-        load_affinity(1, 1)
-        for c in range(3):
-            load_conf(1, c)
-        load_student(1, 0)
-        nc.sync.dma_start(out=gain_sb[:], in_=gain.partition_broadcast(P))
-        load_within(0)
-        load_student(1, 1)
-        for c in range(3):
-            load_conf(2, c)
-        load_student(2, 0)
-        load_within(1)
-        load_student(2, 1)
-        load_within(2)
+        ident = sbuf.tile([P, P], F32, name="ident", tag="ident")
+        keep_sb = sbuf.tile([P, 2, 4], BF16, name="keep_sb", tag="keep_sb")
+        gain_in = sbuf.tile([P, G, 4], BF16, name="gain_in", tag="gain_in")
+        gain_f32 = sbuf.tile([P, G, 4], F32, name="gain_f32", tag="gain_f32")
+        gain_sb = sbuf.tile([P, G, 512], BF16, name="gain_sb", tag="gain_sb", align_bytes=64)
 
-        conf_codes = {}
-        conf_scales = {}
-        tea_codes = {}
-        tea_scales = {}
-        aff_codes = {}
-        aff_scales = {}
-        win_codes = {}
-        win_scales = {}
-        z1_codes = {}
-        z1_scales = {}
-        z1_f32 = {}
-        z1_grp = {}
-        grouped_t = {}
-
-        def interleave(engine, key, src, parts=((0, 512),)):
-            if key not in grouped_t:
-                grouped_t[key] = grp.tile([P, 512, 4], BF16, name="grouped", tag="grouped", align_bytes=64)
-            dst = grouped_t[key]
-            for lo, hi in parts:
-                o = dst[:, lo:hi, :].rearrange("p (n i) t -> p n t i", i=4)
-                s = src[:, :, lo:hi].rearrange("p t (n i) -> p n t i", i=4)
-                if engine == "v":
-                    nc.vector.tensor_copy(out=o, in_=s)
-                elif engine == "s":
-                    nc.scalar.copy(out=o, in_=s)
-                else:
-                    nc.gpsimd.tensor_scalar(out=o, in0=s, scalar1=1.0, scalar2=0.0, op0=MULT, op1=ADD)
-
-        def quant_conf(h, c):
-            if h not in conf_codes:
-                conf_codes[h] = cpool.tile([P, 3, 512], U32, name="ccodes", tag="ccodes", align_bytes=64)
-                conf_scales[h] = cpool.tile([P, 3, 512], U8, name="cscales", tag="cscales", align_bytes=64)
-            nc.vector.quantize_mx(
-                out=conf_codes[h][:, c, :].bitcast(FP8X4),
-                scales=conf_scales[h][:, c, :],
-                in_=grouped_t["c", h, c][:].rearrange("p n t -> p (n t)"),
+        def spread_gain(h):
+            bank = turn_bank([P, 4, P])
+            for j in range(4):
+                nc.tensor.transpose(bank[:, j, :], gain_f32[:, h, j : j + 1].to_broadcast([P, P]), ident[:])
+            nc.scalar.copy(
+                out=gain_sb[:, h, :].rearrange("p (e i b r) -> p e i b r", e=2, i=2, r=2),
+                in_=bank[:].rearrange("p (i r) (b e) -> p e i b r", i=2, e=2),
             )
 
-        def quant_within(h):
-            win_codes[h] = cpool.tile([P, 512], U32, name="wcodes", tag="wcodes", align_bytes=64)
-            win_scales[h] = cpool.tile([P, 512], U8, name="wscales", tag="wscales", align_bytes=64)
-            nc.vector.quantize_mx(
-                out=win_codes[h][:].bitcast(FP8X4),
-                scales=win_scales[h][:],
-                in_=grouped_t["w", h][:].rearrange("p n t -> p (n t)"),
+        def copy_on(engine, o, s):
+            if engine == "vector":
+                nc.vector.tensor_copy(out=o, in_=s)
+            else:
+                nc.scalar.copy(out=o, in_=s)
+
+        def interleave(engine, key, half):
+            if key not in grouped:
+                grouped[key] = ring(sbuf, "grouped", 4, [P, 512, 4], BF16)
+            src = z1[key[1:]] if key[0] == "z1" else loaded[key]
+            cols = HALVES[half]
+            copy_on(
+                engine,
+                grouped[key][:, cols, :].rearrange("p (n i) t -> p n t i", i=4),
+                src[:, :, cols].rearrange("p t (n i) -> p n t i", i=4),
             )
 
-        banks = {}
+        depth = {"c": 6, "w": 2, "z1": 4, "t": 12, "a": 8, "z2": 4}
 
-        def turn(kind, g, q, c):
-            src = (tea_raw if kind == "t" else aff_raw)[g, q]
-            words = src[:].bitcast(F32)
-            bank = psum.tile([P, 2, 2, P], F32, name="bank", tag="bank")
+        def quantise(key, cols=None):
+            width = grouped[key].shape[1]
+            if key not in codes:
+                codes[key] = ring(sbuf, key[0] + "codes", depth[key[0]], [P, width], U32)
+                scales[key] = ring(sbuf, key[0] + "scales", depth[key[0]], [P, width], U8)
+            if cols is None:
+                cols = slice(0, width)
+            nc.vector.quantize_mx(
+                out=codes[key][:, cols].bitcast(FP8X4),
+                scales=scales[key][:, cols],
+                in_=grouped[key][:, cols, :].rearrange("p n t -> p (n t)"),
+            )
+
+        def turn(key):
+            bank = turn_bank([P, 2, 2, P])
             for a in range(2):
                 for u in range(2):
-                    nc.tensor.transpose(bank[:, a, u, :], words[:, a, 256 * c + u : 256 * (c + 1) : 2], ident[:])
-            banks[kind, g, q, c] = bank
+                    nc.tensor.transpose(bank[:, a, u, :], words[key][:, a, u:256:2], ident[:])
+            banks[key] = bank
 
-        def turn_copy(kind, g, q, c):
-            dst = grp.tile([P, 256, 4], BF16, name="grouped", tag="grouped", align_bytes=64)
+        def turn_out(key):
+            grouped[key] = ring(sbuf, "turned", 4, [P, 256, 4], BF16)
             nc.scalar.copy(
-                out=dst[:].bitcast(F32).rearrange("p (a r) u -> p a r u", a=2),
-                in_=banks[kind, g, q, c][:].rearrange("p a u r -> p a r u"),
-            )
-            grouped_t[kind, g, q, c] = dst
-
-        def turn_quant(kind, g, q, c):
-            codes, scales, n = (tea_codes, tea_scales, 3) if kind == "t" else (aff_codes, aff_scales, 2)
-            if (g, q) not in codes:
-                codes[g, q] = keepc.tile([P, n, 256], U32, name=f"{kind}codes{g}{q}", tag=f"{kind}codes{g}{q}", align_bytes=64)
-                scales[g, q] = keepc.tile([P, n, 256], U8, name=f"{kind}scales{g}{q}", tag=f"{kind}scales{g}{q}", align_bytes=64)
-            nc.vector.quantize_mx(
-                out=codes[g, q][:, c, :].bitcast(FP8X4),
-                scales=scales[g, q][:, c, :],
-                in_=grouped_t[kind, g, q, c][:].rearrange("p n t -> p (n t)"),
+                out=grouped[key][:].bitcast(F32).rearrange("p (a r) u -> p a r u", a=2),
+                in_=banks[key][:].rearrange("p a u r -> p a r u"),
             )
 
-        def mm1(k, passes=(0, 1, 2)):
-            h, g, q = k // 4, k // 2 % 2, k % 2
-            for a in range(2):
-                if passes[0] == 0:
-                    banks["s1", k, a] = psum.tile([P, 512], F32, name="bank", tag="bank")
-            if len(passes) == 3:
-                order = [(a, c) for a in range(2) for c in passes]
-            else:
-                order = [(a, c) for c in passes for a in range(2)]
-            for a, c in order:
-                cols = slice(a * P, (a + 1) * P)
-                nc.tensor.matmul_mx(
-                    out=banks["s1", k, a][:],
-                    lhsT=tea_codes[g, q][:, c, cols].bitcast(FP8X4),
-                    lhsT_scale=tea_scales[g, q][:, c, cols],
-                    rhs=conf_codes[h][:, c, :].bitcast(FP8X4),
-                    rhs_scale=conf_scales[h][:, c, :],
-                    start=(c == 0),
-                    stop=(c == 2),
-                )
+        def product(bank, left, cols, right, start, stop):
+            nc.tensor.matmul_mx(
+                out=bank[:],
+                lhsT=codes[left][:, cols].bitcast(FP8X4),
+                lhsT_scale=scales[left][:, cols],
+                rhs=codes[right][:].bitcast(FP8X4),
+                rhs_scale=scales[right][:],
+                start=start,
+                stop=stop,
+            )
 
-        def add1(k):
-            h, g, q = k // 4, k // 2 % 2, k % 2
-            if (h, g) not in z1_f32:
-                z1_f32[h, g] = z1pool.tile([P, 4, 512], F32, name="z1", tag="z1", align_bytes=64)
+        def pair(s):
+            return s // 4, s // 2 % 2, s % 2
+
+        def mm1(s, passes=(0, 1, 2)):
+            h, g, q = pair(s)
+            for a, c in [(a, c) for a in range(2) for c in passes]:
+                if c == 0:
+                    banks["z1", s, a] = sum_bank()
+                product(banks["z1", s, a], ("t", g, q, c), slice(a * P, (a + 1) * P), ("c", h, c), c == 0, c == 2)
+
+        def add1(s):
+            h, g, q = pair(s)
+            if q == 0:
+                z1[h, g] = ring(sbuf, "z1", 4, [P, 4, 512], F32)
             for a in range(2):
                 t = 2 * q + a
                 nc.vector.tensor_tensor(
-                    out=z1_f32[h, g][:, t, :].rearrange("p (u m) -> p u m", u=4),
-                    in0=banks["s1", k, a][:].rearrange("p (m u) -> p u m", u=4),
-                    in1=stu_raw[h, g][:, t, :].rearrange("p (m u) -> p u m", u=4),
+                    out=z1[h, g][:, t, :].rearrange("p (u b r) -> p b u r", u=4, r=2),
+                    in0=banks["z1", s, a][:].rearrange("p (b u r) -> p b u r", u=4, r=2),
+                    in1=loaded["s", h, g][:, t, :].rearrange("p (b u r) -> p b u r", u=4, r=2),
                     op=ADD,
                 )
 
-        def z1_round(h, g, half):
-            if half == 0:
-                z1_grp[h, g] = zgrp.tile([P, 512, 4], BF16, name="zgrouped", tag="zgrouped", align_bytes=64)
-            cols = slice(half * 256, half * 256 + 256)
-            nc.scalar.copy(
-                out=z1_grp[h, g][:, cols, :].rearrange("p (n i) t -> p n t i", i=4),
-                in_=z1_f32[h, g][:, :, cols].rearrange("p t (n i) -> p n t i", i=4),
-            )
-
-        def z1_quant(h, g, half):
-            if half == 0:
-                z1_codes[h, g] = cpool.tile([P, 512], U32, name=f"zcodes{g}", tag=f"zcodes{g}", align_bytes=64)
-                z1_scales[h, g] = cpool.tile([P, 512], U8, name=f"zscales{g}", tag=f"zscales{g}", align_bytes=64)
-            cols = slice(half * 256, half * 256 + 256)
-            nc.vector.quantize_mx(
-                out=z1_codes[h, g][:, cols].bitcast(FP8X4),
-                scales=z1_scales[h, g][:, cols],
-                in_=z1_grp[h, g][:, cols, :].rearrange("p n t -> p (n t)"),
-            )
-
-        z2_f32 = {}
-        gz_f32 = {}
-        z2_grp = {}
-        z2_codes = {}
-        z2_scales = {}
-        outs = {}
-
         def mm2(s):
-            h, g, q = s // 4, s // 2 % 2, s % 2
+            h, g, q = pair(s)
             for a in range(2):
-                bank = psum.tile([P, 512], F32, name="bank", tag="bank")
-                banks["s2", s, a] = bank
-                cols = slice(a * P, (a + 1) * P)
+                banks["z2", s, a] = sum_bank()
                 for c in range(2):
-                    nc.tensor.matmul_mx(
-                        out=bank[:],
-                        lhsT=aff_codes[g, q][:, c, cols].bitcast(FP8X4),
-                        lhsT_scale=aff_scales[g, q][:, c, cols],
-                        rhs=z1_codes[h, c][:].bitcast(FP8X4),
-                        rhs_scale=z1_scales[h, c][:],
-                        start=(c == 0),
-                        stop=(c == 1),
-                    )
+                    product(banks["z2", s, a], ("a", g, q, c), slice(a * P, (a + 1) * P), ("z1", h, c), c == 0, c == 1)
 
         def add2(s):
-            h, g, q = s // 4, s // 2 % 2, s % 2
+            h, g, q = pair(s)
             for a in range(2):
                 t = 2 * q + a
-                z2 = z2pool.tile([P, 512], F32, name="z2", tag="z2", align_bytes=64)
+                z2[s, a] = ring(sbuf, "z2", 4, [P, 512], F32)
                 nc.vector.scalar_tensor_tensor(
-                    out=z2[:],
-                    in0=z1_f32[h, g][:, t, :],
-                    scalar=keep32[:, g, t : t + 1],
-                    in1=banks["s2", s, a][:],
+                    out=z2[s, a][:],
+                    in0=z1[h, g][:, t, :],
+                    scalar=keep_sb[:, g, t : t + 1],
+                    in1=banks["z2", s, a][:],
                     op0=MULT,
                     op1=ADD,
                 )
-                z2_f32[s, a] = z2
 
         def gain_mul(s):
-            h = s // 4
             for a in range(2):
-                gz = gzpool.tile([P, 512], F32, name="gz", tag="gz", align_bytes=64)
-                nc.gpsimd.tensor_tensor(
-                    out=gz[:].rearrange("p (m u) -> p m u", u=4),
-                    in0=z2_f32[s, a][:].rearrange("p (u m) -> p m u", u=4),
-                    in1=gain_sb[:, h * 512 : (h + 1) * 512].rearrange("p (m u) -> p m u", u=4),
-                    op=MULT,
-                )
-                gz_f32[s, a] = gz
+                gained[s, a] = ring(sbuf, "gained", 4, [P, 512], F32)
+                nc.gpsimd.tensor_tensor(out=gained[s, a][:], in0=z2[s, a][:], in1=gain_sb[:, s // 4, :], op=MULT)
 
         def turn2(s):
             for a in range(2):
-                bank = psum.tile([P, 4, P], F32, name="bank", tag="bank")
-                banks["t2", s, a] = bank
+                bank = turn_bank([P, 4, P])
+                banks["z2t", s, a] = bank
                 for u in range(4):
-                    nc.tensor.transpose(bank[:, u, :], z2_f32[s, a][:, u * P : (u + 1) * P], ident[:])
+                    nc.tensor.transpose(bank[:, u, :], z2[s, a][:, u * P : (u + 1) * P], ident[:])
 
         def round2(s):
             for a in range(2):
-                dst = z2grp.tile([P, P, 4], BF16, name="z2g", tag="z2g", align_bytes=64)
-                nc.scalar.copy(out=dst[:], in_=banks["t2", s, a][:].rearrange("p u n -> p n u"))
-                z2_grp[s, a] = dst
+                grouped["z2", s, a] = ring(sbuf, "z2grouped", 4, [P, P, 4], BF16)
+                nc.scalar.copy(out=grouped["z2", s, a][:], in_=banks["z2t", s, a][:].rearrange("p u n -> p n u"))
 
         def quant2(s):
             for a in range(2):
-                codes = z2codes.tile([P, P], U32, name="z2c", tag="z2c", align_bytes=64)
-                scales = z2codes.tile([P, P], U8, name="z2s", tag="z2s", align_bytes=64)
-                nc.vector.quantize_mx(
-                    out=codes[:].bitcast(FP8X4),
-                    scales=scales[:],
-                    in_=z2_grp[s, a][:].rearrange("p n t -> p (n t)"),
-                )
-                z2_codes[s, a] = codes
-                z2_scales[s, a] = scales
+                quantise(("z2", s, a))
 
         def mm3(s):
-            h = s // 4
             for a in range(2):
-                bank = psum.tile([P, 512], F32, name="bank", tag="bank")
-                banks["s3", s, a] = bank
-                nc.tensor.matmul_mx(
-                    out=bank[:],
-                    lhsT=z2_codes[s, a][:].bitcast(FP8X4),
-                    lhsT_scale=z2_scales[s, a][:],
-                    rhs=win_codes[h][:].bitcast(FP8X4),
-                    rhs_scale=win_scales[h][:],
-                    start=True,
-                    stop=True,
-                )
+                banks["out", s, a] = sum_bank()
+                product(banks["out", s, a], ("z2", s, a), slice(0, P), ("w", s // 4), True, True)
 
         def add3(s):
-            outs[s] = outpool.tile([P, 2, 512], F32, name="outt", tag="outt", align_bytes=64)
+            h, g, q = pair(s)
+            outs[s] = ring(sbuf, "outs", 3, [P, 2, 512], F32)
             for a in range(2):
-                nc.vector.tensor_tensor(out=outs[s][:, a, :], in0=banks["s3", s, a][:], in1=gz_f32[s, a][:], op=ADD)
+                nc.vector.tensor_tensor(
+                    out=outs[s][:, a, :].rearrange("p (b u r) -> p b u r", u=4, r=2),
+                    in0=banks["out", s, a][:].rearrange("p (b u r) -> p b u r", u=4, r=2),
+                    in1=gained[s, a][:].rearrange("p (u b r) -> p b u r", u=4, r=2),
+                    op=ADD,
+                )
 
         def store(s):
-            h, g, q = s // 4, s // 2 % 2, s % 2
+            h, g, q = pair(s)
             nc.sync.dma_start(out=out_v[g, :, 2 * q : 2 * q + 2, h * 512 : (h + 1) * 512], in_=outs[s][:])
 
-        HB = ((0, 256), (256, 512))
-        HA = ((0, 256),)
-        HC = ((256, 512),)
+        def turn_both(*keys):
+            for key in keys:
+                turn(key)
+            for key in keys:
+                turn_out(key)
 
-        def turns(kind, g, q):
-            for c in range(3 if kind == "t" else 2):
-                turn(kind, g, q, c)
-                turn_copy(kind, g, q, c)
+        def quantise_all(*keys):
+            for key in keys:
+                quantise(key)
 
-        def turn_quants(kind, g, q):
-            for c in range(3 if kind == "t" else 2):
-                turn_quant(kind, g, q, c)
+        def both(engine, key):
+            for half in range(2):
+                interleave(engine, key, half)
 
-        turns("t", 0, 0)
-        turn_quants("t", 0, 0)
-        turns("t", 0, 1)
-        interleave("v", ("c", 0, 0), conf_raw[0, 0])
-        turn_quants("t", 0, 1)
-        quant_conf(0, 0)
+        def tea(i):
+            return ("t", i // 6, i // 3 % 2, i % 3)
+
+        def aff(g, q):
+            return ("a", g, q, 0), ("a", g, q, 1)
+
+        nc.sync.dma_start(out=gain_in[:], in_=gain.rearrange("(h p j) -> p h j", p=P, j=4))
+        load_confusion(0, 0)
+        load_teacher(0, 0, (0,))
+        load_teacher(0, 0, (1,))
+        load_confusion(0, 1)
+        load_teacher(0, 0, (2,))
+        load_teacher(0, 1)
+        load_confusion(0, 2)
+        load_teacher(1, 0)
+        load_student(0, 0)
+        load_teacher(1, 1)
+        load_student(0, 1)
+        load_affinity(0, 0)
+        nc.sync.dma_start(out=keep_sb[:], in_=keep.rearrange("(g p t) -> p g t", p=P, t=4))
+        load_confusion(1, 0)
+        load_affinity(0, 1)
+        load_confusion(1, 1)
+        load_confusion(1, 2)
+        load_within(0)
+        load_affinity(1, 0)
+        load_affinity(1, 1)
+        make_identity(nc, ident[:])
+
+        nc.scalar.copy(out=gain_f32[:], in_=gain_in[:])
+        spread_gain(0)
+        spread_gain(1)
+        both("vector", ("c", 0, 0))
+        turn_both(tea(0), tea(1))
+        quantise_all(("c", 0, 0), tea(0))
         mm1(0, (0,))
-        mm1(1, (0,))
-        interleave("v", ("c", 0, 1), conf_raw[0, 1], HA)
-        interleave("s", ("c", 0, 1), conf_raw[0, 1], HC)
-        interleave("v", ("c", 0, 2), conf_raw[0, 2], HA)
-        interleave("s", ("c", 0, 2), conf_raw[0, 2], HC)
-        quant_conf(0, 1)
+        both("vector", ("c", 0, 1))
+        turn_both(tea(2))
+        spread_gain(2)
+        quantise_all(tea(1), ("c", 0, 1), tea(2))
         mm1(0, (1,))
-        mm1(1, (1,))
-        quant_conf(0, 2)
-        turns("t", 1, 0)
+        turn_both(tea(3), tea(4), tea(5))
+        both("vector", ("c", 0, 2))
+        load_student(1, 0)
+        load_student(1, 1)
+        quantise_all(tea(3), tea(4), ("c", 0, 2), tea(5))
+        mm1(1, (0, 1))
+        turn_both(tea(6), tea(7))
         mm1(0, (2,))
         mm1(1, (2,))
-        turn_quants("t", 1, 0)
+        quantise_all(tea(6), tea(7))
         add1(0)
-        turns("t", 1, 1)
+        turn_both(tea(8), tea(9))
         add1(1)
-        mm1(2)
-        turn_quants("t", 1, 1)
-        z1_round(0, 0, 0)
-        z1_round(0, 0, 1)
+        mm1(2, (0, 1))
+        quantise_all(tea(8), tea(9))
+        interleave("scalar", ("z1", 0, 0), 0)
+        turn_both(tea(10), tea(11))
+        for c in range(3):
+            load_confusion(2, c)
+        load_within(1)
+        load_student(2, 0)
+        load_student(2, 1)
+        load_within(2)
+        mm1(2, (2,))
+        interleave("vector", ("c", 1, 0), 0)
+        quantise_all(tea(10), tea(11))
+        interleave("scalar", ("z1", 0, 0), 1)
         mm1(3)
         add1(2)
-        z1_quant(0, 0, 0)
-        z1_quant(0, 0, 1)
-        turns("a", 0, 0)
-        turns("a", 0, 1)
-        turns("a", 1, 0)
+        interleave("vector", ("c", 1, 0), 1)
+        quantise(("z1", 0, 0))
+        turn_both(*aff(0, 0))
         add1(3)
-        z1_round(0, 1, 0)
-        z1_round(0, 1, 1)
-        turns("a", 1, 1)
-        turn_quants("a", 0, 0)
-        turn_quants("a", 0, 1)
-        nc.vector.tensor_copy(out=keep32[:], in_=keep16[:])
-        turn_quants("a", 1, 0)
-        z1_quant(0, 1, 0)
-        z1_quant(0, 1, 1)
-        interleave("v", ("c", 1, 0), conf_raw[1, 0])
-        interleave("s", ("c", 1, 1), conf_raw[1, 1], HB)
-        turn_quants("a", 1, 1)
-        quant_conf(1, 0)
+        interleave("scalar", ("z1", 0, 1), 0)
+        interleave("vector", ("z1", 0, 1), 1)
+        quantise_all(*aff(0, 0))
+        quantise(("z1", 0, 1), HALVES[1])
+        quantise(("z1", 0, 1), HALVES[0])
+        turn_both(*aff(0, 1))
+        quantise(("c", 1, 0))
+        both("scalar", ("c", 1, 1))
 
-        s1_at = {0: [4], 1: [5], 2: [6, 7], 4: [8], 5: [9], 6: [10, 11]}
-        pre_s = {2: [("z1", 1, 0)], 3: [("z1", 1, 1)], 6: [("z1", 2, 0)], 7: [("z1", 2, 1)]}
-        side_s = {
-            0: [("c", 1, 2)],
-            1: [("w", 0), ("c", 2, 0)],
-            2: [("c", 2, 1)],
-            3: [("c", 2, 2)],
-            5: [("w", 1)],
-            7: [("w", 2)],
-        }
-        for s in range(14):
-            if s == 0:
-                interleave("s", ("c", 1, 2), conf_raw[1, 2], HC)
-                interleave("v", ("c", 1, 2), conf_raw[1, 2], HA)
-                quant_conf(1, 1)
-                quant_conf(1, 2)
-            ks = s1_at.get(s, [])
-            for item in pre_s.get(s, ()):
-                for half in range(2):
-                    z1_round(item[1], item[2], half)
+        first_pairs = {1: [4, 5], 2: [6, 7], 5: [8, 9], 6: [10, 11]}
+        before = {2: [("z1", 1, 0)], 3: [("z1", 1, 1)], 4: [("w", 1)], 6: [("z1", 2, 0)], 7: [("z1", 2, 1)]}
+        after = {1: [("c", 2, 0)], 2: [("c", 2, 1)], 3: [("c", 2, 2)], 5: [("w", 2)]}
+        pending = []
+        for s in range(13):
             if s < 12:
                 mm2(s)
-            if 1 <= s < 13:
-                turn2(s - 1)
-            if s >= 2:
-                mm3(s - 2)
-            for k in ks:
-                mm1(k)
-            if s < 12:
                 add2(s)
                 gain_mul(s)
-            if 1 <= s < 13:
-                round2(s - 1)
-            if s >= 2:
-                add3(s - 2)
-                store(s - 2)
-            for k in ks:
+            for key in before.get(s, []):
+                both("scalar", key)
+            for k in first_pairs.get(s, []):
+                mm1(k)
                 add1(k)
-            for item in pre_s.get(s, ()):
-                for half in range(2):
-                    z1_quant(item[1], item[2], half)
-            if s > 0:
-                for item in side_s.get(s, ()):
-                    if item[0] == "c":
-                        interleave("s", item, conf_raw[item[1], item[2]], HB)
-                    else:
-                        interleave("s", item, win_raw[item[1]], HB)
-            if 1 <= s < 13:
-                quant2(s - 1)
-            if s > 0:
-                for item in side_s.get(s, ()):
-                    if item[0] == "c":
-                        quant_conf(item[1], item[2])
-                    else:
-                        quant_within(item[1])
+            if s >= 1:
+                mm3(s - 1)
+                add3(s - 1)
+                store(s - 1)
+            quantise_all(*before.get(s, []))
+            quantise_all(*pending)
+            if s == 0:
+                turn_both(*aff(1, 0))
+                quantise_all(*aff(0, 1))
+                both("vector", ("c", 1, 2))
+                quantise_all(("c", 1, 1), ("c", 1, 2))
+            if s == 1:
+                quantise_all(*aff(1, 1))
+            if s < 12:
+                turn2(s)
+                round2(s)
+            if s == 0:
+                quantise_all(*aff(1, 0))
+            if s < 12:
+                quant2(s)
+            if s == 0:
+                both("scalar", ("w", 0))
+                quantise(("w", 0))
+                turn_both(*aff(1, 1))
+            pending = after.get(s, [])
+            for key in pending:
+                both("scalar", key)

@@ -64,7 +64,6 @@ def tile_teacher_student_logits_t1_kernel(
         z1 = {}
         z2 = {}
         gained = {}
-        outs = {}
 
         def raw_tile(key, shape, offset):
             name = "raw_" + "_".join(str(x) for x in key)
@@ -153,7 +152,7 @@ def tile_teacher_student_logits_t1_kernel(
                 src[:, :, cols].rearrange("p t (n i) -> p n t i", i=4),
             )
 
-        depth = {"c": 6, "w": 2, "z1": 4, "t": 12, "a": 8, "z2": 4}
+        depth = {"c": 6, "w": 2, "z1": 4, "t": 12, "a": 8, "z2": 6}
 
         def quantise(key, cols=None):
             width = grouped[key].shape[1]
@@ -216,67 +215,56 @@ def tile_teacher_student_logits_t1_kernel(
                     op=ADD,
                 )
 
-        def mm2(s):
-            h, g, q = pair(s)
-            for a in range(2):
-                banks["z2", s, a] = sum_bank()
-                for c in range(2):
-                    product(banks["z2", s, a], ("a", g, q, c), slice(a * P, (a + 1) * P), ("z1", h, c), c == 0, c == 1)
+        def tile(i):
+            return i // 8, i // 4 % 2, i % 4
 
-        def add2(s):
-            h, g, q = pair(s)
-            for a in range(2):
-                t = 2 * q + a
-                z2[s, a] = ring(sbuf, "z2", 4, [P, 512], F32)
-                nc.vector.scalar_tensor_tensor(
-                    out=z2[s, a][:],
-                    in0=z1[h, g][:, t, :],
-                    scalar=keep_sb[:, g, t : t + 1],
-                    in1=banks["z2", s, a][:],
-                    op0=MULT,
-                    op1=ADD,
-                )
+        def mm2(i):
+            h, g, t = tile(i)
+            banks["z2", i] = sum_bank()
+            cols = slice(t % 2 * P, (t % 2 + 1) * P)
+            for c in range(2):
+                product(banks["z2", i], ("a", g, t // 2, c), cols, ("z1", h, c), c == 0, c == 1)
 
-        def gain_mul(s):
-            for a in range(2):
-                gained[s, a] = ring(sbuf, "gained", 4, [P, 512], F32)
-                nc.gpsimd.tensor_tensor(out=gained[s, a][:], in0=z2[s, a][:], in1=gain_sb[:, s // 4, :], op=MULT)
+        def add2(i):
+            h, g, t = tile(i)
+            z2[i] = ring(sbuf, "z2", 4, [P, 512], F32)
+            nc.vector.scalar_tensor_tensor(
+                out=z2[i][:],
+                in0=z1[h, g][:, t, :],
+                scalar=keep_sb[:, g, t : t + 1],
+                in1=banks["z2", i][:],
+                op0=MULT,
+                op1=ADD,
+            )
 
-        def turn2(s):
-            for a in range(2):
-                bank = turn_bank([P, 4, P])
-                banks["z2t", s, a] = bank
-                for u in range(4):
-                    nc.tensor.transpose(bank[:, u, :], z2[s, a][:, u * P : (u + 1) * P], ident[:])
+        def gain_mul(i):
+            gained[i] = ring(sbuf, "gained", 7, [P, 512], F32)
+            nc.gpsimd.tensor_tensor(out=gained[i][:], in0=z2[i][:], in1=gain_sb[:, i // 8, :], op=MULT)
 
-        def round2(s):
-            for a in range(2):
-                grouped["z2", s, a] = ring(sbuf, "z2grouped", 4, [P, P, 4], BF16)
-                nc.scalar.copy(out=grouped["z2", s, a][:], in_=banks["z2t", s, a][:].rearrange("p u n -> p n u"))
+        def turn2(i):
+            bank = turn_bank([P, 4, P])
+            banks["z2t", i] = bank
+            for u in range(4):
+                nc.tensor.transpose(bank[:, u, :], z2[i][:, u * P : (u + 1) * P], ident[:])
 
-        def quant2(s):
-            for a in range(2):
-                quantise(("z2", s, a))
+        def round2(i):
+            grouped["z2", i] = ring(sbuf, "z2grouped", 4, [P, P, 4], BF16)
+            nc.scalar.copy(out=grouped["z2", i][:], in_=banks["z2t", i][:].rearrange("p u n -> p n u"))
 
-        def mm3(s):
-            for a in range(2):
-                banks["out", s, a] = sum_bank()
-                product(banks["out", s, a], ("z2", s, a), slice(0, P), ("w", s // 4), True, True)
+        def mm3(i):
+            banks["out", i] = sum_bank()
+            product(banks["out", i], ("z2", i), slice(0, P), ("w", i // 8), True, True)
 
-        def add3(s):
-            h, g, q = pair(s)
-            outs[s] = ring(sbuf, "outs", 3, [P, 2, 512], F32)
-            for a in range(2):
-                nc.vector.tensor_tensor(
-                    out=outs[s][:, a, :].rearrange("p (b u r) -> p b u r", u=4, r=2),
-                    in0=banks["out", s, a][:].rearrange("p (b u r) -> p b u r", u=4, r=2),
-                    in1=gained[s, a][:].rearrange("p (u b r) -> p b u r", u=4, r=2),
-                    op=ADD,
-                )
-
-        def store(s):
-            h, g, q = pair(s)
-            nc.sync.dma_start(out=out_v[g, :, 2 * q : 2 * q + 2, h * 512 : (h + 1) * 512], in_=outs[s][:])
+        def add3(i):
+            h, g, t = tile(i)
+            result = ring(sbuf, "outs", 6, [P, 512], F32)
+            nc.vector.tensor_tensor(
+                out=result[:].rearrange("p (b u r) -> p b u r", u=4, r=2),
+                in0=banks["out", i][:].rearrange("p (b u r) -> p b u r", u=4, r=2),
+                in1=gained[i][:].rearrange("p (u b r) -> p b u r", u=4, r=2),
+                op=ADD,
+            )
+            nc.sync.dma_start(out=out_v[g, :, t, h * 512 : (h + 1) * 512], in_=result[:])
 
         def turn_both(*keys):
             for key in keys:
@@ -292,63 +280,70 @@ def tile_teacher_student_logits_t1_kernel(
             for half in range(2):
                 interleave(engine, key, half)
 
+        def shared(key):
+            interleave("scalar", key, 0)
+            interleave("vector", key, 1)
+
         def tea(i):
             return ("t", i // 6, i // 3 % 2, i % 3)
 
         def aff(g, q):
             return ("a", g, q, 0), ("a", g, q, 1)
 
-        nc.sync.dma_start(out=gain_in[:], in_=gain.rearrange("(h p j) -> p h j", p=P, j=4))
         load_confusion(0, 0)
         load_teacher(0, 0, (0,))
+        nc.sync.dma_start(out=gain_in[:], in_=gain.rearrange("(h p j) -> p h j", p=P, j=4))
         load_teacher(0, 0, (1,))
         load_confusion(0, 1)
         load_teacher(0, 0, (2,))
         load_teacher(0, 1)
         load_confusion(0, 2)
+        load_confusion(1, 0)
         load_teacher(1, 0)
         load_student(0, 0)
+        load_confusion(1, 1)
         load_teacher(1, 1)
+        load_confusion(1, 2)
         load_student(0, 1)
         load_affinity(0, 0)
         nc.sync.dma_start(out=keep_sb[:], in_=keep.rearrange("(g p t) -> p g t", p=P, t=4))
-        load_confusion(1, 0)
         load_affinity(0, 1)
-        load_confusion(1, 1)
-        load_confusion(1, 2)
         load_within(0)
         load_affinity(1, 0)
-        load_affinity(1, 1)
         make_identity(nc, ident[:])
 
-        nc.scalar.copy(out=gain_f32[:], in_=gain_in[:])
-        spread_gain(0)
-        spread_gain(1)
         both("vector", ("c", 0, 0))
-        turn_both(tea(0), tea(1))
+        turn_both(tea(0))
+        nc.scalar.copy(out=gain_f32[:], in_=gain_in[:])
+        turn_both(tea(1))
         quantise_all(("c", 0, 0), tea(0))
         mm1(0, (0,))
-        both("vector", ("c", 0, 1))
+        shared(("c", 0, 1))
+        quantise(tea(1))
         turn_both(tea(2))
-        spread_gain(2)
-        quantise_all(tea(1), ("c", 0, 1), tea(2))
+        quantise_all(("c", 0, 1), tea(2))
         mm1(0, (1,))
-        turn_both(tea(3), tea(4), tea(5))
         both("vector", ("c", 0, 2))
+        turn_both(tea(3), tea(4))
         load_student(1, 0)
+        load_affinity(1, 1)
         load_student(1, 1)
-        quantise_all(tea(3), tea(4), ("c", 0, 2), tea(5))
-        mm1(1, (0, 1))
-        turn_both(tea(6), tea(7))
+        quantise_all(tea(3), ("c", 0, 2), tea(4))
+        turn_both(tea(5))
+        mm1(1, (0,))
         mm1(0, (2,))
-        mm1(1, (2,))
-        quantise_all(tea(6), tea(7))
+        both("vector", ("c", 1, 0))
+        quantise(tea(5))
+        turn_both(tea(6), tea(7))
+        mm1(1, (1, 2))
         add1(0)
+        quantise_all(("c", 1, 0), tea(6), tea(7))
+        both("scalar", ("c", 1, 1))
         turn_both(tea(8), tea(9))
         add1(1)
         mm1(2, (0, 1))
-        quantise_all(tea(8), tea(9))
-        interleave("scalar", ("z1", 0, 0), 0)
+        quantise_all(("c", 1, 1), tea(8), tea(9))
+        interleave("scalar", ("c", 1, 2), 0)
         turn_both(tea(10), tea(11))
         for c in range(3):
             load_confusion(2, c)
@@ -357,62 +352,96 @@ def tile_teacher_student_logits_t1_kernel(
         load_student(2, 1)
         load_within(2)
         mm1(2, (2,))
-        interleave("vector", ("c", 1, 0), 0)
+        interleave("scalar", ("c", 1, 2), 1)
         quantise_all(tea(10), tea(11))
-        interleave("scalar", ("z1", 0, 0), 1)
         mm1(3)
         add1(2)
-        interleave("vector", ("c", 1, 0), 1)
-        quantise(("z1", 0, 0))
+        both("scalar", ("z1", 0, 0))
+        quantise(("c", 1, 2))
         turn_both(*aff(0, 0))
         add1(3)
         interleave("scalar", ("z1", 0, 1), 0)
+        quantise(("z1", 0, 0))
         interleave("vector", ("z1", 0, 1), 1)
         quantise_all(*aff(0, 0))
         quantise(("z1", 0, 1), HALVES[1])
         quantise(("z1", 0, 1), HALVES[0])
         turn_both(*aff(0, 1))
-        quantise(("c", 1, 0))
-        both("scalar", ("c", 1, 1))
+        spread_gain(0)
+        quantise_all(*aff(0, 1))
+        both("scalar", ("w", 0))
 
-        first_pairs = {1: [4, 5], 2: [6, 7], 5: [8, 9], 6: [10, 11]}
-        before = {2: [("z1", 1, 0)], 3: [("z1", 1, 1)], 4: [("w", 1)], 6: [("z1", 2, 0)], 7: [("z1", 2, 1)]}
-        after = {1: [("c", 2, 0)], 2: [("c", 2, 1)], 3: [("c", 2, 2)], 5: [("w", 2)]}
-        pending = []
-        for s in range(13):
-            if s < 12:
-                mm2(s)
-                add2(s)
-                gain_mul(s)
-            for key in before.get(s, []):
+        interleaved = {
+            0: [("c", 2, 0)],
+            1: [("c", 2, 1)],
+            2: [("c", 2, 2), ("z1", 1, 0)],
+            4: [("w", 1)],
+            5: [("z1", 2, 0)],
+            6: [("w", 2)],
+        }
+        quantised = {
+            1: [*aff(1, 0), ("w", 0), ("c", 2, 0)],
+            2: [*aff(1, 1), ("c", 2, 1)],
+            3: [("c", 2, 2), ("z1", 1, 0)],
+            5: [("w", 1)],
+            6: [("z1", 2, 0)],
+            7: [("w", 2)],
+        }
+
+        def tiles(*numbers):
+            return [i for i in numbers if 0 <= i < 24]
+
+        def finish(i):
+            mm3(i)
+            add3(i)
+
+        for s in range(12):
+            for i in tiles(2 * s - 1):
+                gain_mul(i)
+            if s in (1, 2):
+                mm2(2 * s)
+                add2(2 * s)
+                gain_mul(2 * s)
+            if s < 8:
+                mm1(s + 4)
+                add1(s + 4)
+                if s % 4 == 3:
+                    interleave("scalar", ("z1", s // 4 + 1, 1), 0)
+            if s not in (1, 2):
+                if s <= 8:
+                    mm2(2 * s)
+                add2(2 * s)
+                gain_mul(2 * s)
+            for i in tiles(2 * s - 5, 2 * s - 4):
+                finish(i)
+            mm2(2 * s + 1)
+            add2(2 * s + 1)
+            if 8 <= s < 11:
+                mm2(2 * s + 2)
+            if s < 2:
+                turn_both(*aff(1, s))
+            for i in tiles(2 * s - 1, 2 * s):
+                turn2(i)
+                round2(i)
+            if s in (3, 7):
+                spread_gain(s // 4 + 1)
+            if s in (3, 7):
+                interleave("vector", ("z1", s // 4 + 1, 1), 1)
+            quantise_all(*quantised.get(s, []))
+            for i in tiles(2 * s - 3, 2 * s - 2):
+                quantise(("z2", i))
+            if s in (3, 7):
+                for cols in HALVES:
+                    quantise(("z1", s // 4 + 1, 1), cols)
+            for key in interleaved.get(s, []):
                 both("scalar", key)
-            for k in first_pairs.get(s, []):
-                mm1(k)
-                add1(k)
-            if s >= 1:
-                mm3(s - 1)
-                add3(s - 1)
-                store(s - 1)
-            quantise_all(*before.get(s, []))
-            quantise_all(*pending)
-            if s == 0:
-                turn_both(*aff(1, 0))
-                quantise_all(*aff(0, 1))
-                both("vector", ("c", 1, 2))
-                quantise_all(("c", 1, 1), ("c", 1, 2))
-            if s == 1:
-                quantise_all(*aff(1, 1))
-            if s < 12:
-                turn2(s)
-                round2(s)
-            if s == 0:
-                quantise_all(*aff(1, 0))
-            if s < 12:
-                quant2(s)
-            if s == 0:
-                both("scalar", ("w", 0))
-                quantise(("w", 0))
-                turn_both(*aff(1, 1))
-            pending = after.get(s, [])
-            for key in pending:
-                both("scalar", key)
+        quantise(("z2", 21))
+        gain_mul(23)
+        finish(19)
+        finish(20)
+        turn2(23)
+        round2(23)
+        finish(21)
+        quantise_all(("z2", 22), ("z2", 23))
+        finish(22)
+        finish(23)

@@ -109,6 +109,12 @@ def tile_teacher_student_logits_t1_kernel(
             for c in passes:
                 words["t", g, q, c] = t[:].bitcast(F32)[:, :, 256 * (c - passes[0]) : 256 * (c - passes[0] + 1)]
 
+        def load_teacher_pass(c):
+            t = raw_tile(("t", 0, "pass", c), [P, 4, 512], teacher_at + c * BLOCK_BYTES)
+            nc.sync.dma_start(out=t[:], in_=teacher_v[0, :, :, 512 * c : 512 * (c + 1)])
+            for q in range(2):
+                words["t", 0, q, c] = t[:].bitcast(F32)[:, 2 * q : 2 * q + 2, :]
+
         def load_affinity(g, q):
             t = raw_tile(("a", g, q), [P, 2, B], place["a", g, q])
             nc.sync.dma_start(out=t[:], in_=affinity_v[g, :, 2 * q : 2 * q + 2, :])
@@ -195,18 +201,21 @@ def tile_teacher_student_logits_t1_kernel(
         def pair(s):
             return s // 4, s // 2 % 2, s % 2
 
-        def mm1(s, passes=(0, 1, 2)):
+        def mm1(s, passes=(0, 1, 2), by_pass=False, tiles=(0, 1)):
             h, g, q = pair(s)
-            for a, c in [(a, c) for a in range(2) for c in passes]:
+            order = [(a, c) for a in tiles for c in passes]
+            if by_pass:
+                order = [(a, c) for c in passes for a in tiles]
+            for a, c in order:
                 if c == 0:
                     banks["z1", s, a] = sum_bank()
                 product(banks["z1", s, a], ("t", g, q, c), slice(a * P, (a + 1) * P), ("c", h, c), c == 0, c == 2)
 
-        def add1(s):
+        def add1(s, tiles=(0, 1)):
             h, g, q = pair(s)
-            if q == 0:
+            if (h, g) not in z1:
                 z1[h, g] = ring(sbuf, "z1", 4, [P, 4, 512], F32)
-            for a in range(2):
+            for a in tiles:
                 t = 2 * q + a
                 nc.vector.tensor_tensor(
                     out=z1[h, g][:, t, :].rearrange("p (u b r) -> p b u r", u=4, r=2),
@@ -290,9 +299,9 @@ def tile_teacher_student_logits_t1_kernel(
         def aff(g, q):
             return ("a", g, q, 0), ("a", g, q, 1)
 
+        nc.sync.dma_start(out=gain_in[:], in_=gain.rearrange("(h p j) -> p h j", p=P, j=4))
         load_confusion(0, 0)
         load_teacher(0, 0, (0,))
-        nc.sync.dma_start(out=gain_in[:], in_=gain.rearrange("(h p j) -> p h j", p=P, j=4))
         load_teacher(0, 0, (1,))
         load_confusion(0, 1)
         load_teacher(0, 0, (2,))
@@ -307,14 +316,13 @@ def tile_teacher_student_logits_t1_kernel(
         load_student(0, 1)
         load_affinity(0, 0)
         nc.sync.dma_start(out=keep_sb[:], in_=keep.rearrange("(g p t) -> p g t", p=P, t=4))
-        load_affinity(0, 1)
-        load_within(0)
-        load_affinity(1, 0)
         make_identity(nc, ident[:])
+        nc.scalar.copy(out=gain_f32[:], in_=gain_in[:])
+        for h in range(G):
+            spread_gain(h)
 
         both("vector", ("c", 0, 0))
         turn_both(tea(0))
-        nc.scalar.copy(out=gain_f32[:], in_=gain_in[:])
         turn_both(tea(1))
         quantise_all(("c", 0, 0), tea(0))
         mm1(0, (0,))
@@ -326,8 +334,8 @@ def tile_teacher_student_logits_t1_kernel(
         both("vector", ("c", 0, 2))
         turn_both(tea(3), tea(4))
         load_student(1, 0)
-        load_affinity(1, 1)
-        load_student(1, 1)
+        load_within(0)
+        load_affinity(0, 1)
         quantise_all(tea(3), ("c", 0, 2), tea(4))
         turn_both(tea(5))
         mm1(1, (0,))
@@ -343,49 +351,44 @@ def tile_teacher_student_logits_t1_kernel(
         add1(1)
         mm1(2, (0, 1))
         quantise_all(("c", 1, 1), tea(8), tea(9))
-        interleave("scalar", ("c", 1, 2), 0)
+        both("vector", ("z1", 0, 0))
         turn_both(tea(10), tea(11))
-        for c in range(3):
-            load_confusion(2, c)
+        load_confusion(2, 0)
+        load_affinity(1, 0)
+        load_student(1, 1)
+        load_confusion(2, 1)
+        load_affinity(1, 1)
+        load_confusion(2, 2)
         load_within(1)
         load_student(2, 0)
         load_student(2, 1)
         load_within(2)
         mm1(2, (2,))
-        interleave("scalar", ("c", 1, 2), 1)
-        quantise_all(tea(10), tea(11))
+        both("scalar", ("c", 1, 2))
+        quantise_all(tea(10), tea(11), ("z1", 0, 0))
         mm1(3)
         add1(2)
-        both("scalar", ("z1", 0, 0))
-        quantise(("c", 1, 2))
         turn_both(*aff(0, 0))
         add1(3)
         interleave("scalar", ("z1", 0, 1), 0)
-        quantise(("z1", 0, 0))
+        quantise(("c", 1, 2))
         interleave("vector", ("z1", 0, 1), 1)
         quantise_all(*aff(0, 0))
         quantise(("z1", 0, 1), HALVES[1])
         quantise(("z1", 0, 1), HALVES[0])
-        turn_both(*aff(0, 1))
-        spread_gain(0)
-        quantise_all(*aff(0, 1))
         both("scalar", ("w", 0))
 
-        interleaved = {
-            0: [("c", 2, 0)],
-            1: [("c", 2, 1)],
-            2: [("c", 2, 2), ("z1", 1, 0)],
-            4: [("w", 1)],
-            5: [("z1", 2, 0)],
-            6: [("w", 2)],
-        }
+        first_pairs = {0: [4], 1: [5], 2: [6], 3: [7], 4: [8], 5: [9, 10], 6: [11]}
+        interleaved = {0: ("c", 2, 0), 1: ("c", 2, 1), 2: ("c", 2, 2), 3: ("w", 1), 5: ("z1", 2, 0), 7: ("w", 2)}
         quantised = {
-            1: [*aff(1, 0), ("w", 0), ("c", 2, 0)],
-            2: [*aff(1, 1), ("c", 2, 1)],
-            3: [("c", 2, 2), ("z1", 1, 0)],
-            5: [("w", 1)],
+            0: [("w", 0)],
+            1: [("c", 2, 0)],
+            2: [("c", 2, 1)],
+            3: [("c", 2, 2)],
+            4: [("w", 1)],
             6: [("z1", 2, 0)],
-            7: [("w", 2)],
+            7: [("z1", 2, 1)],
+            8: [("w", 2)],
         }
 
         def tiles(*numbers):
@@ -398,43 +401,45 @@ def tile_teacher_student_logits_t1_kernel(
         for s in range(12):
             for i in tiles(2 * s - 1):
                 gain_mul(i)
-            if s in (1, 2):
+            for k in first_pairs.get(s, []):
+                mm1(k, by_pass=k == 8)
+                add1(k)
+            if s == 3:
+                interleave("scalar", ("z1", 1, 1), 0)
+            if s == 6:
+                both("scalar", ("z1", 2, 1))
+            if s <= 6:
                 mm2(2 * s)
-                add2(2 * s)
-                gain_mul(2 * s)
-            if s < 8:
-                mm1(s + 4)
-                add1(s + 4)
-                if s % 4 == 3:
-                    interleave("scalar", ("z1", s // 4 + 1, 1), 0)
-            if s not in (1, 2):
-                if s <= 8:
-                    mm2(2 * s)
-                add2(2 * s)
-                gain_mul(2 * s)
+            add2(2 * s)
+            gain_mul(2 * s)
+            if s < 3:
+                turn_both(*aff((s + 1) // 2, (s + 1) % 2))
             for i in tiles(2 * s - 5, 2 * s - 4):
                 finish(i)
             mm2(2 * s + 1)
             add2(2 * s + 1)
             if 8 <= s < 11:
                 mm2(2 * s + 2)
-            if s < 2:
-                turn_both(*aff(1, s))
             for i in tiles(2 * s - 1, 2 * s):
                 turn2(i)
                 round2(i)
-            if s in (3, 7):
-                spread_gain(s // 4 + 1)
-            if s in (3, 7):
-                interleave("vector", ("z1", s // 4 + 1, 1), 1)
+            if s < 3:
+                quantise_all(*aff((s + 1) // 2, (s + 1) % 2))
             quantise_all(*quantised.get(s, []))
+            if s == 2:
+                both("vector", ("z1", 1, 0))
+            if s == 3:
+                interleave("vector", ("z1", 1, 1), 1)
+                quantise(("z1", 1, 0))
             for i in tiles(2 * s - 3, 2 * s - 2):
                 quantise(("z2", i))
-            if s in (3, 7):
+            if s == 3:
                 for cols in HALVES:
-                    quantise(("z1", s // 4 + 1, 1), cols)
-            for key in interleaved.get(s, []):
-                both("scalar", key)
+                    quantise(("z1", 1, 1), cols)
+            if s in (6, 7):
+                mm2(2 * s + 2)
+            if s in interleaved:
+                both("scalar", interleaved[s])
         quantise(("z2", 21))
         gain_mul(23)
         finish(19)

@@ -17,9 +17,12 @@ ADD = mybir.AluOpType.add
 
 BLOCK_BYTES = 4 * 512 * 2
 TEACHER_BYTES = 2 * C * 2
+WHOLE = slice(0, 512)
 HALVES = (slice(0, 256), slice(256, 512))
 TURN_BANKS = 3
 SUM_BANKS = 5
+Z2_SLOTS = 6
+RESULT_SLOTS = 5
 
 
 def tile_teacher_student_logits_t1_kernel(
@@ -52,18 +55,19 @@ def tile_teacher_student_logits_t1_kernel(
         affinity_v = affinity.rearrange("(g p t) k -> g p t k", p=P, t=4)
         student_v = student.rearrange("(g p t) c -> g p t c", p=P, t=4)
         confusion_v = confusion.rearrange("(c p j) n -> c p j n", p=P, j=4)
-        within_v = within.rearrange("(h b t r) n -> h r b t n", b=64, t=4, r=2)
+        within_v = within.rearrange("(h b t r) n -> h r b t n", b=32, t=4, r=4)
         out_v = out.rearrange("(g p t) c -> g p t c", p=P, t=4)
 
         loaded = {}
         words = {}
         grouped = {}
+        parts = {}
         codes = {}
         scales = {}
         banks = {}
         z1 = {}
         z2 = {}
-        gained = {}
+        result = {}
 
         def raw_tile(key, shape, offset):
             name = "raw_" + "_".join(str(x) for x in key)
@@ -123,8 +127,8 @@ def tile_teacher_student_logits_t1_kernel(
 
         def load_within(h):
             t = raw_tile(("w", h), [P, 4, 512], place["w", h])
-            for r in range(2):
-                nc.sync.dma_start(out=t[r:P:2], in_=within_v[h, r])
+            for r in range(4):
+                nc.sync.dma_start(out=t[r:P:4], in_=within_v[h, r])
 
         ident = sbuf.tile([P, P], F32, name="ident", tag="ident")
         keep_sb = sbuf.tile([P, 2, 4], BF16, name="keep_sb", tag="keep_sb")
@@ -137,8 +141,7 @@ def tile_teacher_student_logits_t1_kernel(
             for j in range(4):
                 nc.tensor.transpose(bank[:, j, :], gain_f32[:, h, j : j + 1].to_broadcast([P, P]), ident[:])
             nc.scalar.copy(
-                out=gain_sb[:, h, :].rearrange("p (e i b r) -> p e i b r", e=2, i=2, r=2),
-                in_=bank[:].rearrange("p (i r) (b e) -> p e i b r", i=2, e=2),
+                out=gain_sb[:, h, :].rearrange("p (n j) -> p n j", j=4), in_=bank[:].rearrange("p j n -> p n j")
             )
 
         def copy_on(engine, o, s):
@@ -147,24 +150,28 @@ def tile_teacher_student_logits_t1_kernel(
             else:
                 nc.scalar.copy(out=o, in_=s)
 
-        def interleave(engine, key, half):
+        def interleave(engine, key, cols=WHOLE):
             if key not in grouped:
                 grouped[key] = ring(sbuf, "grouped", 4, [P, 512, 4], BF16)
             src = z1[key[1:]] if key[0] == "z1" else loaded[key]
-            cols = HALVES[half]
             copy_on(
                 engine,
                 grouped[key][:, cols, :].rearrange("p (n i) t -> p n t i", i=4),
                 src[:, :, cols].rearrange("p t (n i) -> p n t i", i=4),
             )
 
-        depth = {"c": 6, "w": 2, "z1": 4, "t": 12, "a": 8, "z2": 6}
+        depth = {"c": 6, "w": 2, "z1": 4, "t": 12, "a": 4, "z2": 3}
 
         def quantise(key, cols=None):
             width = grouped[key].shape[1]
             if key not in codes:
-                codes[key] = ring(sbuf, key[0] + "codes", depth[key[0]], [P, width], U32)
-                scales[key] = ring(sbuf, key[0] + "scales", depth[key[0]], [P, width], U8)
+                name = key[0] + str(width)
+                codes[key] = ring(sbuf, name + "codes", depth[key[0]], [P, width], U32)
+                scales[key] = ring(sbuf, name + "scales", depth[key[0]], [P, width], U8)
+                share = width // len(parts.get(key, [key]))
+                for n, part in enumerate(parts.get(key, [])):
+                    codes[part] = codes[key][:, n * share : (n + 1) * share]
+                    scales[part] = scales[key][:, n * share : (n + 1) * share]
             if cols is None:
                 cols = slice(0, width)
             nc.vector.quantize_mx(
@@ -173,19 +180,21 @@ def tile_teacher_student_logits_t1_kernel(
                 in_=grouped[key][:, cols, :].rearrange("p n t -> p (n t)"),
             )
 
-        def turn(key):
-            bank = turn_bank([P, 2, 2, P])
-            for a in range(2):
-                for u in range(2):
-                    nc.tensor.transpose(bank[:, a, u, :], words[key][:, a, u:256:2], ident[:])
-            banks[key] = bank
-
-        def turn_out(key):
-            grouped[key] = ring(sbuf, "turned", 4, [P, 256, 4], BF16)
-            nc.scalar.copy(
-                out=grouped[key][:].bitcast(F32).rearrange("p (a r) u -> p a r u", a=2),
-                in_=banks[key][:].rearrange("p a u r -> p a r u"),
-            )
+        def turn(*keys):
+            run = (keys[0][0], "run", *keys)
+            parts[run] = keys
+            for key in keys:
+                banks[key] = turn_bank([P, 2, 2, P])
+                for a in range(2):
+                    for u in range(2):
+                        nc.tensor.transpose(banks[key][:, a, u, :], words[key][:, a, u:256:2], ident[:])
+            grouped[run] = ring(sbuf, "turned", 3, [P, 256 * len(keys), 4], BF16)
+            for n, key in enumerate(keys):
+                nc.scalar.copy(
+                    out=grouped[run][:, 256 * n : 256 * (n + 1), :].bitcast(F32).rearrange("p (a r) u -> p a r u", a=2),
+                    in_=banks[key][:].rearrange("p a u r -> p a r u"),
+                )
+            return run
 
         def product(bank, left, cols, right, start, stop):
             nc.tensor.matmul_mx(
@@ -218,9 +227,9 @@ def tile_teacher_student_logits_t1_kernel(
             for a in tiles:
                 t = 2 * q + a
                 nc.vector.tensor_tensor(
-                    out=z1[h, g][:, t, :].rearrange("p (u b r) -> p b u r", u=4, r=2),
-                    in0=banks["z1", s, a][:].rearrange("p (b u r) -> p b u r", u=4, r=2),
-                    in1=loaded["s", h, g][:, t, :].rearrange("p (b u r) -> p b u r", u=4, r=2),
+                    out=z1[h, g][:, t, :].rearrange("p (u b r) -> p b u r", u=4, r=4),
+                    in0=banks["z1", s, a][:].rearrange("p (b u r) -> p b u r", u=4, r=4),
+                    in1=loaded["s", h, g][:, t, :].rearrange("p (b u r) -> p b u r", u=4, r=4),
                     op=ADD,
                 )
 
@@ -236,7 +245,7 @@ def tile_teacher_student_logits_t1_kernel(
 
         def add2(i):
             h, g, t = tile(i)
-            z2[i] = ring(sbuf, "z2", 4, [P, 512], F32)
+            z2[i] = ring(sbuf, "z2", Z2_SLOTS, [P, 512], F32)
             nc.vector.scalar_tensor_tensor(
                 out=z2[i][:],
                 in0=z1[h, g][:, t, :],
@@ -247,18 +256,28 @@ def tile_teacher_student_logits_t1_kernel(
             )
 
         def gain_mul(i):
-            gained[i] = ring(sbuf, "gained", 7, [P, 512], F32)
-            nc.gpsimd.tensor_tensor(out=gained[i][:], in0=z2[i][:], in1=gain_sb[:, i // 8, :], op=MULT)
+            if i % 2 == 0:
+                result[i // 2] = ring(sbuf, "result", RESULT_SLOTS, [P, 2, 512], F32)
+            nc.gpsimd.tensor_tensor(
+                out=result[i // 2][:, i % 2, :].rearrange("p (b u r) -> p b u r", u=4, r=4),
+                in0=z2[i][:].rearrange("p (u b r) -> p b u r", u=4, r=4),
+                in1=gain_sb[:, i // 8, :].rearrange("p (b u r) -> p b u r", u=4, r=4),
+                op=MULT,
+            )
 
-        def turn2(i):
-            bank = turn_bank([P, 4, P])
-            banks["z2t", i] = bank
-            for u in range(4):
-                nc.tensor.transpose(bank[:, u, :], z2[i][:, u * P : (u + 1) * P], ident[:])
-
-        def round2(i):
-            grouped["z2", i] = ring(sbuf, "z2grouped", 4, [P, P, 4], BF16)
-            nc.scalar.copy(out=grouped["z2", i][:], in_=banks["z2t", i][:].rearrange("p u n -> p n u"))
+        def turn2(*numbers):
+            run = ("z2", "run", *numbers)
+            parts[run] = [("z2", i) for i in numbers]
+            for i in numbers:
+                banks["z2t", i] = turn_bank([P, 4, P])
+                for u in range(4):
+                    nc.tensor.transpose(banks["z2t", i][:, u, :], z2[i][:, u * P : (u + 1) * P], ident[:])
+            grouped[run] = ring(sbuf, "z2grouped", 2, [P, P * len(numbers), 4], BF16)
+            for n, i in enumerate(numbers):
+                nc.scalar.copy(
+                    out=grouped[run][:, n * P : (n + 1) * P, :], in_=banks["z2t", i][:].rearrange("p u n -> p n u")
+                )
+            return run
 
         def mm3(i):
             banks["out", i] = sum_bank()
@@ -266,38 +285,34 @@ def tile_teacher_student_logits_t1_kernel(
 
         def add3(i):
             h, g, t = tile(i)
-            result = ring(sbuf, "outs", 6, [P, 512], F32)
-            nc.vector.tensor_tensor(
-                out=result[:].rearrange("p (b u r) -> p b u r", u=4, r=2),
-                in0=banks["out", i][:].rearrange("p (b u r) -> p b u r", u=4, r=2),
-                in1=gained[i][:].rearrange("p (u b r) -> p b u r", u=4, r=2),
-                op=ADD,
-            )
-            nc.sync.dma_start(out=out_v[g, :, t, h * 512 : (h + 1) * 512], in_=result[:])
+            part = result[i // 2][:, i % 2, :]
+            nc.vector.tensor_tensor(out=part, in0=banks["out", i][:], in1=part, op=ADD)
 
-        def turn_both(*keys):
-            for key in keys:
-                turn(key)
-            for key in keys:
-                turn_out(key)
+        def store(k):
+            h, g, q = pair(k)
+            nc.sync.dma_start(out=out_v[g, :, 2 * q : 2 * q + 2, h * 512 : (h + 1) * 512], in_=result[k][:])
+
+        def store_tile(i):
+            h, g, t = tile(i)
+            nc.sync.dma_start(out=out_v[g, :, t, h * 512 : (h + 1) * 512], in_=result[i // 2][:, i % 2, :])
 
         def quantise_all(*keys):
             for key in keys:
                 quantise(key)
 
         def both(engine, key):
-            for half in range(2):
-                interleave(engine, key, half)
+            for cols in HALVES:
+                interleave(engine, key, cols)
 
         def shared(key):
-            interleave("scalar", key, 0)
-            interleave("vector", key, 1)
+            interleave("scalar", key, HALVES[0])
+            interleave("vector", key, HALVES[1])
 
         def tea(i):
             return ("t", i // 6, i // 3 % 2, i % 3)
 
-        def aff(g, q):
-            return ("a", g, q, 0), ("a", g, q, 1)
+        def turn_affinity(n):
+            return turn(("a", n // 2, n % 2, 0), ("a", n // 2, n % 2, 1))
 
         nc.sync.dma_start(out=gain_in[:], in_=gain.rearrange("(h p j) -> p h j", p=P, j=4))
         load_confusion(0, 0)
@@ -321,38 +336,38 @@ def tile_teacher_student_logits_t1_kernel(
         for h in range(G):
             spread_gain(h)
 
-        both("vector", ("c", 0, 0))
-        turn_both(tea(0))
-        turn_both(tea(1))
-        quantise_all(("c", 0, 0), tea(0))
+        interleave("vector", ("c", 0, 0))
+        t0 = turn(tea(0))
+        t1 = turn(tea(1))
+        quantise_all(("c", 0, 0), t0)
         mm1(0, (0,))
         shared(("c", 0, 1))
-        quantise(tea(1))
-        turn_both(tea(2))
-        quantise_all(("c", 0, 1), tea(2))
+        quantise(t1)
+        t2 = turn(tea(2))
+        quantise_all(("c", 0, 1), t2)
         mm1(0, (1,))
-        both("vector", ("c", 0, 2))
-        turn_both(tea(3), tea(4))
+        interleave("vector", ("c", 0, 2))
+        t3 = turn(tea(3))
+        t4 = turn(tea(4), tea(5))
         load_student(1, 0)
         load_within(0)
         load_affinity(0, 1)
-        quantise_all(tea(3), ("c", 0, 2), tea(4))
-        turn_both(tea(5))
+        quantise_all(t3, ("c", 0, 2), t4)
         mm1(1, (0,))
         mm1(0, (2,))
-        both("vector", ("c", 1, 0))
-        quantise(tea(5))
-        turn_both(tea(6), tea(7))
+        interleave("vector", ("c", 1, 0))
+        t6 = turn(tea(6), tea(7))
         mm1(1, (1, 2))
         add1(0)
-        quantise_all(("c", 1, 0), tea(6), tea(7))
+        quantise_all(("c", 1, 0), t6)
         both("scalar", ("c", 1, 1))
-        turn_both(tea(8), tea(9))
+        t8 = turn(tea(8), tea(9))
         add1(1)
         mm1(2, (0, 1))
-        quantise_all(("c", 1, 1), tea(8), tea(9))
-        both("vector", ("z1", 0, 0))
-        turn_both(tea(10), tea(11))
+        quantise_all(("c", 1, 1), t8)
+        interleave("vector", ("z1", 0, 0))
+        t10 = turn(tea(10))
+        t11 = turn(tea(11))
         load_confusion(2, 0)
         load_affinity(1, 0)
         load_student(1, 1)
@@ -365,31 +380,22 @@ def tile_teacher_student_logits_t1_kernel(
         load_within(2)
         mm1(2, (2,))
         both("scalar", ("c", 1, 2))
-        quantise_all(tea(10), tea(11), ("z1", 0, 0))
+        quantise_all(t10, t11, ("z1", 0, 0))
         mm1(3)
         add1(2)
-        turn_both(*aff(0, 0))
+        a0 = turn_affinity(0)
         add1(3)
-        interleave("scalar", ("z1", 0, 1), 0)
+        interleave("scalar", ("z1", 0, 1), HALVES[0])
         quantise(("c", 1, 2))
-        interleave("vector", ("z1", 0, 1), 1)
-        quantise_all(*aff(0, 0))
+        interleave("vector", ("z1", 0, 1), HALVES[1])
+        quantise(a0)
         quantise(("z1", 0, 1), HALVES[1])
         quantise(("z1", 0, 1), HALVES[0])
         both("scalar", ("w", 0))
 
         first_pairs = {0: [4], 1: [5], 2: [6], 3: [7], 4: [8], 5: [9, 10], 6: [11]}
-        interleaved = {0: ("c", 2, 0), 1: ("c", 2, 1), 2: ("c", 2, 2), 3: ("w", 1), 5: ("z1", 2, 0), 7: ("w", 2)}
-        quantised = {
-            0: [("w", 0)],
-            1: [("c", 2, 0)],
-            2: [("c", 2, 1)],
-            3: [("c", 2, 2)],
-            4: [("w", 1)],
-            6: [("z1", 2, 0)],
-            7: [("z1", 2, 1)],
-            8: [("w", 2)],
-        }
+        interleaved = {0: ("c", 2, 0), 1: ("c", 2, 1), 2: ("c", 2, 2), 3: ("w", 1), 4: ("w", 2), 5: ("z1", 2, 0)}
+        quantised = {0: ("w", 0), 1: ("c", 2, 0), 2: ("c", 2, 1), 4: ("w", 1), 6: ("z1", 2, 0), 7: ("w", 2)}
 
         def tiles(*numbers):
             return [i for i in numbers if 0 <= i < 24]
@@ -398,55 +404,66 @@ def tile_teacher_student_logits_t1_kernel(
             mm3(i)
             add3(i)
 
+        turned = {}
         for s in range(12):
+            ahead = s >= 7
             for i in tiles(2 * s - 1):
                 gain_mul(i)
             for k in first_pairs.get(s, []):
                 mm1(k, by_pass=k == 8)
                 add1(k)
             if s == 3:
-                interleave("scalar", ("z1", 1, 1), 0)
+                interleave("scalar", ("z1", 1, 1), HALVES[0])
             if s == 6:
                 both("scalar", ("z1", 2, 1))
-            if s <= 6:
+            if not ahead:
                 mm2(2 * s)
             add2(2 * s)
             gain_mul(2 * s)
             if s < 3:
-                turn_both(*aff((s + 1) // 2, (s + 1) % 2))
-            for i in tiles(2 * s - 5, 2 * s - 4):
+                affinity_run = turn_affinity(s + 1)
+            for i in tiles(2 * s - 4, 2 * s - 5):
                 finish(i)
-            mm2(2 * s + 1)
+            if s >= 3:
+                store(s - 3)
+            if not ahead:
+                mm2(2 * s + 1)
             add2(2 * s + 1)
             if 8 <= s < 11:
                 mm2(2 * s + 2)
-            for i in tiles(2 * s - 1, 2 * s):
-                turn2(i)
-                round2(i)
+            turned[s] = turn2(*tiles(2 * s - 1, 2 * s))
             if s < 3:
-                quantise_all(*aff((s + 1) // 2, (s + 1) % 2))
-            quantise_all(*quantised.get(s, []))
-            if s == 2:
-                both("vector", ("z1", 1, 0))
+                quantise(affinity_run)
             if s == 3:
-                interleave("vector", ("z1", 1, 1), 1)
+                quantise(("c", 2, 2))
+                interleave("vector", ("z1", 1, 1), HALVES[1])
                 quantise(("z1", 1, 0))
-            for i in tiles(2 * s - 3, 2 * s - 2):
-                quantise(("z2", i))
+            if s == 7:
+                quantise(("z1", 2, 1))
+            if s > 0:
+                quantise(turned[s - 1])
+            if s in quantised:
+                quantise(quantised[s])
+            if s == 2:
+                interleave("vector", ("z1", 1, 0))
             if s == 3:
                 for cols in HALVES:
                     quantise(("z1", 1, 1), cols)
             if s in (6, 7):
                 mm2(2 * s + 2)
+            if 6 <= s < 11:
+                mm2(2 * s + 3)
             if s in interleaved:
                 both("scalar", interleaved[s])
-        quantise(("z2", 21))
         gain_mul(23)
-        finish(19)
         finish(20)
-        turn2(23)
-        round2(23)
+        finish(19)
+        store(9)
+        last = turn2(23)
+        quantise_all(turned[11], last)
         finish(21)
-        quantise_all(("z2", 22), ("z2", 23))
+        store(10)
         finish(22)
+        store_tile(22)
         finish(23)
+        store_tile(23)

@@ -21,8 +21,8 @@ WHOLE = slice(0, 512)
 HALVES = (slice(0, 256), slice(256, 512))
 TURN_BANKS = 3
 SUM_BANKS = 5
-Z2_SLOTS = 6
-RESULT_SLOTS = 5
+LATE_SLOTS = 4
+GPSIMD_COLS = 384
 
 
 def tile_teacher_student_logits_t1_kernel(
@@ -45,6 +45,10 @@ def tile_teacher_student_logits_t1_kernel(
                 return pool.tile(shape, dtype, name=tag, tag=tag)
             return pool.tile(shape, dtype, name=tag, tag=tag, align_bytes=64)
 
+        def late_slot(n, shape, dtype):
+            tag = "late" + str(n % LATE_SLOTS)
+            return sbuf.tile(shape, dtype, name=tag, tag=tag, align_bytes=64)
+
         def turn_bank(shape):
             return ring(psum, "turn", TURN_BANKS, shape, F32)
 
@@ -60,6 +64,7 @@ def tile_teacher_student_logits_t1_kernel(
 
         loaded = {}
         words = {}
+        sorted_words = {}
         grouped = {}
         parts = {}
         codes = {}
@@ -68,6 +73,7 @@ def tile_teacher_student_logits_t1_kernel(
         z1 = {}
         z2 = {}
         result = {}
+        gained = {}
 
         def raw_tile(key, shape, offset):
             name = "raw_" + "_".join(str(x) for x in key)
@@ -141,7 +147,8 @@ def tile_teacher_student_logits_t1_kernel(
             for j in range(4):
                 nc.tensor.transpose(bank[:, j, :], gain_f32[:, h, j : j + 1].to_broadcast([P, P]), ident[:])
             nc.scalar.copy(
-                out=gain_sb[:, h, :].rearrange("p (n j) -> p n j", j=4), in_=bank[:].rearrange("p j n -> p n j")
+                out=gain_sb[:, h, :].rearrange("p (u b r) -> p u b r", u=4, r=4),
+                in_=bank[:].rearrange("p r (b u) -> p u b r", u=4),
             )
 
         def copy_on(engine, o, s):
@@ -160,7 +167,7 @@ def tile_teacher_student_logits_t1_kernel(
                 src[:, :, cols].rearrange("p t (n i) -> p n t i", i=4),
             )
 
-        depth = {"c": 6, "w": 2, "z1": 4, "t": 12, "a": 4, "z2": 3}
+        depth = {"c": 6, "w": 2, "z1": 4, "t": 12, "a": 4, "z2": 2}
 
         def quantise(key, cols=None):
             width = grouped[key].shape[1]
@@ -180,6 +187,16 @@ def tile_teacher_student_logits_t1_kernel(
                 in_=grouped[key][:, cols, :].rearrange("p n t -> p (n t)"),
             )
 
+        def sort_words(n):
+            key = ("a", n // 2, n % 2)
+            ordered = ring(sbuf, "grouped", 4, [P, 2, 2, 2, P], F32)
+            nc.vector.tensor_copy(
+                out=ordered[:].rearrange("p a c u m -> p (a c) u m"),
+                in_=loaded[key][:].bitcast(F32).rearrange("p a (c m u) -> p (a c) u m", c=2, u=2),
+            )
+            for c in range(2):
+                sorted_words[key + (c,)] = ordered[:, :, c]
+
         def turn(*keys):
             run = (keys[0][0], "run", *keys)
             parts[run] = keys
@@ -187,7 +204,8 @@ def tile_teacher_student_logits_t1_kernel(
                 banks[key] = turn_bank([P, 2, 2, P])
                 for a in range(2):
                     for u in range(2):
-                        nc.tensor.transpose(banks[key][:, a, u, :], words[key][:, a, u:256:2], ident[:])
+                        src = sorted_words[key][:, a, u] if key in sorted_words else words[key][:, a, u:256:2]
+                        nc.tensor.transpose(banks[key][:, a, u, :], src, ident[:])
             grouped[run] = ring(sbuf, "turned", 3, [P, 256 * len(keys), 4], BF16)
             for n, key in enumerate(keys):
                 nc.scalar.copy(
@@ -236,18 +254,20 @@ def tile_teacher_student_logits_t1_kernel(
         def tile(i):
             return i // 8, i // 4 % 2, i % 4
 
-        def mm2(i):
+        def mm2(i, passes=(0, 1)):
             h, g, t = tile(i)
-            banks["z2", i] = sum_bank()
             cols = slice(t % 2 * P, (t % 2 + 1) * P)
-            for c in range(2):
+            for c in passes:
+                if c == 0:
+                    banks["z2", i] = sum_bank()
                 product(banks["z2", i], ("a", g, t // 2, c), cols, ("z1", h, c), c == 0, c == 1)
 
         def add2(i):
             h, g, t = tile(i)
-            z2[i] = ring(sbuf, "z2", Z2_SLOTS, [P, 512], F32)
+            if i % 2 == 0:
+                z2[i // 2] = ring(sbuf, "z2", 3, [P, 2, 512], F32)
             nc.vector.scalar_tensor_tensor(
-                out=z2[i][:],
+                out=z2[i // 2][:, i % 2, :],
                 in0=z1[h, g][:, t, :],
                 scalar=keep_sb[:, g, t : t + 1],
                 in1=banks["z2", i][:],
@@ -255,27 +275,28 @@ def tile_teacher_student_logits_t1_kernel(
                 op1=ADD,
             )
 
-        def gain_mul(i):
-            if i % 2 == 0:
-                result[i // 2] = ring(sbuf, "result", RESULT_SLOTS, [P, 2, 512], F32)
-            nc.gpsimd.tensor_tensor(
-                out=result[i // 2][:, i % 2, :].rearrange("p (b u r) -> p b u r", u=4, r=4),
-                in0=z2[i][:].rearrange("p (u b r) -> p b u r", u=4, r=4),
-                in1=gain_sb[:, i // 8, :].rearrange("p (b u r) -> p b u r", u=4, r=4),
+        def gain_mul(k, engine=nc.gpsimd, tiles=slice(0, 2), cols=WHOLE):
+            if k not in gained:
+                gained[k] = late_slot(k, [P, 2, 512], F32)
+            shape = [P, tiles.stop - tiles.start, cols.stop - cols.start]
+            engine.tensor_tensor(
+                out=gained[k][:, tiles, cols],
+                in0=z2[k][:, tiles, cols],
+                in1=gain_sb[:, k // 4, cols].unsqueeze(1).to_broadcast(shape),
                 op=MULT,
             )
 
-        def turn2(*numbers):
-            run = ("z2", "run", *numbers)
-            parts[run] = [("z2", i) for i in numbers]
-            for i in numbers:
-                banks["z2t", i] = turn_bank([P, 4, P])
+        def turn2(k):
+            run = ("z2", "run", k)
+            parts[run] = [("z2", 2 * k), ("z2", 2 * k + 1)]
+            for a in range(2):
+                banks["z2t", a] = turn_bank([P, 4, P])
                 for u in range(4):
-                    nc.tensor.transpose(banks["z2t", i][:, u, :], z2[i][:, u * P : (u + 1) * P], ident[:])
-            grouped[run] = ring(sbuf, "z2grouped", 2, [P, P * len(numbers), 4], BF16)
-            for n, i in enumerate(numbers):
+                    nc.tensor.transpose(banks["z2t", a][:, u, :], z2[k][:, a, u * P : (u + 1) * P], ident[:])
+            grouped[run] = late_slot(k + 1 if k < 5 else k + 2, [P, 2 * P, 4], BF16)
+            for a in range(2):
                 nc.scalar.copy(
-                    out=grouped[run][:, n * P : (n + 1) * P, :], in_=banks["z2t", i][:].rearrange("p u n -> p n u")
+                    out=grouped[run][:, a * P : (a + 1) * P, :], in_=banks["z2t", a][:].rearrange("p u n -> p n u")
                 )
             return run
 
@@ -284,9 +305,14 @@ def tile_teacher_student_logits_t1_kernel(
             product(banks["out", i], ("z2", i), slice(0, P), ("w", i // 8), True, True)
 
         def add3(i):
-            h, g, t = tile(i)
-            part = result[i // 2][:, i % 2, :]
-            nc.vector.tensor_tensor(out=part, in0=banks["out", i][:], in1=part, op=ADD)
+            if i // 2 not in result:
+                result[i // 2] = ring(sbuf, "result", 3, [P, 2, 512], F32)
+            nc.vector.tensor_tensor(
+                out=result[i // 2][:, i % 2, :].rearrange("p (b u r) -> p b u r", u=4, r=4),
+                in0=banks["out", i][:].rearrange("p (b u r) -> p b u r", u=4, r=4),
+                in1=gained[i // 2][:, i % 2, :].rearrange("p (u b r) -> p b u r", u=4, r=4),
+                op=ADD,
+            )
 
         def store(k):
             h, g, q = pair(k)
@@ -397,41 +423,42 @@ def tile_teacher_student_logits_t1_kernel(
         interleaved = {0: ("c", 2, 0), 1: ("c", 2, 1), 2: ("c", 2, 2), 3: ("w", 1), 4: ("w", 2), 5: ("z1", 2, 0)}
         quantised = {0: ("w", 0), 1: ("c", 2, 0), 2: ("c", 2, 1), 4: ("w", 1), 6: ("z1", 2, 0), 7: ("w", 2)}
 
-        def tiles(*numbers):
-            return [i for i in numbers if 0 <= i < 24]
+        def finish(k):
+            for i in (2 * k, 2 * k + 1):
+                mm3(i)
+                add3(i)
+            store(k)
 
-        def finish(i):
-            mm3(i)
-            add3(i)
-
-        turned = {}
         for s in range(12):
-            ahead = s >= 7
-            for i in tiles(2 * s - 1):
-                gain_mul(i)
+            if s > 6:
+                gain_mul(s - 1, cols=slice(0, GPSIMD_COLS))
+            elif s > 0:
+                gain_mul(s - 1)
             for k in first_pairs.get(s, []):
                 mm1(k, by_pass=k == 8)
                 add1(k)
             if s == 3:
                 interleave("scalar", ("z1", 1, 1), HALVES[0])
+            if s > 0:
+                turned = turn2(s - 1)
             if s == 6:
                 both("scalar", ("z1", 2, 1))
-            if not ahead:
+            if s < 7:
                 mm2(2 * s)
+            if s == 8:
+                mm2(16, (1,))
             add2(2 * s)
-            gain_mul(2 * s)
             if s < 3:
                 affinity_run = turn_affinity(s + 1)
-            for i in tiles(2 * s - 4, 2 * s - 5):
-                finish(i)
-            if s >= 3:
-                store(s - 3)
-            if not ahead:
+            if s >= 2:
+                finish(s - 2)
+            if s < 7:
                 mm2(2 * s + 1)
-            add2(2 * s + 1)
+            if s == 8:
+                mm2(17, (1,))
             if 8 <= s < 11:
                 mm2(2 * s + 2)
-            turned[s] = turn2(*tiles(2 * s - 1, 2 * s))
+            add2(2 * s + 1)
             if s < 3:
                 quantise(affinity_run)
             if s == 3:
@@ -439,31 +466,33 @@ def tile_teacher_student_logits_t1_kernel(
                 interleave("vector", ("z1", 1, 1), HALVES[1])
                 quantise(("z1", 1, 0))
             if s == 7:
+                mm2(16, (0,))
+                mm2(17, (0,))
                 quantise(("z1", 2, 1))
-            if s > 0:
-                quantise(turned[s - 1])
             if s in quantised:
                 quantise(quantised[s])
-            if s == 2:
-                interleave("vector", ("z1", 1, 0))
             if s == 3:
                 for cols in HALVES:
                     quantise(("z1", 1, 1), cols)
-            if s in (6, 7):
-                mm2(2 * s + 2)
-            if 6 <= s < 11:
+            if s < 2:
+                sort_words(s + 2)
+            if s > 0:
+                quantise(turned)
+            if s >= 6:
+                gain_mul(s, nc.vector, cols=slice(GPSIMD_COLS, 512))
+            if s == 6:
+                mm2(14)
+            if s == 6 or 8 <= s < 11:
                 mm2(2 * s + 3)
             if s in interleaved:
                 both("scalar", interleaved[s])
-        gain_mul(23)
-        finish(20)
-        finish(19)
-        store(9)
-        last = turn2(23)
-        quantise_all(turned[11], last)
-        finish(21)
-        store(10)
-        finish(22)
-        store_tile(22)
-        finish(23)
-        store_tile(23)
+            if s == 2:
+                both("scalar", ("z1", 1, 0))
+        gain_mul(11, cols=slice(0, GPSIMD_COLS))
+        turned = turn2(11)
+        finish(10)
+        quantise(turned)
+        for i in (22, 23):
+            mm3(i)
+            add3(i)
+            store_tile(i)

@@ -64,7 +64,6 @@ def tile_teacher_student_logits_t1_kernel(
 
         loaded = {}
         words = {}
-        sorted_words = {}
         grouped = {}
         parts = {}
         codes = {}
@@ -187,26 +186,16 @@ def tile_teacher_student_logits_t1_kernel(
                 in_=grouped[key][:, cols, :].rearrange("p n t -> p (n t)"),
             )
 
-        def sort_words(n):
-            key = ("a", n // 2, n % 2)
-            ordered = ring(sbuf, "grouped", 4, [P, 2, 2, 2, P], F32)
-            nc.vector.tensor_copy(
-                out=ordered[:].rearrange("p a c u m -> p (a c) u m"),
-                in_=loaded[key][:].bitcast(F32).rearrange("p a (c m u) -> p (a c) u m", c=2, u=2),
-            )
-            for c in range(2):
-                sorted_words[key + (c,)] = ordered[:, :, c]
-
-        def turn(*keys):
+        def turn(*keys, late=False):
             run = (keys[0][0], "run", *keys)
             parts[run] = keys
             for key in keys:
                 banks[key] = turn_bank([P, 2, 2, P])
                 for a in range(2):
                     for u in range(2):
-                        src = sorted_words[key][:, a, u] if key in sorted_words else words[key][:, a, u:256:2]
-                        nc.tensor.transpose(banks[key][:, a, u, :], src, ident[:])
-            grouped[run] = ring(sbuf, "turned", 3, [P, 256 * len(keys), 4], BF16)
+                        nc.tensor.transpose(banks[key][:, a, u, :], words[key][:, a, u:256:2], ident[:])
+            shape = [P, 256 * len(keys), 4]
+            grouped[run] = late_slot(0, shape, BF16) if late else ring(sbuf, "turned", 3, shape, BF16)
             for n, key in enumerate(keys):
                 nc.scalar.copy(
                     out=grouped[run][:, 256 * n : 256 * (n + 1), :].bitcast(F32).rearrange("p (a r) u -> p a r u", a=2),
@@ -238,7 +227,7 @@ def tile_teacher_student_logits_t1_kernel(
                     banks["z1", s, a] = sum_bank()
                 product(banks["z1", s, a], ("t", g, q, c), slice(a * P, (a + 1) * P), ("c", h, c), c == 0, c == 2)
 
-        def add1(s, tiles=(0, 1)):
+        def add1(s, tiles=(1, 0)):
             h, g, q = pair(s)
             if (h, g) not in z1:
                 z1[h, g] = ring(sbuf, "z1", 4, [P, 4, 512], F32)
@@ -264,7 +253,7 @@ def tile_teacher_student_logits_t1_kernel(
 
         def add2(i):
             h, g, t = tile(i)
-            if i % 2 == 0:
+            if i // 2 not in z2:
                 z2[i // 2] = ring(sbuf, "z2", 3, [P, 2, 512], F32)
             nc.vector.scalar_tensor_tensor(
                 out=z2[i // 2][:, i % 2, :],
@@ -277,7 +266,7 @@ def tile_teacher_student_logits_t1_kernel(
 
         def gain_mul(k, engine=nc.gpsimd, tiles=slice(0, 2), cols=WHOLE):
             if k not in gained:
-                gained[k] = late_slot(k, [P, 2, 512], F32)
+                gained[k] = late_slot(k + k // 11, [P, 2, 512], F32)
             shape = [P, tiles.stop - tiles.start, cols.stop - cols.start]
             engine.tensor_tensor(
                 out=gained[k][:, tiles, cols],
@@ -293,7 +282,7 @@ def tile_teacher_student_logits_t1_kernel(
                 banks["z2t", a] = turn_bank([P, 4, P])
                 for u in range(4):
                     nc.tensor.transpose(banks["z2t", a][:, u, :], z2[k][:, a, u * P : (u + 1) * P], ident[:])
-            grouped[run] = late_slot(k + 1 if k < 5 else k + 2, [P, 2 * P, 4], BF16)
+            grouped[run] = late_slot(k + 1, [P, 2 * P, 4], BF16)
             for a in range(2):
                 nc.scalar.copy(
                     out=grouped[run][:, a * P : (a + 1) * P, :], in_=banks["z2t", a][:].rearrange("p u n -> p n u")
@@ -338,7 +327,7 @@ def tile_teacher_student_logits_t1_kernel(
             return ("t", i // 6, i // 3 % 2, i % 3)
 
         def turn_affinity(n):
-            return turn(("a", n // 2, n % 2, 0), ("a", n // 2, n % 2, 1))
+            return turn(("a", n // 2, n % 2, 0), ("a", n // 2, n % 2, 1), late=n == 1)
 
         nc.sync.dma_start(out=gain_in[:], in_=gain.rearrange("(h p j) -> p h j", p=P, j=4))
         load_confusion(0, 0)
@@ -424,47 +413,45 @@ def tile_teacher_student_logits_t1_kernel(
         quantised = {0: ("w", 0), 1: ("c", 2, 0), 2: ("c", 2, 1), 4: ("w", 1), 6: ("z1", 2, 0), 7: ("w", 2)}
 
         def finish(k):
-            for i in (2 * k, 2 * k + 1):
-                mm3(i)
-                add3(i)
+            mm3(2 * k)
+            mm3(2 * k + 1)
+            add3(2 * k + 1)
+            add3(2 * k)
             store(k)
 
+        turned = {}
         for s in range(12):
-            if s > 6:
-                gain_mul(s - 1, cols=slice(0, GPSIMD_COLS))
-            elif s > 0:
+            if s > 0:
                 gain_mul(s - 1)
             for k in first_pairs.get(s, []):
                 mm1(k, by_pass=k == 8)
                 add1(k)
             if s == 3:
-                interleave("scalar", ("z1", 1, 1), HALVES[0])
-            if s > 0:
-                turned = turn2(s - 1)
+                both("scalar", ("z1", 1, 1))
+            if 0 < s < 8:
+                turned[s - 1] = turn2(s - 1)
             if s == 6:
                 both("scalar", ("z1", 2, 1))
-            if s < 7:
-                mm2(2 * s)
-            if s == 8:
-                mm2(16, (1,))
+            for i in (2 * s, 2 * s + 1):
+                if s < 7:
+                    mm2(i)
+                if s == 8:
+                    mm2(i, (1,))
+            add2(2 * s + 1)
             add2(2 * s)
             if s < 3:
                 affinity_run = turn_affinity(s + 1)
             if s >= 2:
                 finish(s - 2)
-            if s < 7:
-                mm2(2 * s + 1)
-            if s == 8:
-                mm2(17, (1,))
             if 8 <= s < 11:
                 mm2(2 * s + 2)
-            add2(2 * s + 1)
-            if s < 3:
+                mm2(2 * s + 3)
+            if s >= 7:
+                turned[s] = turn2(s)
+            if 0 < s < 3:
                 quantise(affinity_run)
             if s == 3:
-                quantise(("c", 2, 2))
-                interleave("vector", ("z1", 1, 1), HALVES[1])
-                quantise(("z1", 1, 0))
+                quantise_all(("c", 2, 2), ("z1", 1, 0))
             if s == 7:
                 mm2(16, (0,))
                 mm2(17, (0,))
@@ -472,27 +459,24 @@ def tile_teacher_student_logits_t1_kernel(
             if s in quantised:
                 quantise(quantised[s])
             if s == 3:
-                for cols in HALVES:
-                    quantise(("z1", 1, 1), cols)
-            if s < 2:
-                sort_words(s + 2)
+                quantise(("z1", 1, 1))
             if s > 0:
-                quantise(turned)
-            if s >= 6:
-                gain_mul(s, nc.vector, cols=slice(GPSIMD_COLS, 512))
+                quantise(turned[s - 1])
+            if s == 0:
+                quantise(affinity_run)
             if s == 6:
-                mm2(14)
-            if s == 6 or 8 <= s < 11:
+                mm2(2 * s + 2)
                 mm2(2 * s + 3)
             if s in interleaved:
                 both("scalar", interleaved[s])
             if s == 2:
                 both("scalar", ("z1", 1, 0))
-        gain_mul(11, cols=slice(0, GPSIMD_COLS))
-        turned = turn2(11)
+        quantise(turned[11])
+        gain_mul(11, tiles=slice(0, 1))
+        gain_mul(11, tiles=slice(1, 2))
         finish(10)
-        quantise(turned)
+        mm3(22)
+        mm3(23)
         for i in (22, 23):
-            mm3(i)
             add3(i)
             store_tile(i)

@@ -64,6 +64,7 @@ def tile_teacher_student_logits_t1_kernel(
 
         loaded = {}
         words = {}
+        sorted_words = {}
         grouped = {}
         parts = {}
         codes = {}
@@ -186,6 +187,12 @@ def tile_teacher_student_logits_t1_kernel(
                 in_=grouped[key][:, cols, :].rearrange("p n t -> p (n t)"),
             )
 
+        def sort_words(engine, *keys):
+            ordered = ring(sbuf, "result", 3, [P, len(keys), 2, 2, P], F32)
+            for n, key in enumerate(keys):
+                copy_on(engine, ordered[:, n], words[key].rearrange("p a (m u) -> p a u m", u=2))
+                sorted_words[key] = ordered[:, n]
+
         def turn(*keys, late=False):
             run = (keys[0][0], "run", *keys)
             parts[run] = keys
@@ -193,7 +200,8 @@ def tile_teacher_student_logits_t1_kernel(
                 banks[key] = turn_bank([P, 2, 2, P])
                 for a in range(2):
                     for u in range(2):
-                        nc.tensor.transpose(banks[key][:, a, u, :], words[key][:, a, u:256:2], ident[:])
+                        src = sorted_words[key][:, a, u] if key in sorted_words else words[key][:, a, u:256:2]
+                        nc.tensor.transpose(banks[key][:, a, u, :], src, ident[:])
             shape = [P, 256 * len(keys), 4]
             grouped[run] = late_slot(0, shape, BF16) if late else ring(sbuf, "turned", 3, shape, BF16)
             for n, key in enumerate(keys):
@@ -326,6 +334,9 @@ def tile_teacher_student_logits_t1_kernel(
         def tea(i):
             return ("t", i // 6, i // 3 % 2, i % 3)
 
+        def aff(n):
+            return ("a", n // 2, n % 2, 0), ("a", n // 2, n % 2, 1)
+
         def turn_affinity(n):
             return turn(("a", n // 2, n % 2, 0), ("a", n // 2, n % 2, 1), late=n == 1)
 
@@ -379,8 +390,8 @@ def tile_teacher_student_logits_t1_kernel(
         t8 = turn(tea(8), tea(9))
         add1(1)
         mm1(2, (0, 1))
-        quantise_all(("c", 1, 1), t8)
         interleave("vector", ("z1", 0, 0))
+        quantise_all(("c", 1, 1), t8)
         t10 = turn(tea(10))
         t11 = turn(tea(11))
         load_confusion(2, 0)
@@ -448,8 +459,6 @@ def tile_teacher_student_logits_t1_kernel(
                 mm2(2 * s + 3)
             if s >= 7:
                 turned[s] = turn2(s)
-            if 0 < s < 3:
-                quantise(affinity_run)
             if s == 3:
                 quantise_all(("c", 2, 2), ("z1", 1, 0))
             if s == 7:
@@ -458,6 +467,10 @@ def tile_teacher_student_logits_t1_kernel(
                 quantise(("z1", 2, 1))
             if s in quantised:
                 quantise(quantised[s])
+            if s < 2:
+                sort_words("vector", *aff(s + 2))
+            if 0 < s < 3:
+                quantise(affinity_run)
             if s == 3:
                 quantise(("z1", 1, 1))
             if s > 0:

@@ -351,8 +351,8 @@ def tile_teacher_student_logits_t1_kernel(
         load_confusion(1, 0)
         load_teacher(1, 0)
         load_student(0, 0)
-        load_confusion(1, 1)
         load_teacher(1, 1)
+        load_confusion(1, 1)
         load_confusion(1, 2)
         load_student(0, 1)
         load_affinity(0, 0)
@@ -382,16 +382,18 @@ def tile_teacher_student_logits_t1_kernel(
         mm1(1, (0,))
         mm1(0, (2,))
         interleave("vector", ("c", 1, 0))
+        sort_words("scalar", tea(6), tea(7))
+        sort_words("scalar", tea(8))
         t6 = turn(tea(6), tea(7))
         mm1(1, (1, 2))
         add1(0)
         quantise_all(("c", 1, 0), t6)
-        both("scalar", ("c", 1, 1))
         t8 = turn(tea(8), tea(9))
         add1(1)
         mm1(2, (0, 1))
         interleave("vector", ("z1", 0, 0))
-        quantise_all(("c", 1, 1), t8)
+        quantise(t8)
+        interleave("scalar", ("c", 1, 1), HALVES[0])
         t10 = turn(tea(10))
         t11 = turn(tea(11))
         load_confusion(2, 0)
@@ -405,19 +407,20 @@ def tile_teacher_student_logits_t1_kernel(
         load_student(2, 1)
         load_within(2)
         mm1(2, (2,))
-        both("scalar", ("c", 1, 2))
-        quantise_all(t10, t11, ("z1", 0, 0))
+        quantise_all(("z1", 0, 0), t10, t11)
+        interleave("scalar", ("c", 1, 1), HALVES[1])
+        interleave("scalar", ("c", 1, 2))
         mm1(3)
         add1(2)
         a0 = turn_affinity(0)
         add1(3)
         interleave("scalar", ("z1", 0, 1), HALVES[0])
-        quantise(("c", 1, 2))
+        quantise_all(("c", 1, 1), ("c", 1, 2))
         interleave("vector", ("z1", 0, 1), HALVES[1])
         quantise(a0)
         quantise(("z1", 0, 1), HALVES[1])
         quantise(("z1", 0, 1), HALVES[0])
-        both("scalar", ("w", 0))
+        interleave("scalar", ("w", 0))
 
         first_pairs = {0: [4], 1: [5], 2: [6], 3: [7], 4: [8], 5: [9, 10], 6: [11]}
         interleaved = {0: ("c", 2, 0), 1: ("c", 2, 1), 2: ("c", 2, 2), 3: ("w", 1), 4: ("w", 2), 5: ("z1", 2, 0)}
@@ -435,14 +438,14 @@ def tile_teacher_student_logits_t1_kernel(
             if s > 0:
                 gain_mul(s - 1)
             for k in first_pairs.get(s, []):
-                mm1(k, by_pass=k == 8)
+                mm1(k, by_pass=k in (4, 8))
                 add1(k)
             if s == 3:
-                both("scalar", ("z1", 1, 1))
+                interleave("scalar", ("z1", 1, 1))
             if 0 < s < 8:
                 turned[s - 1] = turn2(s - 1)
             if s == 6:
-                both("scalar", ("z1", 2, 1))
+                interleave("scalar", ("z1", 2, 1))
             for i in (2 * s, 2 * s + 1):
                 if s < 7:
                     mm2(i)
@@ -465,6 +468,8 @@ def tile_teacher_student_logits_t1_kernel(
                 mm2(16, (0,))
                 mm2(17, (0,))
                 quantise(("z1", 2, 1))
+            if s in (4, 6):
+                quantise(turned[s - 1])
             if s in quantised:
                 quantise(quantised[s])
             if s < 2:
@@ -473,7 +478,7 @@ def tile_teacher_student_logits_t1_kernel(
                 quantise(affinity_run)
             if s == 3:
                 quantise(("z1", 1, 1))
-            if s > 0:
+            if s > 0 and s not in (4, 6):
                 quantise(turned[s - 1])
             if s == 0:
                 quantise(affinity_run)
@@ -481,9 +486,9 @@ def tile_teacher_student_logits_t1_kernel(
                 mm2(2 * s + 2)
                 mm2(2 * s + 3)
             if s in interleaved:
-                both("scalar", interleaved[s])
+                interleave("scalar", interleaved[s])
             if s == 2:
-                both("scalar", ("z1", 1, 0))
+                interleave("scalar", ("z1", 1, 0))
         quantise(turned[11])
         gain_mul(11, tiles=slice(0, 1))
         gain_mul(11, tiles=slice(1, 2))

@@ -272,16 +272,20 @@ def tile_teacher_student_logits_t1_kernel(
                 op1=ADD,
             )
 
-        def gain_mul(k, engine=nc.gpsimd, tiles=slice(0, 2), cols=WHOLE):
-            if k not in gained:
-                gained[k] = late_slot(k + k // 11, [P, 2, 512], F32)
-            shape = [P, tiles.stop - tiles.start, cols.stop - cols.start]
-            engine.tensor_tensor(
-                out=gained[k][:, tiles, cols],
-                in0=z2[k][:, tiles, cols],
-                in1=gain_sb[:, k // 4, cols].unsqueeze(1).to_broadcast(shape),
+        def gain_mul(k):
+            pair_tile = late_slot(k, [P, 2, 512], F32)
+            for a in range(2):
+                gained[2 * k + a] = pair_tile[:, a, :]
+            nc.gpsimd.tensor_tensor(
+                out=pair_tile[:],
+                in0=z2[k][:],
+                in1=gain_sb[:, k // 4, :].unsqueeze(1).to_broadcast([P, 2, 512]),
                 op=MULT,
             )
+
+        def gain_mul_tile(i, engine, slot):
+            gained[i] = late_slot(slot, [P, 512], F32)[:]
+            engine.tensor_tensor(out=gained[i], in0=z2[i // 2][:, i % 2, :], in1=gain_sb[:, i // 8, :], op=MULT)
 
         def turn2(k):
             run = ("z2", "run", k)
@@ -307,7 +311,7 @@ def tile_teacher_student_logits_t1_kernel(
             nc.vector.tensor_tensor(
                 out=result[i // 2][:, i % 2, :].rearrange("p (b u r) -> p b u r", u=4, r=4),
                 in0=banks["out", i][:].rearrange("p (b u r) -> p b u r", u=4, r=4),
-                in1=gained[i // 2][:, i % 2, :].rearrange("p (u b r) -> p b u r", u=4, r=4),
+                in1=gained[i].rearrange("p (u b r) -> p b u r", u=4, r=4),
                 op=ADD,
             )
 
@@ -340,7 +344,8 @@ def tile_teacher_student_logits_t1_kernel(
         def turn_affinity(n):
             return turn(("a", n // 2, n % 2, 0), ("a", n // 2, n % 2, 1), late=n == 1)
 
-        nc.sync.dma_start(out=gain_in[:], in_=gain.rearrange("(h p j) -> p h j", p=P, j=4))
+        nc.scalar.dma_start(out=gain_in[:], in_=gain.rearrange("(h p j) -> p h j", p=P, j=4))
+        nc.scalar.dma_start(out=keep_sb[:], in_=keep.rearrange("(g p t) -> p g t", p=P, t=4))
         load_confusion(0, 0)
         load_teacher(0, 0, (0,))
         load_teacher(0, 0, (1,))
@@ -356,7 +361,6 @@ def tile_teacher_student_logits_t1_kernel(
         load_confusion(1, 2)
         load_student(0, 1)
         load_affinity(0, 0)
-        nc.sync.dma_start(out=keep_sb[:], in_=keep.rearrange("(g p t) -> p g t", p=P, t=4))
         make_identity(nc, ident[:])
         nc.scalar.copy(out=gain_f32[:], in_=gain_in[:])
         for h in range(G):
@@ -376,8 +380,8 @@ def tile_teacher_student_logits_t1_kernel(
         t3 = turn(tea(3))
         t4 = turn(tea(4), tea(5))
         load_student(1, 0)
-        load_within(0)
         load_affinity(0, 1)
+        load_within(0)
         quantise_all(t3, ("c", 0, 2), t4)
         mm1(1, (0,))
         mm1(0, (2,))
@@ -420,6 +424,7 @@ def tile_teacher_student_logits_t1_kernel(
         quantise(a0)
         quantise(("z1", 0, 1), HALVES[1])
         quantise(("z1", 0, 1), HALVES[0])
+        sort_words("vector", *aff(1))
         interleave("scalar", ("w", 0))
 
         first_pairs = {0: [4], 1: [5], 2: [6], 3: [7], 4: [8], 5: [9, 10], 6: [11]}
@@ -442,10 +447,10 @@ def tile_teacher_student_logits_t1_kernel(
                 add1(k)
             if s == 3:
                 interleave("scalar", ("z1", 1, 1))
-            if 0 < s < 8:
+            if 0 < s < 8 and s not in (5, 6,):
                 turned[s - 1] = turn2(s - 1)
             if s == 6:
-                interleave("scalar", ("z1", 2, 1))
+                interleave("scalar", ("z1", 2, 1), HALVES[0])
             for i in (2 * s, 2 * s + 1):
                 if s < 7:
                     mm2(i)
@@ -453,8 +458,12 @@ def tile_teacher_student_logits_t1_kernel(
                     mm2(i, (1,))
             add2(2 * s + 1)
             add2(2 * s)
+            if s in (5, 6,):
+                turned[s - 1] = turn2(s - 1)
             if s < 3:
                 affinity_run = turn_affinity(s + 1)
+            if s == 6:
+                interleave("scalar", ("z1", 2, 1), HALVES[1])
             if s >= 2:
                 finish(s - 2)
             if 8 <= s < 11:
@@ -489,12 +498,12 @@ def tile_teacher_student_logits_t1_kernel(
                 interleave("scalar", interleaved[s])
             if s == 2:
                 interleave("scalar", ("z1", 1, 0))
+        gain_mul_tile(23, nc.vector, 13)
         quantise(turned[11])
-        gain_mul(11, tiles=slice(0, 1))
-        gain_mul(11, tiles=slice(1, 2))
+        gain_mul_tile(22, nc.gpsimd, 12)
         finish(10)
         mm3(22)
         mm3(23)
-        for i in (22, 23):
+        for i in (23, 22):
             add3(i)
             store_tile(i)

@@ -37,10 +37,14 @@ def tile_teacher_student_logits_t1_kernel(
 
         counts = {}
 
+        last_tag = {}
+        held = {}
+
         def ring(pool, name, depth, shape, dtype):
             n = counts.get(name, 0)
             counts[name] = n + 1
             tag = name + str(n % depth)
+            last_tag[name] = tag
             if pool is psum:
                 return pool.tile(shape, dtype, name=tag, tag=tag)
             return pool.tile(shape, dtype, name=tag, tag=tag, align_bytes=64)
@@ -158,9 +162,21 @@ def tile_teacher_student_logits_t1_kernel(
                 nc.scalar.copy(out=o, in_=s)
 
         def interleave(engine, key, cols=WHOLE):
+            if key in held and key not in grouped:
+                grouped[key] = sbuf.tile([P, 512, 4], BF16, name=held[key], tag=held[key], align_bytes=64)
             if key not in grouped:
                 grouped[key] = ring(sbuf, "grouped", 4, [P, 512, 4], BF16)
             src = z1[key[1:]] if key[0] == "z1" else loaded[key]
+            if engine == "gpsimd":
+                nc.gpsimd.tensor_scalar(
+                    out=grouped[key][:, cols, :],
+                    in0=src[:, :, cols].rearrange("p t n -> p n t"),
+                    scalar1=1.0,
+                    scalar2=0.0,
+                    op0=MULT,
+                    op1=ADD,
+                )
+                return
             copy_on(
                 engine,
                 grouped[key][:, cols, :].rearrange("p (n i) t -> p n t i", i=4),
@@ -192,6 +208,17 @@ def tile_teacher_student_logits_t1_kernel(
             for n, key in enumerate(keys):
                 copy_on(engine, ordered[:, n], words[key].rearrange("p a (m u) -> p a u m", u=2))
                 sorted_words[key] = ordered[:, n]
+
+        def sort_affinity(engine, n):
+            key = ("a", n // 2, n % 2)
+            ordered = ring(sbuf, "result", 3, [P, 2, 2, 2, P], F32)
+            copy_on(
+                engine,
+                ordered[:].rearrange("p a c u m -> p (a c) u m"),
+                loaded[key][:].bitcast(F32).rearrange("p a (c m u) -> p (a c) u m", c=2, u=2),
+            )
+            for c in range(2):
+                sorted_words[key + (c,)] = ordered[:, :, c]
 
         def turn(*keys, late=False):
             run = (keys[0][0], "run", *keys)
@@ -344,8 +371,7 @@ def tile_teacher_student_logits_t1_kernel(
         def turn_affinity(n):
             return turn(("a", n // 2, n % 2, 0), ("a", n // 2, n % 2, 1), late=n == 1)
 
-        nc.scalar.dma_start(out=gain_in[:], in_=gain.rearrange("(h p j) -> p h j", p=P, j=4))
-        nc.scalar.dma_start(out=keep_sb[:], in_=keep.rearrange("(g p t) -> p g t", p=P, t=4))
+        nc.sync.dma_start(out=gain_in[:], in_=gain.rearrange("(h p j) -> p h j", p=P, j=4))
         load_confusion(0, 0)
         load_teacher(0, 0, (0,))
         load_teacher(0, 0, (1,))
@@ -361,6 +387,7 @@ def tile_teacher_student_logits_t1_kernel(
         load_confusion(1, 2)
         load_student(0, 1)
         load_affinity(0, 0)
+        nc.sync.dma_start(out=keep_sb[:], in_=keep.rearrange("(g p t) -> p g t", p=P, t=4))
         make_identity(nc, ident[:])
         nc.scalar.copy(out=gain_f32[:], in_=gain_in[:])
         for h in range(G):
@@ -419,13 +446,15 @@ def tile_teacher_student_logits_t1_kernel(
         a0 = turn_affinity(0)
         add1(3)
         interleave("scalar", ("z1", 0, 1), HALVES[0])
+        held["w", 0] = last_tag["grouped"]
         quantise_all(("c", 1, 1), ("c", 1, 2))
         interleave("vector", ("z1", 0, 1), HALVES[1])
         quantise(a0)
         quantise(("z1", 0, 1), HALVES[1])
         quantise(("z1", 0, 1), HALVES[0])
-        sort_words("vector", *aff(1))
-        interleave("scalar", ("w", 0))
+        sort_affinity("scalar", 1)
+        interleave("gpsimd", ("w", 0), HALVES[0])
+        interleave("scalar", ("w", 0), HALVES[1])
 
         first_pairs = {0: [4], 1: [5], 2: [6], 3: [7], 4: [8], 5: [9, 10], 6: [11]}
         interleaved = {0: ("c", 2, 0), 1: ("c", 2, 1), 2: ("c", 2, 2), 3: ("w", 1), 4: ("w", 2), 5: ("z1", 2, 0)}
@@ -466,6 +495,9 @@ def tile_teacher_student_logits_t1_kernel(
                 interleave("scalar", ("z1", 2, 1), HALVES[1])
             if s >= 2:
                 finish(s - 2)
+            if s == 7:
+                mm2(16, (0,))
+                mm2(17, (0,))
             if 8 <= s < 11:
                 mm2(2 * s + 2)
                 mm2(2 * s + 3)
@@ -474,15 +506,13 @@ def tile_teacher_student_logits_t1_kernel(
             if s == 3:
                 quantise_all(("c", 2, 2), ("z1", 1, 0))
             if s == 7:
-                mm2(16, (0,))
-                mm2(17, (0,))
                 quantise(("z1", 2, 1))
             if s in (4, 6):
                 quantise(turned[s - 1])
             if s in quantised:
                 quantise(quantised[s])
             if s < 2:
-                sort_words("vector", *aff(s + 2))
+                sort_affinity("vector", s + 2)
             if 0 < s < 3:
                 quantise(affinity_run)
             if s == 3:

@@ -15,14 +15,21 @@ FP8X4 = mybir.dt.float8_e4m3fn_x4
 MULT = mybir.AluOpType.mult
 ADD = mybir.AluOpType.add
 
-BLOCK_BYTES = 4 * 512 * 2
-TEACHER_BYTES = 2 * C * 2
+BLOCK = 4 * 512 * 2
 WHOLE = slice(0, 512)
 HALVES = (slice(0, 256), slice(256, 512))
-TURN_BANKS = 3
-SUM_BANKS = 5
+BANKS = 8
 LATE_SLOTS = 4
-GPSIMD_COLS = 384
+GROUPED = 4
+TURNED = 3
+GPSIMD_COLS = 192
+PLACE = {
+    ("tpass", 0, 0): 0, ("tpass", 0, 1): 1, ("tpass", 0, 2): 2, ("t", 1, 0): 3, ("t", 1, 1): 4.5,
+    ("c", 0, 0): 6, ("c", 0, 1): 7, ("c", 0, 2): 8, ("s", 0, 0): 9, ("s", 0, 1): 10,
+    ("c", 1, 0): 11, ("c", 1, 1): 12, ("c", 1, 2): 13, ("a", 0, 0): 14, ("a", 0, 1): 15,
+    ("a", 1, 0): 0, ("a", 1, 1): 1, ("w", 1): 2, ("c", 2, 0): 3, ("c", 2, 1): 4, ("c", 2, 2): 5,
+    ("s", 1, 0): 6, ("s", 1, 1): 7, ("w", 0): 8, ("s", 2, 0): 9, ("s", 2, 1): 10, ("w", 2): 11,
+}
 
 
 def tile_teacher_student_logits_t1_kernel(
@@ -36,15 +43,12 @@ def tile_teacher_student_logits_t1_kernel(
         ctx.enter_context(tc.manual_schedule())
 
         counts = {}
-
-        last_tag = {}
-        held = {}
+        banks = {}
 
         def ring(pool, name, depth, shape, dtype):
             n = counts.get(name, 0)
             counts[name] = n + 1
             tag = name + str(n % depth)
-            last_tag[name] = tag
             if pool is psum:
                 return pool.tile(shape, dtype, name=tag, tag=tag)
             return pool.tile(shape, dtype, name=tag, tag=tag, align_bytes=64)
@@ -53,11 +57,17 @@ def tile_teacher_student_logits_t1_kernel(
             tag = "late" + str(n % LATE_SLOTS)
             return sbuf.tile(shape, dtype, name=tag, tag=tag, align_bytes=64)
 
-        def turn_bank(shape):
-            return ring(psum, "turn", TURN_BANKS, shape, F32)
+        free_banks = list(range(BANKS))
+        bank_of = {}
 
-        def sum_bank():
-            return ring(psum, "sum", SUM_BANKS, [P, 512], F32)
+        def take_bank(key, shape, newest=False):
+            bank_of[key] = free_banks.pop(-1 if newest else 0)
+            tag = "bank" + str(bank_of[key])
+            banks[key] = psum.tile(shape, F32, name=tag, tag=tag)
+            return banks[key]
+
+        def give_back(key):
+            free_banks.append(bank_of[key])
 
         teacher_v = teacher.rearrange("(g p t) k -> g p t k", p=P, t=4)
         affinity_v = affinity.rearrange("(g p t) k -> g p t k", p=P, t=4)
@@ -73,72 +83,54 @@ def tile_teacher_student_logits_t1_kernel(
         parts = {}
         codes = {}
         scales = {}
-        banks = {}
         z1 = {}
         z2 = {}
         result = {}
         gained = {}
 
-        def raw_tile(key, shape, offset):
+        def raw_tile(key, shape):
             name = "raw_" + "_".join(str(x) for x in key)
-            loaded[key] = raw.tile(shape, BF16, name=name, tag=name, align_bytes=64, offset=offset)
+            loaded[key] = raw.tile(shape, BF16, name=name, tag=name, align_bytes=64, offset=int(PLACE[key] * BLOCK))
             return loaded[key]
 
-        teacher_at = 0
-        first_at = 4 * TEACHER_BYTES
-        rest_at = first_at + 3 * BLOCK_BYTES
-        place = {
-            ("c", 0, 0): first_at,
-            ("c", 0, 1): first_at + BLOCK_BYTES,
-            ("c", 0, 2): first_at + 2 * BLOCK_BYTES,
-            ("s", 1, 0): first_at,
-            ("s", 1, 1): first_at + BLOCK_BYTES,
-            ("w", 1): first_at + 2 * BLOCK_BYTES,
-            ("c", 2, 0): teacher_at,
-            ("c", 2, 1): teacher_at + BLOCK_BYTES,
-            ("c", 2, 2): teacher_at + 2 * BLOCK_BYTES,
-            ("s", 2, 0): teacher_at + 3 * BLOCK_BYTES,
-            ("s", 2, 1): teacher_at + 4 * BLOCK_BYTES,
-            ("w", 2): teacher_at + 5 * BLOCK_BYTES,
-        }
-        own = [("s", 0, 0), ("s", 0, 1), ("w", 0), ("c", 1, 0), ("c", 1, 1), ("c", 1, 2)]
-        own.extend(("a", g, q) for g in range(2) for q in range(2))
-        for n, key in enumerate(own):
-            place[key] = rest_at + n * BLOCK_BYTES
+        def load(key):
+            if key[0] == "c":
+                t = raw_tile(key, [P, 4, 512])
+                nc.sync.dma_start(out=t[:], in_=confusion_v[key[2], :, :, key[1] * 512 : (key[1] + 1) * 512])
+            if key[0] == "s":
+                t = raw_tile(key, [P, 4, 512])
+                nc.sync.dma_start(out=t[:], in_=student_v[key[2], :, :, key[1] * 512 : (key[1] + 1) * 512])
+            if key[0] == "t":
+                g, q = key[1:]
+                t = raw_tile(key, [P, 2, C])
+                nc.sync.dma_start(out=t[:], in_=teacher_v[g, :, 2 * q : 2 * q + 2, :])
+                for c in range(3):
+                    words["t", g, q, c] = t[:].bitcast(F32)[:, :, 256 * c : 256 * (c + 1)]
+            if key[0] == "tunit":
+                g, q, c = key[1:]
+                t = raw_tile(key, [P, 2, 512])
+                nc.sync.dma_start(out=t[:], in_=teacher_v[g, :, 2 * q : 2 * q + 2, 512 * c : 512 * (c + 1)])
+                words["t", g, q, c] = t[:].bitcast(F32)
+            if key[0] == "tpass":
+                g, c = key[1:]
+                t = raw_tile(key, [P, 4, 512])
+                nc.sync.dma_start(out=t[:], in_=teacher_v[g, :, :, 512 * c : 512 * (c + 1)])
+                for q in range(2):
+                    words["t", g, q, c] = t[:].bitcast(F32)[:, 2 * q : 2 * q + 2, :]
+            if key[0] == "a":
+                g, q = key[1:]
+                t = raw_tile(key, [P, 2, B])
+                nc.sync.dma_start(out=t[:], in_=affinity_v[g, :, 2 * q : 2 * q + 2, :])
+                for c in range(2):
+                    words["a", g, q, c] = t[:].bitcast(F32)[:, :, 256 * c : 256 * (c + 1)]
+            if key[0] == "w":
+                t = raw_tile(key, [P, 4, 512])
+                for r in range(4):
+                    nc.sync.dma_start(out=t[r:P:4], in_=within_v[key[1], r])
 
-        def load_confusion(h, c):
-            t = raw_tile(("c", h, c), [P, 4, 512], place["c", h, c])
-            nc.sync.dma_start(out=t[:], in_=confusion_v[c, :, :, h * 512 : (h + 1) * 512])
-
-        def load_student(h, g):
-            t = raw_tile(("s", h, g), [P, 4, 512], place["s", h, g])
-            nc.sync.dma_start(out=t[:], in_=student_v[g, :, :, h * 512 : (h + 1) * 512])
-
-        def load_teacher(g, q, passes=(0, 1, 2)):
-            width = 512 * len(passes)
-            at = teacher_at + (2 * g + q) * TEACHER_BYTES + passes[0] * TEACHER_BYTES // 3
-            t = raw_tile(("t", g, q, passes[0]), [P, 2, width], at)
-            k0 = 512 * passes[0]
-            nc.sync.dma_start(out=t[:], in_=teacher_v[g, :, 2 * q : 2 * q + 2, k0 : k0 + width])
-            for c in passes:
-                words["t", g, q, c] = t[:].bitcast(F32)[:, :, 256 * (c - passes[0]) : 256 * (c - passes[0] + 1)]
-
-        def load_teacher_pass(c):
-            t = raw_tile(("t", 0, "pass", c), [P, 4, 512], teacher_at + c * BLOCK_BYTES)
-            nc.sync.dma_start(out=t[:], in_=teacher_v[0, :, :, 512 * c : 512 * (c + 1)])
-            for q in range(2):
-                words["t", 0, q, c] = t[:].bitcast(F32)[:, 2 * q : 2 * q + 2, :]
-
-        def load_affinity(g, q):
-            t = raw_tile(("a", g, q), [P, 2, B], place["a", g, q])
-            nc.sync.dma_start(out=t[:], in_=affinity_v[g, :, 2 * q : 2 * q + 2, :])
-            for c in range(2):
-                words["a", g, q, c] = t[:].bitcast(F32)[:, :, 256 * c : 256 * (c + 1)]
-
-        def load_within(h):
-            t = raw_tile(("w", h), [P, 4, 512], place["w", h])
-            for r in range(4):
-                nc.sync.dma_start(out=t[r:P:4], in_=within_v[h, r])
+        def load_all(*keys):
+            for key in keys:
+                load(key)
 
         ident = sbuf.tile([P, P], F32, name="ident", tag="ident")
         keep_sb = sbuf.tile([P, 2, 4], BF16, name="keep_sb", tag="keep_sb")
@@ -147,13 +139,16 @@ def tile_teacher_student_logits_t1_kernel(
         gain_sb = sbuf.tile([P, G, 512], BF16, name="gain_sb", tag="gain_sb", align_bytes=64)
 
         def spread_gain(h):
-            bank = turn_bank([P, 4, P])
+            bank = take_bank(("gain", h), [P, 4, P])
             for j in range(4):
                 nc.tensor.transpose(bank[:, j, :], gain_f32[:, h, j : j + 1].to_broadcast([P, P]), ident[:])
+
+        def fetch_gain(h):
             nc.scalar.copy(
                 out=gain_sb[:, h, :].rearrange("p (u b r) -> p u b r", u=4, r=4),
-                in_=bank[:].rearrange("p r (b u) -> p u b r", u=4),
+                in_=banks["gain", h][:].rearrange("p r (b u) -> p u b r", u=4),
             )
+            give_back(("gain", h))
 
         def copy_on(engine, o, s):
             if engine == "vector":
@@ -161,11 +156,14 @@ def tile_teacher_student_logits_t1_kernel(
             else:
                 nc.scalar.copy(out=o, in_=s)
 
-        def interleave(engine, key, cols=WHOLE):
-            if key in held and key not in grouped:
-                grouped[key] = sbuf.tile([P, 512, 4], BF16, name=held[key], tag=held[key], align_bytes=64)
+        free_groups = list(range(GROUPED))
+        group_of = {}
+
+        def interleave(engine, key, cols=WHOLE, newest=False):
             if key not in grouped:
-                grouped[key] = ring(sbuf, "grouped", 4, [P, 512, 4], BF16)
+                group_of[key] = free_groups.pop(-1 if newest else 0)
+                tag = "grouped" + str(group_of[key])
+                grouped[key] = sbuf.tile([P, 512, 4], BF16, name=tag, tag=tag, align_bytes=64)
             src = z1[key[1:]] if key[0] == "z1" else loaded[key]
             if engine == "gpsimd":
                 nc.gpsimd.tensor_scalar(
@@ -176,12 +174,12 @@ def tile_teacher_student_logits_t1_kernel(
                     op0=MULT,
                     op1=ADD,
                 )
-                return
-            copy_on(
-                engine,
-                grouped[key][:, cols, :].rearrange("p (n i) t -> p n t i", i=4),
-                src[:, :, cols].rearrange("p t (n i) -> p n t i", i=4),
-            )
+            else:
+                copy_on(
+                    engine,
+                    grouped[key][:, cols, :].rearrange("p (n i) t -> p n t i", i=4),
+                    src[:, :, cols].rearrange("p t (n i) -> p n t i", i=4),
+                )
 
         depth = {"c": 6, "w": 2, "z1": 4, "t": 12, "a": 4, "z2": 2}
 
@@ -202,6 +200,12 @@ def tile_teacher_student_logits_t1_kernel(
                 scales=scales[key][:, cols],
                 in_=grouped[key][:, cols, :].rearrange("p n t -> p (n t)"),
             )
+            if key in group_of and cols.stop == width:
+                free_groups.append(group_of[key])
+
+        def quantise_all(*keys):
+            for key in keys:
+                quantise(key)
 
         def sort_words(engine, *keys):
             ordered = ring(sbuf, "result", 3, [P, len(keys), 2, 2, P], F32)
@@ -209,33 +213,45 @@ def tile_teacher_student_logits_t1_kernel(
                 copy_on(engine, ordered[:, n], words[key].rearrange("p a (m u) -> p a u m", u=2))
                 sorted_words[key] = ordered[:, n]
 
-        def sort_affinity(engine, n):
-            key = ("a", n // 2, n % 2)
-            ordered = ring(sbuf, "result", 3, [P, 2, 2, 2, P], F32)
-            copy_on(
-                engine,
-                ordered[:].rearrange("p a c u m -> p (a c) u m"),
-                loaded[key][:].bitcast(F32).rearrange("p a (c m u) -> p (a c) u m", c=2, u=2),
-            )
-            for c in range(2):
-                sorted_words[key + (c,)] = ordered[:, :, c]
+        def sort_block(engine, key):
+            ordered = ring(sbuf, "result", 3, [P, 4, 2, P], F32)
+            flat = loaded[key][:].rearrange("p a n -> p (a n)").bitcast(F32)
+            copy_on(engine, ordered[:], flat.rearrange("p (j m u) -> p j u m", j=4, u=2))
+            for n in range(2):
+                if key[0] == "a":
+                    sorted_words[key + (n,)] = ordered[:, n:4:2]
+                else:
+                    sorted_words["t", key[1], n, key[2]] = ordered[:, 2 * n : 2 * n + 2]
 
-        def turn(*keys, late=False):
+        def sort_pair(engine, key):
+            ordered = ring(sbuf, "sorted", 2, [P, 6, 2, P], F32)
+            flat = loaded[key][:].rearrange("p a n -> p (a n)").bitcast(F32)
+            copy_on(engine, ordered[:], flat.rearrange("p (j m u) -> p j u m", j=6, u=2))
+            for c in range(3):
+                sorted_words[key + (c,)] = ordered[:, c:6:3]
+
+        def turn(*keys):
             run = (keys[0][0], "run", *keys)
             parts[run] = keys
             for key in keys:
-                banks[key] = turn_bank([P, 2, 2, P])
+                take_bank(key, [P, 2, 2, P])
                 for a in range(2):
                     for u in range(2):
                         src = sorted_words[key][:, a, u] if key in sorted_words else words[key][:, a, u:256:2]
                         nc.tensor.transpose(banks[key][:, a, u, :], src, ident[:])
+            return run
+
+        def fetch(run, engines=("scalar", "scalar"), late=False):
+            keys = parts[run]
             shape = [P, 256 * len(keys), 4]
-            grouped[run] = late_slot(0, shape, BF16) if late else ring(sbuf, "turned", 3, shape, BF16)
+            grouped[run] = late_slot(0, shape, BF16) if late else ring(sbuf, "turned", TURNED, shape, BF16)
             for n, key in enumerate(keys):
-                nc.scalar.copy(
-                    out=grouped[run][:, 256 * n : 256 * (n + 1), :].bitcast(F32).rearrange("p (a r) u -> p a r u", a=2),
-                    in_=banks[key][:].rearrange("p a u r -> p a r u"),
+                copy_on(
+                    engines[n],
+                    grouped[run][:, 256 * n : 256 * (n + 1), :].bitcast(F32).rearrange("p (a r) u -> p a r u", a=2),
+                    banks[key][:].rearrange("p a u r -> p a r u"),
                 )
+                give_back(key)
             return run
 
         def product(bank, left, cols, right, start, stop):
@@ -252,15 +268,17 @@ def tile_teacher_student_logits_t1_kernel(
         def pair(s):
             return s // 4, s // 2 % 2, s % 2
 
-        def mm1(s, passes=(0, 1, 2), by_pass=False, tiles=(0, 1)):
+        def mm1(s, passes=(0, 1, 2), by_pass=False):
             h, g, q = pair(s)
-            order = [(a, c) for a in tiles for c in passes]
+            order = [(a, c) for a in range(2) for c in passes]
             if by_pass:
-                order = [(a, c) for c in passes for a in tiles]
+                order = [(a, c) for c in passes for a in range(2)]
             for a, c in order:
-                if c == 0:
-                    banks["z1", s, a] = sum_bank()
-                product(banks["z1", s, a], ("t", g, q, c), slice(a * P, (a + 1) * P), ("c", h, c), c == 0, c == 2)
+                n = counts.get(("z1", s, a), 0)
+                counts["z1", s, a] = n + 1
+                if n == 0:
+                    take_bank(("z1", s, a), [P, 512])
+                product(banks["z1", s, a], ("t", g, q, c), slice(a * P, (a + 1) * P), ("c", h, c), n == 0, n == 2)
 
         def add1(s, tiles=(1, 0)):
             h, g, q = pair(s)
@@ -274,93 +292,87 @@ def tile_teacher_student_logits_t1_kernel(
                     in1=loaded["s", h, g][:, t, :].rearrange("p (b u r) -> p b u r", u=4, r=4),
                     op=ADD,
                 )
+                give_back(("z1", s, a))
 
-        def tile(i):
-            return i // 8, i // 4 % 2, i % 4
+        def mm2(s, passes=(0, 1), by_pass=False, newest=False):
+            h, g, q = pair(s)
+            order = [(a, c) for a in range(2) for c in passes]
+            if by_pass:
+                order = [(a, c) for c in passes for a in range(2)]
+            for a, c in order:
+                first = ("z2", s, a) not in banks
+                if first:
+                    take_bank(("z2", s, a), [P, 512], newest)
+                product(banks["z2", s, a], ("a", g, q, c), slice(a * P, (a + 1) * P), ("z1", h, c), first, not first)
 
-        def mm2(i, passes=(0, 1)):
-            h, g, t = tile(i)
-            cols = slice(t % 2 * P, (t % 2 + 1) * P)
-            for c in passes:
-                if c == 0:
-                    banks["z2", i] = sum_bank()
-                product(banks["z2", i], ("a", g, t // 2, c), cols, ("z1", h, c), c == 0, c == 1)
+        def add2(s, tiles=(1, 0)):
+            h, g, q = pair(s)
+            if s not in z2:
+                z2[s] = ring(sbuf, "z2", 3, [P, 2, 512], F32)
+            for a in tiles:
+                t = 2 * q + a
+                nc.vector.scalar_tensor_tensor(
+                    out=z2[s][:, a, :],
+                    in0=z1[h, g][:, t, :],
+                    scalar=keep_sb[:, g, t : t + 1],
+                    in1=banks["z2", s, a][:],
+                    op0=MULT,
+                    op1=ADD,
+                )
+                give_back(("z2", s, a))
 
-        def add2(i):
-            h, g, t = tile(i)
-            if i // 2 not in z2:
-                z2[i // 2] = ring(sbuf, "z2", 3, [P, 2, 512], F32)
-            nc.vector.scalar_tensor_tensor(
-                out=z2[i // 2][:, i % 2, :],
-                in0=z1[h, g][:, t, :],
-                scalar=keep_sb[:, g, t : t + 1],
-                in1=banks["z2", i][:],
-                op0=MULT,
-                op1=ADD,
-            )
-
-        def gain_mul(k):
-            pair_tile = late_slot(k, [P, 2, 512], F32)
+        def gain_mul(s):
+            pair_tile = late_slot(s, [P, 2, 512], F32)
             for a in range(2):
-                gained[2 * k + a] = pair_tile[:, a, :]
+                gained[s, a] = pair_tile[:, a, :]
             nc.gpsimd.tensor_tensor(
                 out=pair_tile[:],
-                in0=z2[k][:],
-                in1=gain_sb[:, k // 4, :].unsqueeze(1).to_broadcast([P, 2, 512]),
+                in0=z2[s][:],
+                in1=gain_sb[:, s // 4, :].unsqueeze(1).to_broadcast([P, 2, 512]),
                 op=MULT,
             )
 
-        def gain_mul_tile(i, engine, slot):
-            gained[i] = late_slot(slot, [P, 512], F32)[:]
-            engine.tensor_tensor(out=gained[i], in0=z2[i // 2][:, i % 2, :], in1=gain_sb[:, i // 8, :], op=MULT)
+        def gain_mul_tile(s, a, engine, slot):
+            gained[s, a] = late_slot(slot, [P, 512], F32)[:]
+            engine.tensor_tensor(out=gained[s, a], in0=z2[s][:, a, :], in1=gain_sb[:, s // 4, :], op=MULT)
 
-        def turn2(k):
-            run = ("z2", "run", k)
-            parts[run] = [("z2", 2 * k), ("z2", 2 * k + 1)]
+        def turn2(s):
             for a in range(2):
-                banks["z2t", a] = turn_bank([P, 4, P])
+                take_bank(("z2t", s, a), [P, 4, P])
                 for u in range(4):
-                    nc.tensor.transpose(banks["z2t", a][:, u, :], z2[k][:, a, u * P : (u + 1) * P], ident[:])
-            grouped[run] = late_slot(k + 1, [P, 2 * P, 4], BF16)
+                    nc.tensor.transpose(banks["z2t", s, a][:, u, :], z2[s][:, a, u * P : (u + 1) * P], ident[:])
+
+        def fetch2(s):
+            run = ("z2", s)
+            grouped[run] = late_slot(s + 1, [P, 2 * P, 4], BF16)
             for a in range(2):
                 nc.scalar.copy(
-                    out=grouped[run][:, a * P : (a + 1) * P, :], in_=banks["z2t", a][:].rearrange("p u n -> p n u")
+                    out=grouped[run][:, a * P : (a + 1) * P, :],
+                    in_=banks["z2t", s, a][:].rearrange("p u n -> p n u"),
                 )
-            return run
+                give_back(("z2t", s, a))
 
-        def mm3(i):
-            banks["out", i] = sum_bank()
-            product(banks["out", i], ("z2", i), slice(0, P), ("w", i // 8), True, True)
+        def mm3(s):
+            for a in range(2):
+                take_bank(("out", s, a), [P, 512])
+                product(banks["out", s, a], ("z2", s), slice(a * P, (a + 1) * P), ("w", s // 4), True, True)
 
-        def add3(i):
-            if i // 2 not in result:
-                result[i // 2] = ring(sbuf, "result", 3, [P, 2, 512], F32)
-            nc.vector.tensor_tensor(
-                out=result[i // 2][:, i % 2, :].rearrange("p (b u r) -> p b u r", u=4, r=4),
-                in0=banks["out", i][:].rearrange("p (b u r) -> p b u r", u=4, r=4),
-                in1=gained[i].rearrange("p (u b r) -> p b u r", u=4, r=4),
-                op=ADD,
-            )
+        def add3(s, tiles=(1, 0)):
+            if s not in result:
+                result[s] = ring(sbuf, "result", 3, [P, 2, 512], F32)
+            for a in tiles:
+                nc.vector.tensor_tensor(
+                    out=result[s][:, a, :].rearrange("p (b u r) -> p b u r", u=4, r=4),
+                    in0=banks["out", s, a][:].rearrange("p (b u r) -> p b u r", u=4, r=4),
+                    in1=gained[s, a].rearrange("p (u b r) -> p b u r", u=4, r=4),
+                    op=ADD,
+                )
+                give_back(("out", s, a))
 
-        def store(k):
-            h, g, q = pair(k)
-            nc.sync.dma_start(out=out_v[g, :, 2 * q : 2 * q + 2, h * 512 : (h + 1) * 512], in_=result[k][:])
-
-        def store_tile(i):
-            h, g, t = tile(i)
-            nc.sync.dma_start(out=out_v[g, :, t, h * 512 : (h + 1) * 512], in_=result[i // 2][:, i % 2, :])
-
-        def quantise_all(*keys):
-            for key in keys:
-                quantise(key)
-
-        def both(engine, key):
-            for cols in HALVES:
-                interleave(engine, key, cols)
-
-        def shared(key):
-            interleave("scalar", key, HALVES[0])
-            interleave("vector", key, HALVES[1])
+        def store(s, tiles=slice(0, 2)):
+            h, g, q = pair(s)
+            rows = slice(2 * q + tiles.start, 2 * q + tiles.stop)
+            nc.sync.dma_start(out=out_v[g, :, rows, h * 512 : (h + 1) * 512], in_=result[s][:, tiles, :])
 
         def tea(i):
             return ("t", i // 6, i // 3 % 2, i % 3)
@@ -368,172 +380,141 @@ def tile_teacher_student_logits_t1_kernel(
         def aff(n):
             return ("a", n // 2, n % 2, 0), ("a", n // 2, n % 2, 1)
 
-        def turn_affinity(n):
-            return turn(("a", n // 2, n % 2, 0), ("a", n // 2, n % 2, 1), late=n == 1)
+        def passes1(*units):
+            for i in units:
+                mm1(i // 3, (i % 3,))
 
+        def part(engine, key, start, stop, newest=False):
+            interleave(engine, key, slice(start, stop), newest)
+
+        for c in range(3):
+            load_all(("tpass", 0, c), ("c", 0, c))
+        load_all(("t", 1, 0), ("s", 0, 0), ("t", 1, 1), ("c", 1, 0))
         nc.sync.dma_start(out=gain_in[:], in_=gain.rearrange("(h p j) -> p h j", p=P, j=4))
-        load_confusion(0, 0)
-        load_teacher(0, 0, (0,))
-        load_teacher(0, 0, (1,))
-        load_confusion(0, 1)
-        load_teacher(0, 0, (2,))
-        load_teacher(0, 1)
-        load_confusion(0, 2)
-        load_confusion(1, 0)
-        load_teacher(1, 0)
-        load_student(0, 0)
-        load_teacher(1, 1)
-        load_confusion(1, 1)
-        load_confusion(1, 2)
-        load_student(0, 1)
-        load_affinity(0, 0)
+        load_all(("s", 0, 1), ("c", 1, 1), ("c", 1, 2), ("a", 0, 0), ("a", 0, 1))
         nc.sync.dma_start(out=keep_sb[:], in_=keep.rearrange("(g p t) -> p g t", p=P, t=4))
         make_identity(nc, ident[:])
-        nc.scalar.copy(out=gain_f32[:], in_=gain_in[:])
-        for h in range(G):
-            spread_gain(h)
 
+        r0 = fetch(turn(tea(0), tea(3)))
         interleave("vector", ("c", 0, 0))
-        t0 = turn(tea(0))
-        t1 = turn(tea(1))
-        quantise_all(("c", 0, 0), t0)
-        mm1(0, (0,))
-        shared(("c", 0, 1))
-        quantise(t1)
-        t2 = turn(tea(2))
-        quantise_all(("c", 0, 1), t2)
-        mm1(0, (1,))
+        r1 = fetch(turn(tea(1), tea(4)))
+        quantise_all(r0, ("c", 0, 0))
+        passes1(0, 3)
+        interleave("vector", ("c", 0, 1))
+        sort_block("scalar", ("tpass", 0, 2))
+        r2 = fetch(turn(tea(2), tea(5)))
+        quantise_all(r1, ("c", 0, 1))
+        passes1(1, 4)
         interleave("vector", ("c", 0, 2))
-        t3 = turn(tea(3))
-        t4 = turn(tea(4), tea(5))
-        load_student(1, 0)
-        load_affinity(0, 1)
-        load_within(0)
-        quantise_all(t3, ("c", 0, 2), t4)
-        mm1(1, (0,))
-        mm1(0, (2,))
-        interleave("vector", ("c", 1, 0))
-        sort_words("scalar", tea(6), tea(7))
+        load_all(("a", 1, 0), ("s", 1, 0), ("w", 0), ("a", 1, 1))
         sort_words("scalar", tea(8))
-        t6 = turn(tea(6), tea(7))
-        mm1(1, (1, 2))
+        r6 = fetch(turn(tea(6), tea(7)))
+        quantise_all(r2, ("c", 0, 2))
+        passes1(2, 5)
+        quantise(r6)
+        r8 = turn(tea(8), tea(9))
+        sort_words("scalar", tea(10), tea(11))
+        fetch(r8)
+        part("gpsimd", ("c", 1, 0), 256, 512, True)
         add1(0)
-        quantise_all(("c", 1, 0), t6)
-        t8 = turn(tea(8), tea(9))
         add1(1)
-        mm1(2, (0, 1))
+        passes1(6, 7)
+        nc.scalar.copy(out=gain_f32[:], in_=gain_in[:])
+        part("scalar", ("c", 1, 0), 0, 256)
+        r10 = turn(tea(10), tea(11))
+        spread_gain(0)
+        fetch(r10)
+        load_all(("c", 2, 0), ("c", 2, 1), ("s", 1, 1), ("c", 2, 2), ("w", 1))
+        fetch_gain(0)
+        quantise(r8)
+        passes1(8, 9)
+        spread_gain(1)
+        fetch_gain(1)
         interleave("vector", ("z1", 0, 0))
-        quantise(t8)
-        interleave("scalar", ("c", 1, 1), HALVES[0])
-        t10 = turn(tea(10))
-        t11 = turn(tea(11))
-        load_confusion(2, 0)
-        load_affinity(1, 0)
-        load_student(1, 1)
-        load_confusion(2, 1)
-        load_affinity(1, 1)
-        load_confusion(2, 2)
-        load_within(1)
-        load_student(2, 0)
-        load_student(2, 1)
-        load_within(2)
-        mm1(2, (2,))
-        quantise_all(("z1", 0, 0), t10, t11)
-        interleave("scalar", ("c", 1, 1), HALVES[1])
+        quantise(r10)
+        passes1(10, 11)
         interleave("scalar", ("c", 1, 2))
-        mm1(3)
+        quantise_all(("c", 1, 0), ("z1", 0, 0))
+        part("gpsimd", ("c", 1, 1), 96, 512, True)
+        a0 = fetch(turn(*aff(0)))
         add1(2)
-        a0 = turn_affinity(0)
+        mm1(4, (0,))
         add1(3)
-        interleave("scalar", ("z1", 0, 1), HALVES[0])
-        held["w", 0] = last_tag["grouped"]
-        quantise_all(("c", 1, 1), ("c", 1, 2))
-        interleave("vector", ("z1", 0, 1), HALVES[1])
-        quantise(a0)
-        quantise(("z1", 0, 1), HALVES[1])
-        quantise(("z1", 0, 1), HALVES[0])
-        sort_affinity("scalar", 1)
-        interleave("gpsimd", ("w", 0), HALVES[0])
-        interleave("scalar", ("w", 0), HALVES[1])
+        load_all(("s", 2, 0), ("s", 2, 1), ("w", 2))
+        a1 = turn(*aff(1))
+        part("scalar", ("z1", 0, 1), 0, 192)
+        quantise(("c", 1, 2))
+        mm1(4, (2,))
+        part("vector", ("c", 1, 1), 0, 96)
+        part("vector", ("z1", 0, 1), 192, 512)
+        fetch(a1)
+        quantise(("c", 1, 1))
+        a2 = fetch(turn(*aff(2)), late=True)
+        mm1(4, (1,))
+        quantise_all(a0, ("z1", 0, 1), a1)
+        mm2(0, by_pass=True)
 
-        first_pairs = {0: [4], 1: [5], 2: [6], 3: [7], 4: [8], 5: [9, 10], 6: [11]}
-        interleaved = {0: ("c", 2, 0), 1: ("c", 2, 1), 2: ("c", 2, 2), 3: ("w", 1), 4: ("w", 2), 5: ("z1", 2, 0)}
-        quantised = {0: ("w", 0), 1: ("c", 2, 0), 2: ("c", 2, 1), 4: ("w", 1), 6: ("z1", 2, 0), 7: ("w", 2)}
-
-        def finish(k):
-            mm3(2 * k)
-            mm3(2 * k + 1)
-            add3(2 * k + 1)
-            add3(2 * k)
-            store(k)
-
-        turned = {}
+        early = {1: [("c", 2, 1)], 2: [("z1", 1, 0)], 4: [("w", 1)], 5: [("z1", 2, 0)], 6: [("w", 2)]}
+        helped = {0: ("w", 0), 2: ("c", 2, 2), 3: ("z1", 1, 1), 7: ("z1", 2, 1)}
+        quantised = {0: [a2], 1: [("w", 0), ("c", 2, 0)], 2: [("c", 2, 1), ("c", 2, 2)], 3: [("z1", 1, 1), ("z1", 1, 0)], 5: [("w", 1)], 6: [("z1", 2, 0)], 7: [("z1", 2, 1), ("w", 2)]}
         for s in range(12):
+            border = s in (3, 7)
+            split = 128 if s == 0 else 512 - GPSIMD_COLS
             if s > 0:
                 gain_mul(s - 1)
-            for k in first_pairs.get(s, []):
-                mm1(k, by_pass=k in (4, 8))
-                add1(k)
-            if s == 3:
-                interleave("scalar", ("z1", 1, 1))
-            if 0 < s < 8 and s not in (5, 6,):
-                turned[s - 1] = turn2(s - 1)
-            if s == 6:
-                interleave("scalar", ("z1", 2, 1), HALVES[0])
-            for i in (2 * s, 2 * s + 1):
-                if s < 7:
-                    mm2(i)
-                if s == 8:
-                    mm2(i, (1,))
-            add2(2 * s + 1)
-            add2(2 * s)
-            if s in (5, 6,):
-                turned[s - 1] = turn2(s - 1)
-            if s < 3:
-                affinity_run = turn_affinity(s + 1)
-            if s == 6:
-                interleave("scalar", ("z1", 2, 1), HALVES[1])
             if s >= 2:
-                finish(s - 2)
-            if s == 7:
-                mm2(16, (0,))
-                mm2(17, (0,))
-            if 8 <= s < 11:
-                mm2(2 * s + 2)
-                mm2(2 * s + 3)
-            if s >= 7:
-                turned[s] = turn2(s)
-            if s == 3:
-                quantise_all(("c", 2, 2), ("z1", 1, 0))
-            if s == 7:
-                quantise(("z1", 2, 1))
-            if s in (4, 6):
-                quantise(turned[s - 1])
-            if s in quantised:
-                quantise(quantised[s])
-            if s < 2:
-                sort_affinity("vector", s + 2)
-            if 0 < s < 3:
-                quantise(affinity_run)
-            if s == 3:
-                quantise(("z1", 1, 1))
-            if s > 0 and s not in (4, 6):
-                quantise(turned[s - 1])
+                mm3(s - 2)
+            if border:
+                add1(s + 4)
+            if s in helped:
+                part("gpsimd", helped[s], split, 512, True)
+                part("scalar", helped[s], 0, split)
+            if border:
+                fetch2(s - 1)
             if s == 0:
-                quantise(affinity_run)
-            if s == 6:
-                mm2(2 * s + 2)
-                mm2(2 * s + 3)
-            if s in interleaved:
-                interleave("scalar", interleaved[s])
-            if s == 2:
-                interleave("scalar", ("z1", 1, 0))
-        gain_mul_tile(23, nc.vector, 13)
-        quantise(turned[11])
-        gain_mul_tile(22, nc.gpsimd, 12)
-        finish(10)
-        mm3(22)
-        mm3(23)
-        for i in (23, 22):
-            add3(i)
-            store_tile(i)
+                sort_block("scalar", ("a", 1, 1))
+                interleave("scalar", ("c", 2, 0))
+            if s < 8 and not border:
+                add1(s + 4)
+            for key in early.get(s, []):
+                interleave("scalar", key)
+            add2(s)
+            if s < 7:
+                mm1(s + 5)
+            if s == 7:
+                mm2(s + 1, (0,), newest=True)
+            if s < 11 and not border:
+                mm2(s + 1)
+            if s >= 2:
+                add3(s - 2)
+                store(s - 2)
+            turn2(s)
+            if s == 0:
+                a3 = turn(*aff(3))
+            if s == 4:
+                spread_gain(2)
+            if s not in (2, 6):
+                fetch2(s)
+            if s == 0:
+                fetch(a3)
+            if s == 4:
+                fetch_gain(2)
+            quantise_all(*quantised.get(s, []))
+            if s == 1:
+                quantise(a3)
+            if s > 0:
+                quantise(("z2", s - 1))
+            if s == 3:
+                mm2(s + 1, (1, 0), by_pass=True)
+            if s == 7:
+                mm2(s + 1, (1,))
+        gain_mul_tile(11, 1, nc.vector, 13)
+        quantise(("z2", 11))
+        gain_mul_tile(11, 0, nc.gpsimd, 12)
+        mm3(10)
+        add3(10)
+        store(10)
+        mm3(11)
+        for a in (1, 0):
+            add3(11, (a,))
+            store(11, slice(a, a + 1))

@@ -22,7 +22,7 @@ BANKS = 8
 LATE_SLOTS = 4
 GROUPED = 4
 TURNED = 3
-GPSIMD_COLS = 192
+GPSIMD_COLS = 112
 PLACE = {
     ("tpass", 0, 0): 0, ("tpass", 0, 1): 1, ("tpass", 0, 2): 2, ("t", 1, 0): 3, ("t", 1, 1): 4.5,
     ("c", 0, 0): 6, ("c", 0, 1): 7, ("c", 0, 2): 8, ("s", 0, 0): 9, ("s", 0, 1): 10,
@@ -415,12 +415,12 @@ def tile_teacher_student_logits_t1_kernel(
         r8 = turn(tea(8), tea(9))
         sort_words("scalar", tea(10), tea(11))
         fetch(r8)
-        part("gpsimd", ("c", 1, 0), 256, 512, True)
+        part("gpsimd", ("c", 1, 0), 352, 512, True)
         add1(0)
         add1(1)
         passes1(6, 7)
         nc.scalar.copy(out=gain_f32[:], in_=gain_in[:])
-        part("scalar", ("c", 1, 0), 0, 256)
+        part("scalar", ("c", 1, 0), 0, 352)
         r10 = turn(tea(10), tea(11))
         spread_gain(0)
         fetch(r10)
@@ -435,7 +435,7 @@ def tile_teacher_student_logits_t1_kernel(
         passes1(10, 11)
         interleave("scalar", ("c", 1, 2))
         quantise_all(("c", 1, 0), ("z1", 0, 0))
-        part("gpsimd", ("c", 1, 1), 96, 512, True)
+        part("gpsimd", ("c", 1, 1), 256, 512, True)
         a0 = fetch(turn(*aff(0)))
         add1(2)
         mm1(4, (0,))
@@ -445,7 +445,7 @@ def tile_teacher_student_logits_t1_kernel(
         part("scalar", ("z1", 0, 1), 0, 192)
         quantise(("c", 1, 2))
         mm1(4, (2,))
-        part("vector", ("c", 1, 1), 0, 96)
+        part("vector", ("c", 1, 1), 0, 256)
         part("vector", ("z1", 0, 1), 192, 512)
         fetch(a1)
         quantise(("c", 1, 1))
@@ -455,11 +455,11 @@ def tile_teacher_student_logits_t1_kernel(
         mm2(0, by_pass=True)
 
         early = {1: [("c", 2, 1)], 2: [("z1", 1, 0)], 4: [("w", 1)], 5: [("z1", 2, 0)], 6: [("w", 2)]}
-        helped = {0: ("w", 0), 2: ("c", 2, 2), 3: ("z1", 1, 1), 7: ("z1", 2, 1)}
-        quantised = {0: [a2], 1: [("w", 0), ("c", 2, 0)], 2: [("c", 2, 1), ("c", 2, 2)], 3: [("z1", 1, 1), ("z1", 1, 0)], 5: [("w", 1)], 6: [("z1", 2, 0)], 7: [("z1", 2, 1), ("w", 2)]}
+        helped = {0: ("w", 0), 2: ("c", 2, 2)}
+        quantised = {0: [a2], 1: [("w", 0), ("c", 2, 0)], 2: [("c", 2, 1), ("c", 2, 2)], 3: [("z1", 1, 0), ("z1", 1, 1)], 5: [("w", 1)], 6: [("z1", 2, 0)], 7: [("w", 2), ("z1", 2, 1)]}
         for s in range(12):
             border = s in (3, 7)
-            split = 128 if s == 0 else 512 - GPSIMD_COLS
+            split = 256 if s == 0 else 512 - GPSIMD_COLS
             if s > 0:
                 gain_mul(s - 1)
             if s >= 2:
@@ -470,9 +470,8 @@ def tile_teacher_student_logits_t1_kernel(
                 part("gpsimd", helped[s], split, 512, True)
                 part("scalar", helped[s], 0, split)
             if border:
-                fetch2(s - 1)
+                interleave("scalar", ("z1", s // 4 + 1, 1))
             if s == 0:
-                sort_block("scalar", ("a", 1, 1))
                 interleave("scalar", ("c", 2, 0))
             if s < 8 and not border:
                 add1(s + 4)
@@ -493,8 +492,7 @@ def tile_teacher_student_logits_t1_kernel(
                 a3 = turn(*aff(3))
             if s == 4:
                 spread_gain(2)
-            if s not in (2, 6):
-                fetch2(s)
+            fetch2(s)
             if s == 0:
                 fetch(a3)
             if s == 4:
@@ -505,7 +503,7 @@ def tile_teacher_student_logits_t1_kernel(
             if s > 0:
                 quantise(("z2", s - 1))
             if s == 3:
-                mm2(s + 1, (1, 0), by_pass=True)
+                mm2(s + 1, by_pass=True)
             if s == 7:
                 mm2(s + 1, (1,))
         gain_mul_tile(11, 1, nc.vector, 13)

@@ -73,7 +73,7 @@ def tile_teacher_student_logits_t1_kernel(
         affinity_v = affinity.rearrange("(g p t) k -> g p t k", p=P, t=4)
         student_v = student.rearrange("(g p t) c -> g p t c", p=P, t=4)
         confusion_v = confusion.rearrange("(c p j) n -> c p j n", p=P, j=4)
-        within_v = within.rearrange("(h b t r) n -> h r b t n", b=32, t=4, r=4)
+        within_v = within.rearrange("(h p j) n -> h p j n", p=P, j=4)
         out_v = out.rearrange("(g p t) c -> g p t c", p=P, t=4)
 
         loaded = {}
@@ -125,8 +125,7 @@ def tile_teacher_student_logits_t1_kernel(
                     words["a", g, q, c] = t[:].bitcast(F32)[:, :, 256 * c : 256 * (c + 1)]
             if key[0] == "w":
                 t = raw_tile(key, [P, 4, 512])
-                for r in range(4):
-                    nc.sync.dma_start(out=t[r:P:4], in_=within_v[key[1], r])
+                nc.sync.dma_start(out=t[:], in_=within_v[key[1]])
 
         def load_all(*keys):
             for key in keys:
@@ -145,8 +144,8 @@ def tile_teacher_student_logits_t1_kernel(
 
         def fetch_gain(h):
             nc.scalar.copy(
-                out=gain_sb[:, h, :].rearrange("p (u b r) -> p u b r", u=4, r=4),
-                in_=banks["gain", h][:].rearrange("p r (b u) -> p u b r", u=4),
+                out=gain_sb[:, h, :].rearrange("p (u m e) -> p u m e", u=2, e=2),
+                in_=banks["gain", h][:].rearrange("p (u e) m -> p u m e", u=2),
             )
             give_back(("gain", h))
 
@@ -268,7 +267,7 @@ def tile_teacher_student_logits_t1_kernel(
         def pair(s):
             return s // 4, s // 2 % 2, s % 2
 
-        def mm1(s, passes=(0, 1, 2), by_pass=False):
+        def mm1(s, passes=(0, 1, 2), by_pass=False, newest=False):
             h, g, q = pair(s)
             order = [(a, c) for a in range(2) for c in passes]
             if by_pass:
@@ -277,7 +276,7 @@ def tile_teacher_student_logits_t1_kernel(
                 n = counts.get(("z1", s, a), 0)
                 counts["z1", s, a] = n + 1
                 if n == 0:
-                    take_bank(("z1", s, a), [P, 512])
+                    take_bank(("z1", s, a), [P, 512], newest)
                 product(banks["z1", s, a], ("t", g, q, c), slice(a * P, (a + 1) * P), ("c", h, c), n == 0, n == 2)
 
         def add1(s, tiles=(1, 0)):
@@ -287,9 +286,9 @@ def tile_teacher_student_logits_t1_kernel(
             for a in tiles:
                 t = 2 * q + a
                 nc.vector.tensor_tensor(
-                    out=z1[h, g][:, t, :].rearrange("p (u b r) -> p b u r", u=4, r=4),
-                    in0=banks["z1", s, a][:].rearrange("p (b u r) -> p b u r", u=4, r=4),
-                    in1=loaded["s", h, g][:, t, :].rearrange("p (b u r) -> p b u r", u=4, r=4),
+                    out=z1[h, g][:, t, :].rearrange("p (u m e) -> p m u e", u=2, e=2),
+                    in0=banks["z1", s, a][:].rearrange("p (m u e) -> p m u e", u=2, e=2),
+                    in1=loaded["s", h, g][:, t, :].rearrange("p (m u e) -> p m u e", u=2, e=2),
                     op=ADD,
                 )
                 give_back(("z1", s, a))
@@ -321,8 +320,9 @@ def tile_teacher_student_logits_t1_kernel(
                 )
                 give_back(("z2", s, a))
 
-        def gain_mul(s):
-            pair_tile = late_slot(s, [P, 2, 512], F32)
+        def gain_mul(s, held=True):
+            shape = [P, 2, 512]
+            pair_tile = late_slot(s, shape, F32) if held else ring(sbuf, "gained", 2, shape, F32)
             for a in range(2):
                 gained[s, a] = pair_tile[:, a, :]
             nc.gpsimd.tensor_tensor(
@@ -336,21 +336,42 @@ def tile_teacher_student_logits_t1_kernel(
             gained[s, a] = late_slot(slot, [P, 512], F32)[:]
             engine.tensor_tensor(out=gained[s, a], in0=z2[s][:, a, :], in1=gain_sb[:, s // 4, :], op=MULT)
 
+        def round2(engine, s, by_tile=False):
+            shape = [P, 2, 512]
+            if engine == "gpsimd":
+                rounded = late_slot(s, shape, BF16)
+                nc.gpsimd.tensor_scalar(out=rounded[:], in0=z2[s][:], scalar1=1.0, scalar2=0.0, op0=MULT, op1=ADD)
+            else:
+                rounded = ring(sbuf, "rounded", 2, shape, BF16)
+                for tiles in (slice(1, 2), slice(0, 1)) if by_tile else (slice(0, 2),):
+                    copy_on(engine, rounded[:, tiles], z2[s][:, tiles])
+            sorted_words["z2", s] = rounded[:].bitcast(F32).rearrange("p a (u m) -> p a u m", u=2)
+
         def turn2(s):
+            if s > 0:
+                free_banks.append(bank_of["z2t", s - 1])
+            bank = take_bank(("z2t", s), [P, 2, 2, P], s > 0)
             for a in range(2):
-                take_bank(("z2t", s, a), [P, 4, P])
-                for u in range(4):
-                    nc.tensor.transpose(banks["z2t", s, a][:, u, :], z2[s][:, a, u * P : (u + 1) * P], ident[:])
+                for u in range(2):
+                    nc.tensor.transpose(bank[:, a, u, :], sorted_words["z2", s][:, a, u], ident[:])
 
         def fetch2(s):
-            run = ("z2", s)
-            grouped[run] = late_slot(s + 1, [P, 2 * P, 4], BF16)
-            for a in range(2):
+            grouped["z2", s] = late_slot(s + 1, [P, 2 * P, 4], BF16)
+            nc.scalar.copy(
+                out=grouped["z2", s][:].bitcast(F32).rearrange("p (a r) u -> p a r u", a=2),
+                in_=banks["z2t", s][:].rearrange("p a u r -> p a r u"),
+            )
+
+        def turn2_unrounded(s):
+            grouped["z2", s] = late_slot(s + 1, [P, 2 * P, 4], BF16)
+            for a in (1, 0):
+                bank = take_bank(("z2t", s, a), [P, 4, P])
+                for t in range(4):
+                    start = t // 2 * 256 + t % 2
+                    nc.tensor.transpose(bank[:, t, :], z2[s][:, a, start : t // 2 * 256 + 256 : 2], ident[:])
                 nc.scalar.copy(
-                    out=grouped[run][:, a * P : (a + 1) * P, :],
-                    in_=banks["z2t", s, a][:].rearrange("p u n -> p n u"),
+                    out=grouped["z2", s][:, a * P : (a + 1) * P, :], in_=bank[:].rearrange("p t n -> p n t")
                 )
-                give_back(("z2t", s, a))
 
         def mm3(s):
             for a in range(2):
@@ -362,9 +383,9 @@ def tile_teacher_student_logits_t1_kernel(
                 result[s] = ring(sbuf, "result", 3, [P, 2, 512], F32)
             for a in tiles:
                 nc.vector.tensor_tensor(
-                    out=result[s][:, a, :].rearrange("p (b u r) -> p b u r", u=4, r=4),
-                    in0=banks["out", s, a][:].rearrange("p (b u r) -> p b u r", u=4, r=4),
-                    in1=gained[s, a].rearrange("p (u b r) -> p b u r", u=4, r=4),
+                    out=result[s][:, a, :].rearrange("p (m u e) -> p m u e", u=2, e=2),
+                    in0=banks["out", s, a][:].rearrange("p (m u e) -> p m u e", u=2, e=2),
+                    in1=gained[s, a].rearrange("p (u m e) -> p m u e", u=2, e=2),
                     op=ADD,
                 )
                 give_back(("out", s, a))
@@ -420,25 +441,23 @@ def tile_teacher_student_logits_t1_kernel(
         add1(1)
         passes1(6, 7)
         nc.scalar.copy(out=gain_f32[:], in_=gain_in[:])
-        part("scalar", ("c", 1, 0), 0, 352)
         r10 = turn(tea(10), tea(11))
         spread_gain(0)
         fetch(r10)
-        load_all(("c", 2, 0), ("c", 2, 1), ("s", 1, 1), ("c", 2, 2), ("w", 1))
+        part("scalar", ("c", 1, 0), 0, 352)
+        load_all(("c", 2, 0), ("s", 1, 1), ("c", 2, 1), ("c", 2, 2), ("w", 1))
         fetch_gain(0)
         quantise(r8)
         passes1(8, 9)
-        spread_gain(1)
-        fetch_gain(1)
         interleave("vector", ("z1", 0, 0))
         quantise(r10)
         passes1(10, 11)
         interleave("scalar", ("c", 1, 2))
-        quantise_all(("c", 1, 0), ("z1", 0, 0))
+        quantise_all(("z1", 0, 0), ("c", 1, 0))
         part("gpsimd", ("c", 1, 1), 256, 512, True)
-        a0 = fetch(turn(*aff(0)))
         add1(2)
-        mm1(4, (0,))
+        mm1(4, (0,), newest=True)
+        a0 = fetch(turn(*aff(0)))
         add1(3)
         load_all(("s", 2, 0), ("s", 2, 1), ("w", 2))
         a1 = turn(*aff(1))
@@ -454,65 +473,97 @@ def tile_teacher_student_logits_t1_kernel(
         quantise_all(a0, ("z1", 0, 1), a1)
         mm2(0, by_pass=True)
 
-        early = {1: [("c", 2, 1)], 2: [("z1", 1, 0)], 4: [("w", 1)], 5: [("z1", 2, 0)], 6: [("w", 2)]}
-        helped = {0: ("w", 0), 2: ("c", 2, 2)}
-        quantised = {0: [a2], 1: [("w", 0), ("c", 2, 0)], 2: [("c", 2, 1), ("c", 2, 2)], 3: [("z1", 1, 0), ("z1", 1, 1)], 5: [("w", 1)], 6: [("z1", 2, 0)], 7: [("w", 2), ("z1", 2, 1)]}
+        first_pairs = {0: [4], 1: [5], 2: [6], 3: [7], 5: [8], 6: [9, 10], 7: [11]}
+        early = {1: [("c", 2, 0)], 2: [("z1", 1, 0)], 3: [("z1", 1, 1)], 6: [("z1", 2, 0)], 7: [("z1", 2, 1)]}
+        after = {2: [("c", 2, 1)], 3: [("c", 2, 2)], 4: [("w", 1)], 5: [("w", 2)]}
+        quantised = {0: [a2], 1: [("w", 0)], 2: [("c", 2, 0), ("z1", 1, 0)], 3: [("z1", 1, 1), ("c", 2, 1)], 4: [("c", 2, 2)], 5: [("w", 1)], 6: [("z1", 2, 0)], 7: [("z1", 2, 1), ("w", 2)]}
+        BY_GPSIMD = (1, 2, 4, 5, 6)
         for s in range(12):
             border = s in (3, 7)
-            split = 256 if s == 0 else 512 - GPSIMD_COLS
+            ahead = first_pairs.get(s + 1, [])
+            if s - 1 in BY_GPSIMD:
+                round2("gpsimd", s - 1)
             if s > 0:
-                gain_mul(s - 1)
-            if s >= 2:
+                gain_mul(s - 1, s - 1 not in BY_GPSIMD)
+            if s >= 2 and s != 6:
                 mm3(s - 2)
-            if border:
-                add1(s + 4)
-            if s in helped:
-                part("gpsimd", helped[s], split, 512, True)
-                part("scalar", helped[s], 0, split)
-            if border:
-                interleave("scalar", ("z1", s // 4 + 1, 1))
             if s == 0:
-                interleave("scalar", ("c", 2, 0))
-            if s < 8 and not border:
-                add1(s + 4)
+                part("gpsimd", ("w", 0), 256, 512, True)
+                part("scalar", ("w", 0), 0, 256)
+                sort_block("scalar", ("a", 1, 1))
+            if s - 1 not in BY_GPSIMD and s > 0:
+                turn2(s - 1)
+                if s == 4:
+                    spread_gain(1)
+                fetch2(s - 1)
+            if s == 5:
+                add2(s)
+            for k in first_pairs.get(s, []):
+                add1(k)
+                if k == 9:
+                    mm3(4)
             for key in early.get(s, []):
                 interleave("scalar", key)
-            add2(s)
-            if s < 7:
-                mm1(s + 5)
-            if s == 7:
+            if s == 2:
+                a3 = turn(*aff(3))
+            if s in (2, 6):
+                turn2(s - 1)
+            if border:
+                turn2(s - 1)
+                fetch2(s - 1)
+            if s != 5:
+                add2(s)
+            if ahead and s != 4:
+                mm1(ahead[0])
+            if s == 2:
+                fetch(a3)
+            if s - 1 in BY_GPSIMD and not border:
+                if s == 5:
+                    turn2(s - 1)
+                if s == 5:
+                    spread_gain(2)
+                fetch2(s - 1)
+                if s == 5:
+                    fetch_gain(2)
+            for k in ahead[1:]:
+                mm1(k)
+            if border:
                 mm2(s + 1, (0,), newest=True)
-            if s < 11 and not border:
+            if s == 3:
+                mm1(8, (0,))
+            if s not in (2, 5, 11) and not border:
                 mm2(s + 1)
             if s >= 2:
                 add3(s - 2)
                 store(s - 2)
-            turn2(s)
-            if s == 0:
-                a3 = turn(*aff(3))
+            if s == 5:
+                mm2(s + 1)
             if s == 4:
-                spread_gain(2)
-            fetch2(s)
-            if s == 0:
-                fetch(a3)
-            if s == 4:
-                fetch_gain(2)
+                fetch_gain(1)
+            if s not in BY_GPSIMD and s < 11:
+                round2("scalar", s)
+            for key in after.get(s, []):
+                interleave("scalar", key)
             quantise_all(*quantised.get(s, []))
-            if s == 1:
+            if s == 2:
                 quantise(a3)
+                mm2(3)
             if s > 0:
                 quantise(("z2", s - 1))
-            if s == 3:
-                mm2(s + 1, by_pass=True)
-            if s == 7:
+            if s == 4:
+                mm1(8, (2,))
+            if border:
                 mm2(s + 1, (1,))
+            if s == 3:
+                mm1(8, (1,))
+        turn2_unrounded(11)
+        mm3(10)
         gain_mul_tile(11, 1, nc.vector, 13)
         quantise(("z2", 11))
         gain_mul_tile(11, 0, nc.gpsimd, 12)
-        mm3(10)
+        mm3(11)
         add3(10)
         store(10)
-        mm3(11)
         for a in (1, 0):
             add3(11, (a,))
             store(11, slice(a, a + 1))

@@ -19,7 +19,7 @@ BLOCK = 4 * 512 * 2
 WHOLE = slice(0, 512)
 HALVES = (slice(0, 256), slice(256, 512))
 BANKS = 8
-LATE_SLOTS = 4
+LATE_PLACE = (16, 17, 18, 19, 12, 13)
 GROUPED = 4
 TURNED = 3
 GPSIMD_COLS = 112
@@ -54,8 +54,8 @@ def tile_teacher_student_logits_t1_kernel(
             return pool.tile(shape, dtype, name=tag, tag=tag, align_bytes=64)
 
         def late_slot(n, shape, dtype):
-            tag = "late" + str(n % LATE_SLOTS)
-            return sbuf.tile(shape, dtype, name=tag, tag=tag, align_bytes=64)
+            tag = "late" + str(n)+ "_" + str(len(shape)) + "_" + str(shape[1])
+            return raw.tile(shape, dtype, name=tag, tag=tag, align_bytes=64, offset=LATE_PLACE[n % len(LATE_PLACE)] * BLOCK)
 
         free_banks = list(range(BANKS))
         bank_of = {}
@@ -180,7 +180,7 @@ def tile_teacher_student_logits_t1_kernel(
                     src[:, :, cols].rearrange("p t (n i) -> p n t i", i=4),
                 )
 
-        depth = {"c": 6, "w": 2, "z1": 4, "t": 12, "a": 4, "z2": 2}
+        depth = {"c": 6, "w": 2, "z1": 4, "t": 12, "a": 4, "z2": 5}
 
         def quantise(key, cols=None):
             width = grouped[key].shape[1]
@@ -207,13 +207,13 @@ def tile_teacher_student_logits_t1_kernel(
                 quantise(key)
 
         def sort_words(engine, *keys):
-            ordered = ring(sbuf, "result", 3, [P, len(keys), 2, 2, P], F32)
+            ordered = ring(sbuf, "result", 4, [P, len(keys), 2, 2, P], F32)
             for n, key in enumerate(keys):
                 copy_on(engine, ordered[:, n], words[key].rearrange("p a (m u) -> p a u m", u=2))
                 sorted_words[key] = ordered[:, n]
 
         def sort_block(engine, key):
-            ordered = ring(sbuf, "result", 3, [P, 4, 2, P], F32)
+            ordered = ring(sbuf, "result", 4, [P, 4, 2, P], F32)
             flat = loaded[key][:].rearrange("p a n -> p (a n)").bitcast(F32)
             copy_on(engine, ordered[:], flat.rearrange("p (j m u) -> p j u m", j=4, u=2))
             for n in range(2):
@@ -322,7 +322,7 @@ def tile_teacher_student_logits_t1_kernel(
 
         def gain_mul(s, held=True):
             shape = [P, 2, 512]
-            pair_tile = late_slot(s, shape, F32) if held else ring(sbuf, "gained", 2, shape, F32)
+            pair_tile = late_slot(s, shape, F32) if held else raw.tile(shape, F32, name="gained" + str(s), tag="gained" + str(s), align_bytes=64, offset=(14 + s % 2) * BLOCK)
             for a in range(2):
                 gained[s, a] = pair_tile[:, a, :]
             nc.gpsimd.tensor_tensor(
@@ -348,9 +348,10 @@ def tile_teacher_student_logits_t1_kernel(
             sorted_words["z2", s] = rounded[:].bitcast(F32).rearrange("p a (u m) -> p a u m", u=2)
 
         def turn2(s):
-            if s > 0:
-                free_banks.append(bank_of["z2t", s - 1])
-            bank = take_bank(("z2t", s), [P, 2, 2, P], s > 0)
+            if "z2t" in bank_of:
+                free_banks.append(bank_of["z2t"])
+            bank = take_bank(("z2t", s), [P, 2, 2, P], "z2t" in bank_of)
+            bank_of["z2t"] = bank_of["z2t", s]
             for a in range(2):
                 for u in range(2):
                     nc.tensor.transpose(bank[:, a, u, :], sorted_words["z2", s][:, a, u], ident[:])
@@ -372,23 +373,28 @@ def tile_teacher_student_logits_t1_kernel(
                 nc.scalar.copy(
                     out=grouped["z2", s][:, a * P : (a + 1) * P, :], in_=bank[:].rearrange("p t n -> p n t")
                 )
+                give_back(("z2t", s, a))
 
-        def mm3(s):
-            for a in range(2):
-                take_bank(("out", s, a), [P, 512])
-                product(banks["out", s, a], ("z2", s), slice(a * P, (a + 1) * P), ("w", s // 4), True, True)
+        def mm3(*tiles):
+            for i in tiles:
+                take_bank(("out", i), [P, 512])
+                product(banks["out", i], ("z2", i // 2), slice(i % 2 * P, (i % 2 + 1) * P), ("w", i // 8), True, True)
 
-        def add3(s, tiles=(1, 0)):
-            if s not in result:
-                result[s] = ring(sbuf, "result", 3, [P, 2, 512], F32)
-            for a in tiles:
+        def add3(*tiles):
+            for i in tiles:
+                if i // 2 not in result:
+                    result[i // 2] = ring(sbuf, "result", 4, [P, 2, 512], F32)
+            for i in reversed(tiles):
                 nc.vector.tensor_tensor(
-                    out=result[s][:, a, :].rearrange("p (m u e) -> p m u e", u=2, e=2),
-                    in0=banks["out", s, a][:].rearrange("p (m u e) -> p m u e", u=2, e=2),
-                    in1=gained[s, a].rearrange("p (u m e) -> p m u e", u=2, e=2),
+                    out=result[i // 2][:, i % 2, :].rearrange("p (m u e) -> p m u e", u=2, e=2),
+                    in0=banks["out", i][:].rearrange("p (m u e) -> p m u e", u=2, e=2),
+                    in1=gained[i // 2, i % 2].rearrange("p (u m e) -> p m u e", u=2, e=2),
                     op=ADD,
                 )
-                give_back(("out", s, a))
+                give_back(("out", i))
+            for i in tiles:
+                if i % 2 == 1 and i < 20:
+                    store(i // 2)
 
         def store(s, tiles=slice(0, 2)):
             h, g, q = pair(s)
@@ -429,8 +435,10 @@ def tile_teacher_student_logits_t1_kernel(
         interleave("vector", ("c", 0, 2))
         load_all(("a", 1, 0), ("s", 1, 0), ("w", 0), ("a", 1, 1))
         sort_words("scalar", tea(8))
+        quantise(("c", 0, 2))
+        sort_words("vector", tea(6), tea(7))
         r6 = fetch(turn(tea(6), tea(7)))
-        quantise_all(r2, ("c", 0, 2))
+        quantise(r2)
         passes1(2, 5)
         quantise(r6)
         r8 = turn(tea(8), tea(9))
@@ -460,24 +468,24 @@ def tile_teacher_student_logits_t1_kernel(
         a0 = fetch(turn(*aff(0)))
         add1(3)
         load_all(("s", 2, 0), ("s", 2, 1), ("w", 2))
-        a1 = turn(*aff(1))
         part("scalar", ("z1", 0, 1), 0, 192)
         quantise(("c", 1, 2))
         mm1(4, (2,))
+        a1 = turn(*aff(1))
         part("vector", ("c", 1, 1), 0, 256)
         part("vector", ("z1", 0, 1), 192, 512)
-        fetch(a1)
+        fetch(a1, late=True)
         quantise(("c", 1, 1))
-        a2 = fetch(turn(*aff(2)), late=True)
         mm1(4, (1,))
-        quantise_all(a0, ("z1", 0, 1), a1)
+        quantise_all(a0, ("z1", 0, 1))
         mm2(0, by_pass=True)
 
         first_pairs = {0: [4], 1: [5], 2: [6], 3: [7], 5: [8], 6: [9, 10], 7: [11]}
+        last_tiles = {s: (2 * s - 4, 2 * s - 3) for s in range(2, 12)}
         early = {1: [("c", 2, 0)], 2: [("z1", 1, 0)], 3: [("z1", 1, 1)], 6: [("z1", 2, 0)], 7: [("z1", 2, 1)]}
         after = {2: [("c", 2, 1)], 3: [("c", 2, 2)], 4: [("w", 1)], 5: [("w", 2)]}
-        quantised = {0: [a2], 1: [("w", 0)], 2: [("c", 2, 0), ("z1", 1, 0)], 3: [("z1", 1, 1), ("c", 2, 1)], 4: [("c", 2, 2)], 5: [("w", 1)], 6: [("z1", 2, 0)], 7: [("z1", 2, 1), ("w", 2)]}
-        BY_GPSIMD = (1, 2, 4, 5, 6)
+        quantised = {1: [("w", 0)], 2: [("c", 2, 0), ("z1", 1, 0)], 3: [("z1", 1, 1), ("c", 2, 1)], 4: [("c", 2, 2)], 5: [("w", 1)], 6: [("z1", 2, 0)], 7: [("z1", 2, 1), ("w", 2)]}
+        BY_GPSIMD = (1, 2, 5, 6)
         for s in range(12):
             border = s in (3, 7)
             ahead = first_pairs.get(s + 1, [])
@@ -486,13 +494,15 @@ def tile_teacher_student_logits_t1_kernel(
             if s > 0:
                 gain_mul(s - 1, s - 1 not in BY_GPSIMD)
             if s >= 2 and s != 6:
-                mm3(s - 2)
+                mm3(*last_tiles[s])
             if s == 0:
                 part("gpsimd", ("w", 0), 256, 512, True)
                 part("scalar", ("w", 0), 0, 256)
-                sort_block("scalar", ("a", 1, 1))
+                sort_block("scalar", ("a", 1, 0))
             if s - 1 not in BY_GPSIMD and s > 0:
                 turn2(s - 1)
+                if s == 1:
+                    a2 = fetch(turn(*aff(2)))
                 if s == 4:
                     spread_gain(1)
                 fetch2(s - 1)
@@ -501,14 +511,14 @@ def tile_teacher_student_logits_t1_kernel(
             for k in first_pairs.get(s, []):
                 add1(k)
                 if k == 9:
-                    mm3(4)
+                    mm3(*last_tiles[6])
             for key in early.get(s, []):
                 interleave("scalar", key)
             if s == 2:
                 a3 = turn(*aff(3))
-            if s in (2, 6):
+            if s in (2, 6) and s - 1 in BY_GPSIMD:
                 turn2(s - 1)
-            if border:
+            if border and s - 1 in BY_GPSIMD:
                 turn2(s - 1)
                 fetch2(s - 1)
             if s != 5:
@@ -520,31 +530,37 @@ def tile_teacher_student_logits_t1_kernel(
             if s - 1 in BY_GPSIMD and not border:
                 if s == 5:
                     turn2(s - 1)
-                if s == 5:
-                    spread_gain(2)
                 fetch2(s - 1)
-                if s == 5:
-                    fetch_gain(2)
             for k in ahead[1:]:
                 mm1(k)
             if border:
                 mm2(s + 1, (0,), newest=True)
             if s == 3:
                 mm1(8, (0,))
-            if s not in (2, 5, 11) and not border:
+            if s not in (0, 1, 2, 5, 11) and not border:
                 mm2(s + 1)
             if s >= 2:
-                add3(s - 2)
-                store(s - 2)
+                add3(*last_tiles[s])
             if s == 5:
                 mm2(s + 1)
             if s == 4:
                 fetch_gain(1)
+            if s == 7:
+                spread_gain(2)
+                fetch_gain(2)
             if s not in BY_GPSIMD and s < 11:
                 round2("scalar", s)
+            if s == 0:
+                sort_block("scalar", ("a", 1, 1))
             for key in after.get(s, []):
                 interleave("scalar", key)
+            if s == 0:
+                quantise(a1)
+                mm2(1)
             quantise_all(*quantised.get(s, []))
+            if s == 1:
+                quantise(a2)
+                mm2(2)
             if s == 2:
                 quantise(a3)
                 mm2(3)
@@ -557,13 +573,11 @@ def tile_teacher_student_logits_t1_kernel(
             if s == 3:
                 mm1(8, (1,))
         turn2_unrounded(11)
-        mm3(10)
+        mm3(20, 21)
         gain_mul_tile(11, 1, nc.vector, 13)
         quantise(("z2", 11))
         gain_mul_tile(11, 0, nc.gpsimd, 12)
-        mm3(11)
-        add3(10)
-        store(10)
-        for a in (1, 0):
-            add3(11, (a,))
-            store(11, slice(a, a + 1))
+        mm3(22, 23)
+        for i in (21, 20, 23, 22):
+            add3(i)
+            store(i // 2, slice(i % 2, i % 2 + 1))

@@ -15,21 +15,17 @@ FP8X4 = mybir.dt.float8_e4m3fn_x4
 MULT = mybir.AluOpType.mult
 ADD = mybir.AluOpType.add
 
-BLOCK = 4 * 512 * 2
-WHOLE = slice(0, 512)
-HALVES = (slice(0, 256), slice(256, 512))
-BANKS = 8
-LATE_PLACE = (16, 17, 18, 19, 12, 13)
+KIB = 1024
 GROUPED = 4
-TURNED = 3
-GPSIMD_COLS = 112
+TURNED = 4
+HELD = 3
 PLACE = {
-    ("tpass", 0, 0): 0, ("tpass", 0, 1): 1, ("tpass", 0, 2): 2, ("t", 1, 0): 3, ("t", 1, 1): 4.5,
-    ("c", 0, 0): 6, ("c", 0, 1): 7, ("c", 0, 2): 8, ("s", 0, 0): 9, ("s", 0, 1): 10,
-    ("c", 1, 0): 11, ("c", 1, 1): 12, ("c", 1, 2): 13, ("a", 0, 0): 14, ("a", 0, 1): 15,
-    ("a", 1, 0): 0, ("a", 1, 1): 1, ("w", 1): 2, ("c", 2, 0): 3, ("c", 2, 1): 4, ("c", 2, 2): 5,
-    ("s", 1, 0): 6, ("s", 1, 1): 7, ("w", 0): 8, ("s", 2, 0): 9, ("s", 2, 1): 10, ("w", 2): 11,
+    ("c", 0, 0): 0, ("t", 0, 0): 4, ("c", 0, 1): 10, ("c", 0, 2): 14, ("t", 0, 1): 18, ("s", 0, 0): 24, ("cc", 0): 28,
+    ("t", 1, 0): 36, ("t", 1, 1): 42, ("s", 0, 1): 0, ("a", 0, 0): 4, ("c", 1, 1): 10, ("c", 1, 2): 14,
+    ("s", 1, 0): 18, ("a", 0, 1): 24, ("w", 0): 28, ("a", 1, 0): 36, ("s", 1, 1): 42, ("a", 1, 1): 4,
+    ("c", 2, 1): 32, ("c", 2, 2): 10, ("s", 2, 0): 0, ("w", 1): 14, ("s", 2, 1): 24, ("w", 2): 36,
 }
+HELD_PLACE = 48
 
 
 def tile_teacher_student_logits_t1_kernel(
@@ -45,29 +41,20 @@ def tile_teacher_student_logits_t1_kernel(
         counts = {}
         banks = {}
 
-        def ring(pool, name, depth, shape, dtype):
+        def ring(name, depth, shape, dtype):
             n = counts.get(name, 0)
             counts[name] = n + 1
             tag = name + str(n % depth)
-            if pool is psum:
-                return pool.tile(shape, dtype, name=tag, tag=tag)
-            return pool.tile(shape, dtype, name=tag, tag=tag, align_bytes=64)
+            return sbuf.tile(shape, dtype, name=tag, tag=tag, align_bytes=64)
 
-        def late_slot(n, shape, dtype):
-            tag = "late" + str(n)+ "_" + str(len(shape)) + "_" + str(shape[1])
-            return raw.tile(shape, dtype, name=tag, tag=tag, align_bytes=64, offset=LATE_PLACE[n % len(LATE_PLACE)] * BLOCK)
+        def held_slot(n, name, shape, dtype):
+            tag = name + str(n)
+            return raw.tile(shape, dtype, name=tag, tag=tag, align_bytes=64, offset=(HELD_PLACE + 4 * (n % HELD)) * KIB)
 
-        free_banks = list(range(BANKS))
-        bank_of = {}
-
-        def take_bank(key, shape, newest=False):
-            bank_of[key] = free_banks.pop(-1 if newest else 0)
-            tag = "bank" + str(bank_of[key])
+        def take_bank(key, shape, n):
+            tag = "bank" + str(n)
             banks[key] = psum.tile(shape, F32, name=tag, tag=tag)
             return banks[key]
-
-        def give_back(key):
-            free_banks.append(bank_of[key])
 
         teacher_v = teacher.rearrange("(g p t) k -> g p t k", p=P, t=4)
         affinity_v = affinity.rearrange("(g p t) k -> g p t k", p=P, t=4)
@@ -90,46 +77,31 @@ def tile_teacher_student_logits_t1_kernel(
 
         def raw_tile(key, shape):
             name = "raw_" + "_".join(str(x) for x in key)
-            loaded[key] = raw.tile(shape, BF16, name=name, tag=name, align_bytes=64, offset=int(PLACE[key] * BLOCK))
-            return loaded[key]
+            return raw.tile(shape, BF16, name=name, tag=name, align_bytes=64, offset=PLACE[key] * KIB)
 
-        def load(key):
-            if key[0] == "c":
-                t = raw_tile(key, [P, 4, 512])
-                nc.sync.dma_start(out=t[:], in_=confusion_v[key[2], :, :, key[1] * 512 : (key[1] + 1) * 512])
-            if key[0] == "s":
-                t = raw_tile(key, [P, 4, 512])
-                nc.sync.dma_start(out=t[:], in_=student_v[key[2], :, :, key[1] * 512 : (key[1] + 1) * 512])
-            if key[0] == "t":
-                g, q = key[1:]
-                t = raw_tile(key, [P, 2, C])
-                nc.sync.dma_start(out=t[:], in_=teacher_v[g, :, 2 * q : 2 * q + 2, :])
-                for c in range(3):
-                    words["t", g, q, c] = t[:].bitcast(F32)[:, :, 256 * c : 256 * (c + 1)]
-            if key[0] == "tunit":
-                g, q, c = key[1:]
-                t = raw_tile(key, [P, 2, 512])
-                nc.sync.dma_start(out=t[:], in_=teacher_v[g, :, 2 * q : 2 * q + 2, 512 * c : 512 * (c + 1)])
-                words["t", g, q, c] = t[:].bitcast(F32)
-            if key[0] == "tpass":
-                g, c = key[1:]
-                t = raw_tile(key, [P, 4, 512])
-                nc.sync.dma_start(out=t[:], in_=teacher_v[g, :, :, 512 * c : 512 * (c + 1)])
-                for q in range(2):
-                    words["t", g, q, c] = t[:].bitcast(F32)[:, 2 * q : 2 * q + 2, :]
-            if key[0] == "a":
-                g, q = key[1:]
-                t = raw_tile(key, [P, 2, B])
-                nc.sync.dma_start(out=t[:], in_=affinity_v[g, :, 2 * q : 2 * q + 2, :])
-                for c in range(2):
-                    words["a", g, q, c] = t[:].bitcast(F32)[:, :, 256 * c : 256 * (c + 1)]
-            if key[0] == "w":
-                t = raw_tile(key, [P, 4, 512])
-                nc.sync.dma_start(out=t[:], in_=within_v[key[1]])
-
-        def load_all(*keys):
+        def load(*keys):
             for key in keys:
-                load(key)
+                if key[0] in ("c", "s"):
+                    source = confusion_v if key[0] == "c" else student_v
+                    loaded[key] = raw_tile(key, [P, 4, 512])[:]
+                    nc.sync.dma_start(out=loaded[key], in_=source[key[2], :, :, key[1] * 512 : (key[1] + 1) * 512])
+                if key[0] == "cc":
+                    t = raw_tile(key, [P, 4, 1024])
+                    nc.sync.dma_start(out=t[:], in_=confusion_v[key[1], :, :, 512:])
+                    for h in (1, 2):
+                        loaded["c", h, key[1]] = t[:, :, (h - 1) * 512 : h * 512]
+                if key[0] in ("t", "a"):
+                    g, q = key[1:]
+                    source = teacher_v if key[0] == "t" else affinity_v
+                    width = source.shape[-1]
+                    t = raw_tile(key, [P, 2 * width])
+                    nc.sync.dma_start(out=t[:], in_=source[g, :, 2 * q : 2 * q + 2, :].rearrange("p a k -> p (a k)"))
+                    loaded[key] = t[:].bitcast(F32).rearrange("p (a k) -> p a k", a=2)
+                    for c in range(width // 512):
+                        words[key + (c,)] = loaded[key][:, :, 256 * c : 256 * (c + 1)]
+                if key[0] == "w":
+                    loaded[key] = raw_tile(key, [P, 4, 512])[:]
+                    nc.sync.dma_start(out=loaded[key], in_=within_v[key[1]])
 
         ident = sbuf.tile([P, P], F32, name="ident", tag="ident")
         keep_sb = sbuf.tile([P, 2, 4], BF16, name="keep_sb", tag="keep_sb")
@@ -138,7 +110,7 @@ def tile_teacher_student_logits_t1_kernel(
         gain_sb = sbuf.tile([P, G, 512], BF16, name="gain_sb", tag="gain_sb", align_bytes=64)
 
         def spread_gain(h):
-            bank = take_bank(("gain", h), [P, 4, P])
+            bank = take_bank(("gain", h), [P, 4, P], 5 + h)
             for j in range(4):
                 nc.tensor.transpose(bank[:, j, :], gain_f32[:, h, j : j + 1].to_broadcast([P, P]), ident[:])
 
@@ -147,7 +119,6 @@ def tile_teacher_student_logits_t1_kernel(
                 out=gain_sb[:, h, :].rearrange("p (u m e) -> p u m e", u=2, e=2),
                 in_=banks["gain", h][:].rearrange("p (u e) m -> p u m e", u=2),
             )
-            give_back(("gain", h))
 
         def copy_on(engine, o, s):
             if engine == "vector":
@@ -158,7 +129,10 @@ def tile_teacher_student_logits_t1_kernel(
         free_groups = list(range(GROUPED))
         group_of = {}
 
-        def interleave(engine, key, cols=WHOLE, newest=False):
+        def interleave(engine, key, start=0, stop=512, newest=False, held=None):
+            cols = slice(start, stop)
+            if key not in grouped and held is not None:
+                grouped[key] = held_slot(held, "held_group", [P, 512, 4], BF16)
             if key not in grouped:
                 group_of[key] = free_groups.pop(-1 if newest else 0)
                 tag = "grouped" + str(group_of[key])
@@ -180,77 +154,53 @@ def tile_teacher_student_logits_t1_kernel(
                     src[:, :, cols].rearrange("p t (n i) -> p n t i", i=4),
                 )
 
-        depth = {"c": 6, "w": 2, "z1": 4, "t": 12, "a": 4, "z2": 5}
+        depth = {"c512": 9, "w512": 2, "z1512": 4, "t256": 4, "t512": 4, "a512": 4, "z2256": 3}
 
-        def quantise(key, cols=None):
-            width = grouped[key].shape[1]
-            if key not in codes:
+        def quantise(*keys):
+            for key in keys:
+                width = grouped[key].shape[1]
                 name = key[0] + str(width)
-                codes[key] = ring(sbuf, name + "codes", depth[key[0]], [P, width], U32)
-                scales[key] = ring(sbuf, name + "scales", depth[key[0]], [P, width], U8)
+                codes[key] = ring(name + "codes", depth[name], [P, width], U32)
+                scales[key] = ring(name + "scales", depth[name], [P, width], U8)
                 share = width // len(parts.get(key, [key]))
                 for n, part in enumerate(parts.get(key, [])):
                     codes[part] = codes[key][:, n * share : (n + 1) * share]
                     scales[part] = scales[key][:, n * share : (n + 1) * share]
-            if cols is None:
-                cols = slice(0, width)
-            nc.vector.quantize_mx(
-                out=codes[key][:, cols].bitcast(FP8X4),
-                scales=scales[key][:, cols],
-                in_=grouped[key][:, cols, :].rearrange("p n t -> p (n t)"),
-            )
-            if key in group_of and cols.stop == width:
-                free_groups.append(group_of[key])
-
-        def quantise_all(*keys):
-            for key in keys:
-                quantise(key)
-
-        def sort_words(engine, *keys):
-            ordered = ring(sbuf, "result", 4, [P, len(keys), 2, 2, P], F32)
-            for n, key in enumerate(keys):
-                copy_on(engine, ordered[:, n], words[key].rearrange("p a (m u) -> p a u m", u=2))
-                sorted_words[key] = ordered[:, n]
+                nc.vector.quantize_mx(
+                    out=codes[key][:].bitcast(FP8X4),
+                    scales=scales[key][:],
+                    in_=grouped[key][:].rearrange("p n t -> p (n t)"),
+                )
+                if key in group_of:
+                    free_groups.append(group_of[key])
 
         def sort_block(engine, key):
-            ordered = ring(sbuf, "result", 4, [P, 4, 2, P], F32)
-            flat = loaded[key][:].rearrange("p a n -> p (a n)").bitcast(F32)
-            copy_on(engine, ordered[:], flat.rearrange("p (j m u) -> p j u m", j=4, u=2))
-            for n in range(2):
-                if key[0] == "a":
-                    sorted_words[key + (n,)] = ordered[:, n:4:2]
-                else:
-                    sorted_words["t", key[1], n, key[2]] = ordered[:, 2 * n : 2 * n + 2]
+            ordered = ring("result", 4, [P, 4, 2, P], F32)
+            copy_on(engine, ordered[:], loaded[key].rearrange("p a (c m u) -> p (a c) u m", c=2, u=2))
+            for c in range(2):
+                sorted_words[key + (c,)] = ordered[:, c:4:2]
 
-        def sort_pair(engine, key):
-            ordered = ring(sbuf, "sorted", 2, [P, 6, 2, P], F32)
-            flat = loaded[key][:].rearrange("p a n -> p (a n)").bitcast(F32)
-            copy_on(engine, ordered[:], flat.rearrange("p (j m u) -> p j u m", j=6, u=2))
-            for c in range(3):
-                sorted_words[key + (c,)] = ordered[:, c:6:3]
-
-        def turn(*keys):
+        def turn(bank_numbers, *keys):
             run = (keys[0][0], "run", *keys)
             parts[run] = keys
-            for key in keys:
-                take_bank(key, [P, 2, 2, P])
+            for n, key in enumerate(keys):
+                take_bank(key, [P, 2, 2, P], bank_numbers[n])
                 for a in range(2):
                     for u in range(2):
                         src = sorted_words[key][:, a, u] if key in sorted_words else words[key][:, a, u:256:2]
                         nc.tensor.transpose(banks[key][:, a, u, :], src, ident[:])
             return run
 
-        def fetch(run, engines=("scalar", "scalar"), late=False):
+        def fetch(run, engines=("scalar", "scalar"), held=None):
             keys = parts[run]
             shape = [P, 256 * len(keys), 4]
-            grouped[run] = late_slot(0, shape, BF16) if late else ring(sbuf, "turned", TURNED, shape, BF16)
+            grouped[run] = ring("turned", TURNED, shape, BF16) if held is None else held_slot(held, "held_turned", shape, BF16)
             for n, key in enumerate(keys):
                 copy_on(
                     engines[n],
                     grouped[run][:, 256 * n : 256 * (n + 1), :].bitcast(F32).rearrange("p (a r) u -> p a r u", a=2),
                     banks[key][:].rearrange("p a u r -> p a r u"),
                 )
-                give_back(key)
             return run
 
         def product(bank, left, cols, right, start, stop):
@@ -267,23 +217,24 @@ def tile_teacher_student_logits_t1_kernel(
         def pair(s):
             return s // 4, s // 2 % 2, s % 2
 
-        def mm1(s, passes=(0, 1, 2), by_pass=False, newest=False):
+        def passes(name, s, which, total, left, right, first_bank):
             h, g, q = pair(s)
-            order = [(a, c) for a in range(2) for c in passes]
-            if by_pass:
-                order = [(a, c) for c in passes for a in range(2)]
-            for a, c in order:
-                n = counts.get(("z1", s, a), 0)
-                counts["z1", s, a] = n + 1
-                if n == 0:
-                    take_bank(("z1", s, a), [P, 512], newest)
-                product(banks["z1", s, a], ("t", g, q, c), slice(a * P, (a + 1) * P), ("c", h, c), n == 0, n == 2)
+            for c in which:
+                for a in (1, 0):
+                    n = counts.get((name, s, a), 0)
+                    counts[name, s, a] = n + 1
+                    if n == 0:
+                        take_bank((name, s, a), [P, 512], first_bank + a)
+                    product(banks[name, s, a], (left, g, q, c), slice(a * P, (a + 1) * P), (right, h, c), n == 0, n == total - 1)
 
-        def add1(s, tiles=(1, 0)):
+        def mm1(s, which=(0, 1, 2)):
+            passes("z1", s, which, 3, "t", "c", {1: 2, 2: 2, 3: 6, 5: 6}.get(s, 0))
+
+        def add1(s):
             h, g, q = pair(s)
             if (h, g) not in z1:
-                z1[h, g] = ring(sbuf, "z1", 4, [P, 4, 512], F32)
-            for a in tiles:
+                z1[h, g] = ring("z1", 4, [P, 4, 512], F32)
+            for a in (0, 1):
                 t = 2 * q + a
                 nc.vector.tensor_tensor(
                     out=z1[h, g][:, t, :].rearrange("p (u m e) -> p m u e", u=2, e=2),
@@ -291,24 +242,14 @@ def tile_teacher_student_logits_t1_kernel(
                     in1=loaded["s", h, g][:, t, :].rearrange("p (m u e) -> p m u e", u=2, e=2),
                     op=ADD,
                 )
-                give_back(("z1", s, a))
 
-        def mm2(s, passes=(0, 1), by_pass=False, newest=False):
-            h, g, q = pair(s)
-            order = [(a, c) for a in range(2) for c in passes]
-            if by_pass:
-                order = [(a, c) for c in passes for a in range(2)]
-            for a, c in order:
-                first = ("z2", s, a) not in banks
-                if first:
-                    take_bank(("z2", s, a), [P, 512], newest)
-                product(banks["z2", s, a], ("a", g, q, c), slice(a * P, (a + 1) * P), ("z1", h, c), first, not first)
+        def mm2(s, which=(0, 1)):
+            passes("z2", s, which, 2, "a", "z1", 2 * (s % 2) if s >= 8 else 2)
 
-        def add2(s, tiles=(1, 0)):
+        def add2(s):
             h, g, q = pair(s)
-            if s not in z2:
-                z2[s] = ring(sbuf, "z2", 3, [P, 2, 512], F32)
-            for a in tiles:
+            z2[s] = ring("z2", 3, [P, 2, 512], F32)
+            for a in (0, 1):
                 t = 2 * q + a
                 nc.vector.scalar_tensor_tensor(
                     out=z2[s][:, a, :],
@@ -318,11 +259,9 @@ def tile_teacher_student_logits_t1_kernel(
                     op0=MULT,
                     op1=ADD,
                 )
-                give_back(("z2", s, a))
 
-        def gain_mul(s, held=True):
-            shape = [P, 2, 512]
-            pair_tile = late_slot(s, shape, F32) if held else raw.tile(shape, F32, name="gained" + str(s), tag="gained" + str(s), align_bytes=64, offset=(14 + s % 2) * BLOCK)
+        def gain_mul(s):
+            pair_tile = held_slot(s, "gained", [P, 2, 512], F32)
             for a in range(2):
                 gained[s, a] = pair_tile[:, a, :]
             nc.gpsimd.tensor_tensor(
@@ -333,251 +272,199 @@ def tile_teacher_student_logits_t1_kernel(
             )
 
         def gain_mul_tile(s, a, engine, slot):
-            gained[s, a] = late_slot(slot, [P, 512], F32)[:]
+            gained[s, a] = held_slot(slot, "gained_tile", [P, 512], F32)[:]
             engine.tensor_tensor(out=gained[s, a], in0=z2[s][:, a, :], in1=gain_sb[:, s // 4, :], op=MULT)
 
-        def round2(engine, s, by_tile=False):
-            shape = [P, 2, 512]
-            if engine == "gpsimd":
-                rounded = late_slot(s, shape, BF16)
-                nc.gpsimd.tensor_scalar(out=rounded[:], in0=z2[s][:], scalar1=1.0, scalar2=0.0, op0=MULT, op1=ADD)
-            else:
-                rounded = ring(sbuf, "rounded", 2, shape, BF16)
-                for tiles in (slice(1, 2), slice(0, 1)) if by_tile else (slice(0, 2),):
-                    copy_on(engine, rounded[:, tiles], z2[s][:, tiles])
+        def round2(s):
+            rounded = ring("rounded", 2, [P, 2, 512], BF16)
+            nc.scalar.copy(out=rounded[:], in_=z2[s][:])
             sorted_words["z2", s] = rounded[:].bitcast(F32).rearrange("p a (u m) -> p a u m", u=2)
 
         def turn2(s):
-            if "z2t" in bank_of:
-                free_banks.append(bank_of["z2t"])
-            bank = take_bank(("z2t", s), [P, 2, 2, P], "z2t" in bank_of)
-            bank_of["z2t"] = bank_of["z2t", s]
+            bank = take_bank(("z2t", s), [P, 2, 2, P], 4 if s == 0 else 6 + s % 2)
             for a in range(2):
                 for u in range(2):
                     nc.tensor.transpose(bank[:, a, u, :], sorted_words["z2", s][:, a, u], ident[:])
 
         def fetch2(s):
-            grouped["z2", s] = late_slot(s + 1, [P, 2 * P, 4], BF16)
+            grouped["z2", s] = held_slot(s + 1, "z2turned", [P, 2 * P, 4], BF16)
             nc.scalar.copy(
                 out=grouped["z2", s][:].bitcast(F32).rearrange("p (a r) u -> p a r u", a=2),
                 in_=banks["z2t", s][:].rearrange("p a u r -> p a r u"),
             )
 
         def turn2_unrounded(s):
-            grouped["z2", s] = late_slot(s + 1, [P, 2 * P, 4], BF16)
-            for a in (1, 0):
-                bank = take_bank(("z2t", s, a), [P, 4, P])
+            grouped["z2", s] = held_slot(s + 1, "z2turned", [P, 2 * P, 4], BF16)
+            for a in (0, 1):
+                bank = take_bank(("z2t", s, a), [P, 4, P], a)
                 for t in range(4):
                     start = t // 2 * 256 + t % 2
                     nc.tensor.transpose(bank[:, t, :], z2[s][:, a, start : t // 2 * 256 + 256 : 2], ident[:])
                 nc.scalar.copy(
                     out=grouped["z2", s][:, a * P : (a + 1) * P, :], in_=bank[:].rearrange("p t n -> p n t")
                 )
-                give_back(("z2t", s, a))
 
-        def mm3(*tiles):
-            for i in tiles:
-                take_bank(("out", i), [P, 512])
-                product(banks["out", i], ("z2", i // 2), slice(i % 2 * P, (i % 2 + 1) * P), ("w", i // 8), True, True)
+        def mm3(s):
+            for a in (1, 0):
+                take_bank(("out", s, a), [P, 512], (2 if s == 11 else 4) + a)
+                product(banks["out", s, a], ("z2", s), slice(a * P, (a + 1) * P), ("w", s // 4), True, True)
 
-        def add3(*tiles):
-            for i in tiles:
-                if i // 2 not in result:
-                    result[i // 2] = ring(sbuf, "result", 4, [P, 2, 512], F32)
-            for i in reversed(tiles):
+        def add3(s, tiles=(0, 1)):
+            if s not in result:
+                result[s] = ring("result", 4, [P, 2, 512], F32)
+            for a in tiles:
                 nc.vector.tensor_tensor(
-                    out=result[i // 2][:, i % 2, :].rearrange("p (m u e) -> p m u e", u=2, e=2),
-                    in0=banks["out", i][:].rearrange("p (m u e) -> p m u e", u=2, e=2),
-                    in1=gained[i // 2, i % 2].rearrange("p (u m e) -> p m u e", u=2, e=2),
+                    out=result[s][:, a, :].rearrange("p (m u e) -> p m u e", u=2, e=2),
+                    in0=banks["out", s, a][:].rearrange("p (m u e) -> p m u e", u=2, e=2),
+                    in1=gained[s, a].rearrange("p (u m e) -> p m u e", u=2, e=2),
                     op=ADD,
                 )
-                give_back(("out", i))
-            for i in tiles:
-                if i % 2 == 1 and i < 20:
-                    store(i // 2)
-
-        def store(s, tiles=slice(0, 2)):
             h, g, q = pair(s)
-            rows = slice(2 * q + tiles.start, 2 * q + tiles.stop)
-            nc.sync.dma_start(out=out_v[g, :, rows, h * 512 : (h + 1) * 512], in_=result[s][:, tiles, :])
+            rows = slice(min(tiles), max(tiles) + 1)
+            nc.sync.dma_start(
+                out=out_v[g, :, 2 * q + rows.start : 2 * q + rows.stop, h * 512 : (h + 1) * 512], in_=result[s][:, rows, :]
+            )
 
-        def tea(i):
-            return ("t", i // 6, i // 3 % 2, i % 3)
-
-        def aff(n):
-            return ("a", n // 2, n % 2, 0), ("a", n // 2, n % 2, 1)
-
-        def passes1(*units):
-            for i in units:
-                mm1(i // 3, (i % 3,))
-
-        def part(engine, key, start, stop, newest=False):
-            interleave(engine, key, slice(start, stop), newest)
-
-        for c in range(3):
-            load_all(("tpass", 0, c), ("c", 0, c))
-        load_all(("t", 1, 0), ("s", 0, 0), ("t", 1, 1), ("c", 1, 0))
         nc.sync.dma_start(out=gain_in[:], in_=gain.rearrange("(h p j) -> p h j", p=P, j=4))
-        load_all(("s", 0, 1), ("c", 1, 1), ("c", 1, 2), ("a", 0, 0), ("a", 0, 1))
-        nc.sync.dma_start(out=keep_sb[:], in_=keep.rearrange("(g p t) -> p g t", p=P, t=4))
+        load(("c", 0, 0), ("t", 0, 0), ("c", 0, 1), ("c", 0, 2), ("t", 0, 1), ("cc", 0), ("s", 0, 0), ("t", 1, 0), ("t", 1, 1))
         make_identity(nc, ident[:])
-
-        r0 = fetch(turn(tea(0), tea(3)))
-        interleave("vector", ("c", 0, 0))
-        r1 = fetch(turn(tea(1), tea(4)))
-        quantise_all(r0, ("c", 0, 0))
-        passes1(0, 3)
-        interleave("vector", ("c", 0, 1))
-        sort_block("scalar", ("tpass", 0, 2))
-        r2 = fetch(turn(tea(2), tea(5)))
-        quantise_all(r1, ("c", 0, 1))
-        passes1(1, 4)
-        interleave("vector", ("c", 0, 2))
-        load_all(("a", 1, 0), ("s", 1, 0), ("w", 0), ("a", 1, 1))
-        sort_words("scalar", tea(8))
-        quantise(("c", 0, 2))
-        sort_words("vector", tea(6), tea(7))
-        r6 = fetch(turn(tea(6), tea(7)))
-        quantise(r2)
-        passes1(2, 5)
-        quantise(r6)
-        r8 = turn(tea(8), tea(9))
-        sort_words("scalar", tea(10), tea(11))
-        fetch(r8)
-        part("gpsimd", ("c", 1, 0), 352, 512, True)
-        add1(0)
-        add1(1)
-        passes1(6, 7)
         nc.scalar.copy(out=gain_f32[:], in_=gain_in[:])
-        r10 = turn(tea(10), tea(11))
-        spread_gain(0)
-        fetch(r10)
-        part("scalar", ("c", 1, 0), 0, 352)
-        load_all(("c", 2, 0), ("s", 1, 1), ("c", 2, 1), ("c", 2, 2), ("w", 1))
-        fetch_gain(0)
-        quantise(r8)
-        passes1(8, 9)
-        interleave("vector", ("z1", 0, 0))
-        quantise(r10)
-        passes1(10, 11)
-        interleave("scalar", ("c", 1, 2))
-        quantise_all(("z1", 0, 0), ("c", 1, 0))
-        part("gpsimd", ("c", 1, 1), 256, 512, True)
+        for h in range(G):
+            spread_gain(h)
+        for h in range(G):
+            fetch_gain(h)
+
+        def turn_teacher(g, q, bank_numbers, held=None):
+            first = fetch(turn(bank_numbers[:2], ("t", g, q, 0), ("t", g, q, 1)))
+            return first, fetch(turn(bank_numbers[2:], ("t", g, q, 2)), held=held)
+
+        def turn_affinity(s, bank_numbers):
+            return turn(bank_numbers, ("a", s // 2, s % 2, 0), ("a", s // 2, s % 2, 1))
+
+        interleave("vector", ("c", 0, 0))
+        runs = turn_teacher(0, 0, (2, 3, 4))
+        quantise(("c", 0, 0))
+        load(("s", 0, 1), ("a", 0, 0))
+        interleave("vector", ("c", 0, 1))
+        quantise(runs[0])
+        mm1(0, (0,))
+        interleave("vector", ("c", 0, 2))
+        quantise(("c", 0, 1), runs[1], ("c", 0, 2))
+        load(("c", 1, 1), ("c", 1, 2))
+        runs = turn_teacher(0, 1, (5, 6, 7))
+        mm1(0, (1, 2))
+        load(("s", 1, 0))
+        nc.sync.dma_start(out=keep_sb[:], in_=keep.rearrange("(g p t) -> p g t", p=P, t=4))
+        quantise(runs[0])
+        interleave("vector", ("c", 1, 0))
+        quantise(runs[1])
+        mm1(1)
+        interleave("scalar", ("c", 2, 0))
+        add1(0)
+        quantise(("c", 1, 0))
+        add1(1)
+        load(("a", 0, 1))
+        runs = turn_teacher(1, 0, (4, 5, 6))
+        later = turn_teacher(1, 1, (7, 4, 5), held=1)
+        interleave("scalar", ("z1", 0, 0))
+        quantise(("c", 2, 0), *runs)
+        load(("w", 0), ("a", 1, 0))
+        mm1(2)
+        quantise(*later)
+        load(("s", 1, 1))
+        mm1(3)
+        interleave("vector", ("c", 1, 1))
+        interleave("gpsimd", ("c", 1, 2), 192, 512, held=1)
+        interleave("scalar", ("c", 1, 2), 0, 192)
+        a_run = {0: fetch(turn_affinity(0, (4, 5)))}
+        mm1(4, (0,))
+        load(("a", 1, 1))
         add1(2)
-        mm1(4, (0,), newest=True)
-        a0 = fetch(turn(*aff(0)))
+        a_run[1] = turn_affinity(1, (2, 3))
         add1(3)
-        load_all(("s", 2, 0), ("s", 2, 1), ("w", 2))
-        part("scalar", ("z1", 0, 1), 0, 192)
-        quantise(("c", 1, 2))
-        mm1(4, (2,))
-        a1 = turn(*aff(1))
-        part("vector", ("c", 1, 1), 0, 256)
-        part("vector", ("z1", 0, 1), 192, 512)
-        fetch(a1, late=True)
         quantise(("c", 1, 1))
         mm1(4, (1,))
-        quantise_all(a0, ("z1", 0, 1))
-        mm2(0, by_pass=True)
+        a_run[2] = turn_affinity(2, (4, 5))
+        load(("c", 2, 1))
+        interleave("vector", ("z1", 0, 1), 0, 320)
+        interleave("scalar", ("z1", 0, 1), 320, 512)
+        fetch(a_run[1], held=0)
+        interleave("scalar", ("w", 0))
+        quantise(a_run[0], ("z1", 0, 0))
+        mm2(0, (0,))
+        quantise(("z1", 0, 1))
+        mm2(0, (1,))
+        quantise(("c", 1, 2))
+        mm1(4, (2,))
+        mm1(5)
+        quantise(a_run[1])
+        load(("c", 2, 2), ("s", 2, 0), ("w", 1), ("s", 2, 1))
 
-        first_pairs = {0: [4], 1: [5], 2: [6], 3: [7], 5: [8], 6: [9, 10], 7: [11]}
-        last_tiles = {s: (2 * s - 4, 2 * s - 3) for s in range(2, 12)}
-        early = {1: [("c", 2, 0)], 2: [("z1", 1, 0)], 3: [("z1", 1, 1)], 6: [("z1", 2, 0)], 7: [("z1", 2, 1)]}
-        after = {2: [("c", 2, 1)], 3: [("c", 2, 2)], 4: [("w", 1)], 5: [("w", 2)]}
-        quantised = {1: [("w", 0)], 2: [("c", 2, 0), ("z1", 1, 0)], 3: [("z1", 1, 1), ("c", 2, 1)], 4: [("c", 2, 2)], 5: [("w", 1)], 6: [("z1", 2, 0)], 7: [("z1", 2, 1), ("w", 2)]}
-        BY_GPSIMD = (1, 2, 5, 6)
-        for s in range(12):
-            border = s in (3, 7)
-            ahead = first_pairs.get(s + 1, [])
-            if s - 1 in BY_GPSIMD:
-                round2("gpsimd", s - 1)
-            if s > 0:
-                gain_mul(s - 1, s - 1 not in BY_GPSIMD)
-            if s >= 2 and s != 6:
-                mm3(*last_tiles[s])
-            if s == 0:
-                part("gpsimd", ("w", 0), 256, 512, True)
-                part("scalar", ("w", 0), 0, 256)
-                sort_block("scalar", ("a", 1, 0))
-            if s - 1 not in BY_GPSIMD and s > 0:
-                turn2(s - 1)
-                if s == 1:
-                    a2 = fetch(turn(*aff(2)))
-                if s == 4:
-                    spread_gain(1)
-                fetch2(s - 1)
-            if s == 5:
-                add2(s)
-            for k in first_pairs.get(s, []):
-                add1(k)
-                if k == 9:
-                    mm3(*last_tiles[6])
-            for key in early.get(s, []):
-                interleave("scalar", key)
-            if s == 2:
-                a3 = turn(*aff(3))
-            if s in (2, 6) and s - 1 in BY_GPSIMD:
-                turn2(s - 1)
-            if border and s - 1 in BY_GPSIMD:
-                turn2(s - 1)
-                fetch2(s - 1)
-            if s != 5:
-                add2(s)
-            if ahead and s != 4:
-                mm1(ahead[0])
-            if s == 2:
-                fetch(a3)
-            if s - 1 in BY_GPSIMD and not border:
-                if s == 5:
-                    turn2(s - 1)
-                fetch2(s - 1)
-            for k in ahead[1:]:
-                mm1(k)
-            if border:
-                mm2(s + 1, (0,), newest=True)
-            if s == 3:
-                mm1(8, (0,))
-            if s not in (0, 1, 2, 5, 11) and not border:
+        interleave("gpsimd", ("c", 2, 1), 208, 512, held=0)
+        fetch(a_run[2])
+        interleave("scalar", ("c", 2, 1), 0, 208)
+        add2(0)
+        round2(0)
+        a_run[3] = fetch(turn_affinity(3, (4, 5)))
+        mm2(1)
+        load(("w", 2))
+        add1(4)
+        mm1(6)
+        quantise(("w", 0), a_run[2], ("c", 2, 1))
+        gain_mul(0)
+        turn2(0)
+        fetch2(0)
+        interleave("scalar", ("c", 2, 2))
+        add1(5)
+        add2(1)
+        round2(1)
+        mm2(2)
+        interleave("scalar", ("z1", 1, 0))
+        add1(6)
+        mm1(7)
+        quantise(a_run[3], ("z2", 0))
+
+        first_pair = {s: s + 5 for s in range(2, 7)}
+        interleaved = {2: [("z1", 1, 1)], 3: [("w", 1)], 4: [("z1", 2, 0)], 5: [("w", 2)], 6: [("z1", 2, 1)]}
+        quantised = {2: [("c", 2, 2), ("z1", 1, 0)], 3: [("z1", 1, 1)], 4: [("w", 1)], 5: [("z1", 2, 0)], 7: [("z1", 2, 1), ("w", 2)]}
+        for s in range(2, 12):
+            early = s in (4, 5, 6)
+            gain_mul(s - 1)
+            mm3(s - 2)
+            turn2(s - 1)
+            fetch2(s - 1)
+            if early:
+                add1(first_pair[s])
+                if s < 6:
+                    mm1(first_pair[s] + 1)
+            add2(s)
+            if s < 11:
+                round2(s)
+            if s in (3, 7):
+                mm2(s + 1, (0,))
+            elif s < 11:
                 mm2(s + 1)
-            if s >= 2:
-                add3(*last_tiles[s])
-            if s == 5:
-                mm2(s + 1)
-            if s == 4:
-                fetch_gain(1)
-            if s == 7:
-                spread_gain(2)
-                fetch_gain(2)
-            if s not in BY_GPSIMD and s < 11:
-                round2("scalar", s)
-            if s == 0:
-                sort_block("scalar", ("a", 1, 1))
-            for key in after.get(s, []):
-                interleave("scalar", key)
-            if s == 0:
-                quantise(a1)
-                mm2(1)
-            quantise_all(*quantised.get(s, []))
-            if s == 1:
-                quantise(a2)
-                mm2(2)
             if s == 2:
-                quantise(a3)
-                mm2(3)
-            if s > 0:
-                quantise(("z2", s - 1))
-            if s == 4:
-                mm1(8, (2,))
-            if border:
-                mm2(s + 1, (1,))
+                add1(7)
+                mm1(8, (0, 1))
+            for key in interleaved.get(s, []):
+                interleave("scalar", key)
             if s == 3:
-                mm1(8, (1,))
+                add1(8)
+                mm1(9)
+            add3(s - 2)
+            for key in quantised.get(s, []):
+                quantise(key)
+                if key == ("c", 2, 2):
+                    mm1(8, (2,))
+                if key in (("z1", 1, 1), ("z1", 2, 1)):
+                    mm2(s + 1, (1,))
+            quantise(("z2", s - 1))
         turn2_unrounded(11)
-        mm3(20, 21)
-        gain_mul_tile(11, 1, nc.vector, 13)
+        mm3(10)
+        gain_mul_tile(11, 1, nc.vector, 11)
         quantise(("z2", 11))
         gain_mul_tile(11, 0, nc.gpsimd, 12)
-        mm3(22, 23)
-        for i in (21, 20, 23, 22):
-            add3(i)
-            store(i // 2, slice(i % 2, i % 2 + 1))
+        mm3(11)
+        for s, a in ((10, 0), (10, 1), (11, 1), (11, 0)):
+            add3(s, (a,))

@@ -20,10 +20,10 @@ GROUPED = 4
 TURNED = 4
 HELD = 3
 PLACE = {
-    ("c", 0, 0): 0, ("t", 0, 0): 4, ("c", 0, 1): 10, ("c", 0, 2): 14, ("t", 0, 1): 18, ("s", 0, 0): 24, ("cc", 0): 28,
-    ("t", 1, 0): 36, ("t", 1, 1): 42, ("s", 0, 1): 0, ("a", 0, 0): 4, ("c", 1, 1): 10, ("c", 1, 2): 14,
-    ("s", 1, 0): 18, ("a", 0, 1): 24, ("w", 0): 28, ("a", 1, 0): 36, ("s", 1, 1): 42, ("a", 1, 1): 4,
-    ("c", 2, 1): 32, ("c", 2, 2): 10, ("s", 2, 0): 0, ("w", 1): 14, ("s", 2, 1): 24, ("w", 2): 36,
+    ("c", 0, 0): 0, ("t", 0, 0): 4, ("c", 0, 1): 10, ("c", 0, 2): 14, ("t", 0, 1): 18, ("s", 0, 0): 24, ("c", 1, 0): 28,
+    ("c", 1, 1): 32, ("t", 1, 0): 36, ("t", 1, 1): 42, ("s", 0, 1): 0, ("c", 1, 2): 4, ("a", 0, 0): 10, ("c", 2, 0): 14,
+    ("s", 1, 0): 18, ("a", 0, 1): 24, ("w", 0): 28, ("a", 1, 0): 32, ("c", 2, 1): 36, ("s", 1, 1): 42, ("a", 1, 1): 4,
+    ("c", 2, 2): 10, ("s", 2, 0): 0, ("w", 1): 14, ("s", 2, 1): 24, ("w", 2): 28,
 }
 HELD_PLACE = 48
 
@@ -281,7 +281,7 @@ def tile_teacher_student_logits_t1_kernel(
             sorted_words["z2", s] = rounded[:].bitcast(F32).rearrange("p a (u m) -> p a u m", u=2)
 
         def turn2(s):
-            bank = take_bank(("z2t", s), [P, 2, 2, P], 4 if s == 0 else 6 + s % 2)
+            bank = take_bank(("z2t", s), [P, 2, 2, P], 6 + s % 2)
             for a in range(2):
                 for u in range(2):
                     nc.tensor.transpose(bank[:, a, u, :], sorted_words["z2", s][:, a, u], ident[:])
@@ -326,7 +326,7 @@ def tile_teacher_student_logits_t1_kernel(
             )
 
         nc.sync.dma_start(out=gain_in[:], in_=gain.rearrange("(h p j) -> p h j", p=P, j=4))
-        load(("c", 0, 0), ("t", 0, 0), ("c", 0, 1), ("c", 0, 2), ("t", 0, 1), ("cc", 0), ("s", 0, 0), ("t", 1, 0), ("t", 1, 1))
+        load(("c", 0, 0), ("t", 0, 0), ("c", 0, 1), ("t", 0, 1), ("c", 0, 2), ("c", 1, 0), ("s", 0, 0), ("c", 1, 1), ("t", 1, 0), ("t", 1, 1))
         make_identity(nc, ident[:])
         nc.scalar.copy(out=gain_f32[:], in_=gain_in[:])
         for h in range(G):
@@ -344,81 +344,79 @@ def tile_teacher_student_logits_t1_kernel(
         interleave("vector", ("c", 0, 0))
         runs = turn_teacher(0, 0, (2, 3, 4))
         quantise(("c", 0, 0))
-        load(("s", 0, 1), ("a", 0, 0))
+        load(("s", 0, 1), ("c", 1, 2))
         interleave("vector", ("c", 0, 1))
-        quantise(runs[0])
-        mm1(0, (0,))
-        interleave("vector", ("c", 0, 2))
-        quantise(("c", 0, 1), runs[1], ("c", 0, 2))
-        load(("c", 1, 1), ("c", 1, 2))
+        quantise(runs[0], ("c", 0, 1), runs[1])
         runs = turn_teacher(0, 1, (5, 6, 7))
-        mm1(0, (1, 2))
+        mm1(0, (0, 1))
+        interleave("vector", ("c", 0, 2))
+        load(("a", 0, 0), ("c", 2, 0))
+        quantise(runs[0], ("c", 0, 2))
+        mm1(0, (2,))
         load(("s", 1, 0))
         nc.sync.dma_start(out=keep_sb[:], in_=keep.rearrange("(g p t) -> p g t", p=P, t=4))
-        quantise(runs[0])
-        interleave("vector", ("c", 1, 0))
         quantise(runs[1])
         mm1(1)
-        interleave("scalar", ("c", 2, 0))
+        interleave("scalar", ("c", 1, 0))
+        interleave("scalar", ("c", 1, 1))
         add1(0)
         quantise(("c", 1, 0))
         add1(1)
-        load(("a", 0, 1))
+        load(("a", 0, 1), ("w", 0), ("a", 1, 0))
         runs = turn_teacher(1, 0, (4, 5, 6))
-        later = turn_teacher(1, 1, (7, 4, 5), held=1)
-        interleave("scalar", ("z1", 0, 0))
-        quantise(("c", 2, 0), *runs)
-        load(("w", 0), ("a", 1, 0))
+        later = turn_teacher(1, 1, (7, 0, 1), held=1)
+        load(("c", 2, 1), ("s", 1, 1))
+        interleave("scalar", ("c", 1, 2))
+        interleave("vector", ("z1", 0, 0))
+        quantise(*runs)
         mm1(2)
-        quantise(*later)
-        load(("s", 1, 1))
+        quantise(later[0], ("c", 1, 1), ("z1", 0, 0), later[1])
         mm1(3)
-        interleave("vector", ("c", 1, 1))
-        interleave("gpsimd", ("c", 1, 2), 192, 512, held=1)
-        interleave("scalar", ("c", 1, 2), 0, 192)
-        a_run = {0: fetch(turn_affinity(0, (4, 5)))}
-        mm1(4, (0,))
+        interleave("gpsimd", ("c", 2, 0), 208, 512, held=1)
+        interleave("scalar", ("c", 2, 0), 0, 208)
         load(("a", 1, 1))
+        a_run = {0: fetch(turn_affinity(0, (4, 5)))}
+        mm1(4, (0, 1))
         add1(2)
-        a_run[1] = turn_affinity(1, (2, 3))
+        a_run[1] = turn_affinity(1, (4, 5))
         add1(3)
-        quantise(("c", 1, 1))
-        mm1(4, (1,))
-        a_run[2] = turn_affinity(2, (4, 5))
-        load(("c", 2, 1))
+        load(("c", 2, 2), ("s", 2, 0))
+        quantise(("c", 1, 2))
+        mm1(4, (2,))
         interleave("vector", ("z1", 0, 1), 0, 320)
         interleave("scalar", ("z1", 0, 1), 320, 512)
         fetch(a_run[1], held=0)
         interleave("scalar", ("w", 0))
-        quantise(a_run[0], ("z1", 0, 0))
+        quantise(a_run[0])
         mm2(0, (0,))
         quantise(("z1", 0, 1))
         mm2(0, (1,))
-        quantise(("c", 1, 2))
-        mm1(4, (2,))
+        a_run[2] = turn_affinity(2, (4, 5))
         mm1(5)
-        quantise(a_run[1])
-        load(("c", 2, 2), ("s", 2, 0), ("w", 1), ("s", 2, 1))
+        quantise(("c", 2, 0), a_run[1])
+        load(("w", 1), ("s", 2, 1))
 
         interleave("gpsimd", ("c", 2, 1), 208, 512, held=0)
         fetch(a_run[2])
         interleave("scalar", ("c", 2, 1), 0, 208)
+        add1(4)
         add2(0)
         round2(0)
-        a_run[3] = fetch(turn_affinity(3, (4, 5)))
         mm2(1)
-        load(("w", 2))
-        add1(4)
         mm1(6)
+        interleave("scalar", ("c", 2, 2), 0, 320)
+        load(("w", 2))
         quantise(("w", 0), a_run[2], ("c", 2, 1))
         gain_mul(0)
-        turn2(0)
-        fetch2(0)
-        interleave("scalar", ("c", 2, 2))
         add1(5)
+        turn2(0)
+        a_run[3] = turn_affinity(3, (4, 5))
+        fetch2(0)
+        fetch(a_run[3])
         add2(1)
         round2(1)
         mm2(2)
+        interleave("scalar", ("c", 2, 2), 320, 512)
         interleave("scalar", ("z1", 1, 0))
         add1(6)
         mm1(7)

@@ -16,16 +16,10 @@ MULT = mybir.AluOpType.mult
 ADD = mybir.AluOpType.add
 
 KIB = 1024
-GROUPED = 4
-TURNED = 4
-HELD = 3
-PLACE = {
-    ("c", 0, 0): 0, ("t", 0, 0): 4, ("c", 0, 1): 10, ("c", 0, 2): 14, ("t", 0, 1): 18, ("s", 0, 0): 24, ("c", 1, 0): 28,
-    ("c", 1, 1): 32, ("t", 1, 0): 36, ("t", 1, 1): 42, ("s", 0, 1): 0, ("c", 1, 2): 4, ("a", 0, 0): 10, ("c", 2, 0): 14,
-    ("s", 1, 0): 18, ("a", 0, 1): 24, ("w", 0): 28, ("a", 1, 0): 32, ("c", 2, 1): 36, ("s", 1, 1): 42, ("a", 1, 1): 4,
-    ("c", 2, 2): 10, ("s", 2, 0): 0, ("w", 1): 14, ("s", 2, 1): 24, ("w", 2): 28,
-}
-HELD_PLACE = 48
+PLACE = 4 * KIB
+LOAD_PLACES = 7
+WORK_PLACES = 12
+PAIR_BYTES = 6 * KIB
 
 
 def tile_teacher_student_logits_t1_kernel(
@@ -40,6 +34,16 @@ def tile_teacher_student_logits_t1_kernel(
 
         counts = {}
         banks = {}
+        bank_of = {}
+        free_banks = list(range(8))
+        turn_banks = []
+        list_of = {}
+        free_loads = list(range(6, 6 + LOAD_PLACES))
+        free_work = list(range(6 + LOAD_PLACES, 6 + LOAD_PLACES + WORK_PLACES))
+        place_of = {}
+
+        def label(key):
+            return "_".join(str(x) for x in key)
 
         def ring(name, depth, shape, dtype):
             n = counts.get(name, 0)
@@ -47,14 +51,23 @@ def tile_teacher_student_logits_t1_kernel(
             tag = name + str(n % depth)
             return sbuf.tile(shape, dtype, name=tag, tag=tag, align_bytes=64)
 
-        def held_slot(n, name, shape, dtype):
-            tag = name + str(n)
-            return raw.tile(shape, dtype, name=tag, tag=tag, align_bytes=64, offset=(HELD_PLACE + 4 * (n % HELD)) * KIB)
+        def placed(name, place, shape, dtype):
+            return raw.tile(shape, dtype, name=name, tag=name, align_bytes=64, offset=place)
 
-        def take_bank(key, shape, n):
-            tag = "bank" + str(n)
+        def work_tile(key, shape, dtype, newest=False):
+            place_of[key] = free_work.pop(-1 if newest else 0)
+            return placed("work_" + label(key), place_of[key] * PLACE, shape, dtype)
+
+        def take_bank(key, shape):
+            free = turn_banks if key[0] in ("a", "z2") and len(key) != 3 and turn_banks else free_banks
+            bank_of[key] = free.pop(0)
+            list_of[key] = free
+            tag = "bank" + str(bank_of[key])
             banks[key] = psum.tile(shape, F32, name=tag, tag=tag)
             return banks[key]
+
+        def give_bank(key):
+            list_of[key].append(bank_of[key])
 
         teacher_v = teacher.rearrange("(g p t) k -> g p t k", p=P, t=4)
         affinity_v = affinity.rearrange("(g p t) k -> g p t k", p=P, t=4)
@@ -67,41 +80,51 @@ def tile_teacher_student_logits_t1_kernel(
         words = {}
         sorted_words = {}
         grouped = {}
+        done_cols = {}
         parts = {}
         codes = {}
         scales = {}
-        z1 = {}
-        z2 = {}
+        z = {}
         result = {}
         gained = {}
 
-        def raw_tile(key, shape):
-            name = "raw_" + "_".join(str(x) for x in key)
-            return raw.tile(shape, BF16, name=name, tag=name, align_bytes=64, offset=PLACE[key] * KIB)
+        def load(key):
+            name = "raw_" + label(key)
+            if key[0] == "t":
+                place = (2 * key[1] + key[2]) * PAIR_BYTES
+            else:
+                place_of["load", key] = free_loads.pop(0)
+                place = place_of["load", key] * PLACE
+            if key[0] in ("c", "s"):
+                source = confusion_v if key[0] == "c" else student_v
+                loaded[key] = placed(name, place, [P, 4, 512], BF16)[:]
+                nc.sync.dma_start(out=loaded[key], in_=source[key[2], :, :, key[1] * 512 : (key[1] + 1) * 512])
+            if key[0] in ("t", "a"):
+                g, q = key[1:]
+                source = teacher_v if key[0] == "t" else affinity_v
+                width = source.shape[-1]
+                t = placed(name, place, [P, 2 * width], BF16)
+                nc.sync.dma_start(out=t[:], in_=source[g, :, 2 * q : 2 * q + 2, :].rearrange("p a k -> p (a k)"))
+                loaded[key] = t[:].bitcast(F32).rearrange("p (a k) -> p a k", a=2)
+                for c in range(width // 512):
+                    words[key + (c,)] = loaded[key][:, :, 256 * c : 256 * (c + 1)]
+            if key[0] == "w":
+                t = placed(name, place, [P, 4 * 512], BF16)
+                nc.sync.dma_start(out=t[:], in_=within_v[key[1]].rearrange("p j n -> p (j n)"))
+                loaded[key] = t[:].rearrange("p (j n) -> p j n", j=4)
+            if key[0] == "keep":
+                nc.sync.dma_start(out=keep_sb[:], in_=keep.rearrange("(g p t) -> p g t", p=P, t=4))
+                free_loads.insert(0, place_of["load", key])
 
-        def load(*keys):
-            for key in keys:
-                if key[0] in ("c", "s"):
-                    source = confusion_v if key[0] == "c" else student_v
-                    loaded[key] = raw_tile(key, [P, 4, 512])[:]
-                    nc.sync.dma_start(out=loaded[key], in_=source[key[2], :, :, key[1] * 512 : (key[1] + 1) * 512])
-                if key[0] == "cc":
-                    t = raw_tile(key, [P, 4, 1024])
-                    nc.sync.dma_start(out=t[:], in_=confusion_v[key[1], :, :, 512:])
-                    for h in (1, 2):
-                        loaded["c", h, key[1]] = t[:, :, (h - 1) * 512 : h * 512]
-                if key[0] in ("t", "a"):
-                    g, q = key[1:]
-                    source = teacher_v if key[0] == "t" else affinity_v
-                    width = source.shape[-1]
-                    t = raw_tile(key, [P, 2 * width])
-                    nc.sync.dma_start(out=t[:], in_=source[g, :, 2 * q : 2 * q + 2, :].rearrange("p a k -> p (a k)"))
-                    loaded[key] = t[:].bitcast(F32).rearrange("p (a k) -> p a k", a=2)
-                    for c in range(width // 512):
-                        words[key + (c,)] = loaded[key][:, :, 256 * c : 256 * (c + 1)]
-                if key[0] == "w":
-                    loaded[key] = raw_tile(key, [P, 4, 512])[:]
-                    nc.sync.dma_start(out=loaded[key], in_=within_v[key[1]])
+        pending = []
+
+        def load_more():
+            while pending and (pending[0][0] == "t" or free_loads):
+                load(pending.pop(0))
+
+        def release(key):
+            free_loads.append(place_of["load", key])
+            load_more()
 
         ident = sbuf.tile([P, P], F32, name="ident", tag="ident")
         keep_sb = sbuf.tile([P, 2, 4], BF16, name="keep_sb", tag="keep_sb")
@@ -110,7 +133,7 @@ def tile_teacher_student_logits_t1_kernel(
         gain_sb = sbuf.tile([P, G, 512], BF16, name="gain_sb", tag="gain_sb", align_bytes=64)
 
         def spread_gain(h):
-            bank = take_bank(("gain", h), [P, 4, P], 5 + h)
+            bank = take_bank(("gain", h), [P, 4, P])
             for j in range(4):
                 nc.tensor.transpose(bank[:, j, :], gain_f32[:, h, j : j + 1].to_broadcast([P, P]), ident[:])
 
@@ -119,6 +142,7 @@ def tile_teacher_student_logits_t1_kernel(
                 out=gain_sb[:, h, :].rearrange("p (u m e) -> p u m e", u=2, e=2),
                 in_=banks["gain", h][:].rearrange("p (u e) m -> p u m e", u=2),
             )
+            give_bank(("gain", h))
 
         def copy_on(engine, o, s):
             if engine == "vector":
@@ -126,18 +150,11 @@ def tile_teacher_student_logits_t1_kernel(
             else:
                 nc.scalar.copy(out=o, in_=s)
 
-        free_groups = list(range(GROUPED))
-        group_of = {}
-
-        def interleave(engine, key, start=0, stop=512, newest=False, held=None):
+        def interleave(engine, key, start=0, stop=512, newest=False):
             cols = slice(start, stop)
-            if key not in grouped and held is not None:
-                grouped[key] = held_slot(held, "held_group", [P, 512, 4], BF16)
             if key not in grouped:
-                group_of[key] = free_groups.pop(-1 if newest else 0)
-                tag = "grouped" + str(group_of[key])
-                grouped[key] = sbuf.tile([P, 512, 4], BF16, name=tag, tag=tag, align_bytes=64)
-            src = z1[key[1:]] if key[0] == "z1" else loaded[key]
+                grouped[key] = work_tile(key, [P, 512, 4], BF16, newest)
+            src = z[key[1:]] if key[0] == "z1" else loaded[key]
             if engine == "gpsimd":
                 nc.gpsimd.tensor_scalar(
                     out=grouped[key][:, cols, :],
@@ -153,8 +170,11 @@ def tile_teacher_student_logits_t1_kernel(
                     grouped[key][:, cols, :].rearrange("p (n i) t -> p n t i", i=4),
                     src[:, :, cols].rearrange("p t (n i) -> p n t i", i=4),
                 )
+            done_cols[key] = done_cols.get(key, 0) + stop - start
+            if done_cols[key] == 512 and key[0] != "z1":
+                release(key)
 
-        depth = {"c512": 9, "w512": 2, "z1512": 4, "t256": 4, "t512": 4, "a512": 4, "z2256": 3}
+        depth = {"c512": 6, "w512": 2, "z1512": 4, "t256": 4, "t512": 4, "a512": 4, "z2256": 4, "z2512": 1}
 
         def quantise(*keys):
             for key in keys:
@@ -171,36 +191,41 @@ def tile_teacher_student_logits_t1_kernel(
                     scales=scales[key][:],
                     in_=grouped[key][:].rearrange("p n t -> p (n t)"),
                 )
-                if key in group_of:
-                    free_groups.append(group_of[key])
+                free_work.append(place_of[key])
 
-        def sort_block(engine, key):
-            ordered = ring("result", 4, [P, 4, 2, P], F32)
-            copy_on(engine, ordered[:], loaded[key].rearrange("p a (c m u) -> p (a c) u m", c=2, u=2))
-            for c in range(2):
-                sorted_words[key + (c,)] = ordered[:, c:4:2]
+        def z_tile(h, g):
+            tag = "z" + str(h) + str(g)
+            return sbuf.tile([P, 4, 512], F32, name=tag, tag=tag, align_bytes=64)
 
-        def turn(bank_numbers, *keys):
+        def sort_words(engine, key, h, g):
+            n = loaded[key].shape[2] // 256
+            tag = "z" + str(h) + str(g)
+            ordered = sbuf.tile([P, 2 * n, 2, P], F32, name=tag, tag=tag, align_bytes=64)
+            copy_on(engine, ordered[:], loaded[key].rearrange("p a (c m u) -> p (a c) u m", c=n, u=2))
+            for c in range(n):
+                sorted_words[key + (c,)] = ordered[:, c : 2 * n : n]
+
+        def turn(*keys):
             run = (keys[0][0], "run", *keys)
             parts[run] = keys
-            for n, key in enumerate(keys):
-                take_bank(key, [P, 2, 2, P], bank_numbers[n])
+            for key in keys:
+                take_bank(key, [P, 2, 2, P])
                 for a in range(2):
                     for u in range(2):
                         src = sorted_words[key][:, a, u] if key in sorted_words else words[key][:, a, u:256:2]
                         nc.tensor.transpose(banks[key][:, a, u, :], src, ident[:])
             return run
 
-        def fetch(run, engines=("scalar", "scalar"), held=None):
+        def fetch(run, engines=("scalar", "scalar")):
             keys = parts[run]
-            shape = [P, 256 * len(keys), 4]
-            grouped[run] = ring("turned", TURNED, shape, BF16) if held is None else held_slot(held, "held_turned", shape, BF16)
+            grouped[run] = work_tile(run, [P, 256 * len(keys), 4], BF16)
             for n, key in enumerate(keys):
                 copy_on(
                     engines[n],
                     grouped[run][:, 256 * n : 256 * (n + 1), :].bitcast(F32).rearrange("p (a r) u -> p a r u", a=2),
                     banks[key][:].rearrange("p a u r -> p a r u"),
                 )
+                give_bank(key)
             return run
 
         def product(bank, left, cols, right, start, stop):
@@ -217,116 +242,129 @@ def tile_teacher_student_logits_t1_kernel(
         def pair(s):
             return s // 4, s // 2 % 2, s % 2
 
-        def passes(name, s, which, total, left, right, first_bank):
+        def passes(name, s, which, total, left, right, tiles):
             h, g, q = pair(s)
-            for c in which:
-                for a in (1, 0):
+            for a in reversed(tiles):
+                for c in which:
                     n = counts.get((name, s, a), 0)
                     counts[name, s, a] = n + 1
                     if n == 0:
-                        take_bank((name, s, a), [P, 512], first_bank + a)
+                        take_bank((name, s, a), [P, 512])
                     product(banks[name, s, a], (left, g, q, c), slice(a * P, (a + 1) * P), (right, h, c), n == 0, n == total - 1)
 
-        def mm1(s, which=(0, 1, 2)):
-            passes("z1", s, which, 3, "t", "c", {1: 2, 2: 2, 3: 6, 5: 6}.get(s, 0))
+        def mm1(s, which=(0, 1, 2), tiles=(0, 1)):
+            passes("z1", s, which, 3, "t", "c", tiles)
 
-        def add1(s):
+        def add1(s, tiles=(0, 1)):
             h, g, q = pair(s)
-            if (h, g) not in z1:
-                z1[h, g] = ring("z1", 4, [P, 4, 512], F32)
-            for a in (0, 1):
+            if (h, g) not in z:
+                z[h, g] = z_tile(h, g)
+            for a in tiles:
                 t = 2 * q + a
                 nc.vector.tensor_tensor(
-                    out=z1[h, g][:, t, :].rearrange("p (u m e) -> p m u e", u=2, e=2),
+                    out=z[h, g][:, t, :].rearrange("p (u m e) -> p m u e", u=2, e=2),
                     in0=banks["z1", s, a][:].rearrange("p (m u e) -> p m u e", u=2, e=2),
                     in1=loaded["s", h, g][:, t, :].rearrange("p (m u e) -> p m u e", u=2, e=2),
                     op=ADD,
                 )
+                give_bank(("z1", s, a))
+                if t == 3:
+                    release(("s", h, g))
 
-        def mm2(s, which=(0, 1)):
-            passes("z2", s, which, 2, "a", "z1", 2 * (s % 2) if s >= 8 else 2)
+        def mm2(s, which=(0, 1), tiles=(0, 1)):
+            passes("z2", s, which, 2, "a", "z1", tiles)
 
-        def add2(s):
+        def add2(s, tiles=(0, 1)):
             h, g, q = pair(s)
-            z2[s] = ring("z2", 3, [P, 2, 512], F32)
-            for a in (0, 1):
+            for a in tiles:
                 t = 2 * q + a
                 nc.vector.scalar_tensor_tensor(
-                    out=z2[s][:, a, :],
-                    in0=z1[h, g][:, t, :],
+                    out=z[h, g][:, t, :],
+                    in0=z[h, g][:, t, :],
                     scalar=keep_sb[:, g, t : t + 1],
                     in1=banks["z2", s, a][:],
                     op0=MULT,
                     op1=ADD,
                 )
+                give_bank(("z2", s, a))
 
-        def gain_mul(s):
-            pair_tile = held_slot(s, "gained", [P, 2, 512], F32)
+        def z2_of(s):
+            h, g, q = pair(s)
+            return z[h, g][:, 2 * q : 2 * q + 2, :]
+
+        def gain_mul(s, newest=False):
+            pair_tile = work_tile(("gained", s), [P, 2, 512], F32, newest)
             for a in range(2):
                 gained[s, a] = pair_tile[:, a, :]
             nc.gpsimd.tensor_tensor(
                 out=pair_tile[:],
-                in0=z2[s][:],
+                in0=z2_of(s),
                 in1=gain_sb[:, s // 4, :].unsqueeze(1).to_broadcast([P, 2, 512]),
                 op=MULT,
             )
 
-        def gain_mul_tile(s, a, engine, slot):
-            gained[s, a] = held_slot(slot, "gained_tile", [P, 512], F32)[:]
-            engine.tensor_tensor(out=gained[s, a], in0=z2[s][:, a, :], in1=gain_sb[:, s // 4, :], op=MULT)
+        def gain_mul_tile(s, a, engine, newest=False):
+            gained[s, a] = work_tile(("gained", s, a), [P, 512], F32, newest)[:]
+            engine.tensor_tensor(out=gained[s, a], in0=z2_of(s)[:, a, :], in1=gain_sb[:, s // 4, :], op=MULT)
 
         def round2(s):
-            rounded = ring("rounded", 2, [P, 2, 512], BF16)
-            nc.scalar.copy(out=rounded[:], in_=z2[s][:])
+            rounded = ring("rounded", 3, [P, 2, 512], BF16)
+            nc.scalar.copy(out=rounded[:], in_=z2_of(s))
             sorted_words["z2", s] = rounded[:].bitcast(F32).rearrange("p a (u m) -> p a u m", u=2)
 
-        def turn2(s):
-            bank = take_bank(("z2t", s), [P, 2, 2, P], 6 + s % 2)
-            for a in range(2):
-                for u in range(2):
-                    nc.tensor.transpose(bank[:, a, u, :], sorted_words["z2", s][:, a, u], ident[:])
-
-        def fetch2(s):
-            grouped["z2", s] = held_slot(s + 1, "z2turned", [P, 2 * P, 4], BF16)
-            nc.scalar.copy(
-                out=grouped["z2", s][:].bitcast(F32).rearrange("p (a r) u -> p a r u", a=2),
-                in_=banks["z2t", s][:].rearrange("p a u r -> p a r u"),
-            )
+        def turn2(*pairs):
+            return turn(*[("z2", s) for s in pairs])
 
         def turn2_unrounded(s):
-            grouped["z2", s] = held_slot(s + 1, "z2turned", [P, 2 * P, 4], BF16)
+            grouped["z2", s] = work_tile(("z2", s), [P, 2 * P, 4], BF16)
             for a in (0, 1):
-                bank = take_bank(("z2t", s, a), [P, 4, P], a)
+                bank = take_bank(("z2t", s, a), [P, 4, P])
                 for t in range(4):
                     start = t // 2 * 256 + t % 2
-                    nc.tensor.transpose(bank[:, t, :], z2[s][:, a, start : t // 2 * 256 + 256 : 2], ident[:])
+                    nc.tensor.transpose(bank[:, t, :], z2_of(s)[:, a, start : t // 2 * 256 + 256 : 2], ident[:])
                 nc.scalar.copy(
                     out=grouped["z2", s][:, a * P : (a + 1) * P, :], in_=bank[:].rearrange("p t n -> p n t")
                 )
+                give_bank(("z2t", s, a))
+            return ("z2", s)
 
-        def mm3(s):
-            for a in (1, 0):
-                take_bank(("out", s, a), [P, 512], (2 if s == 11 else 4) + a)
+        def mm3(*tiles):
+            for s, a in reversed([divmod(i, 2) for i in tiles]):
+                take_bank(("out", s, a), [P, 512])
                 product(banks["out", s, a], ("z2", s), slice(a * P, (a + 1) * P), ("w", s // 4), True, True)
 
-        def add3(s, tiles=(0, 1)):
-            if s not in result:
-                result[s] = ring("result", 4, [P, 2, 512], F32)
-            for a in tiles:
+        def add3(*tiles, single=False):
+            for s, a in [divmod(i, 2) for i in tiles]:
+                if s not in result:
+                    result[s] = ring("result", 4, [P, 2, 512], F32)
                 nc.vector.tensor_tensor(
                     out=result[s][:, a, :].rearrange("p (m u e) -> p m u e", u=2, e=2),
                     in0=banks["out", s, a][:].rearrange("p (m u e) -> p m u e", u=2, e=2),
                     in1=gained[s, a].rearrange("p (u m e) -> p m u e", u=2, e=2),
                     op=ADD,
                 )
-            h, g, q = pair(s)
-            rows = slice(min(tiles), max(tiles) + 1)
-            nc.sync.dma_start(
-                out=out_v[g, :, 2 * q + rows.start : 2 * q + rows.stop, h * 512 : (h + 1) * 512], in_=result[s][:, rows, :]
-            )
+                give_bank(("out", s, a))
+                counts["added", s] = counts.get(("added", s), 0) + 1
+                if counts["added", s] == 2 and ("gained", s) in place_of:
+                    free_work.append(place_of["gained", s])
+                if single or counts["added", s] == 2:
+                    h, g, q = pair(s)
+                    rows = slice(a, a + 1) if single else slice(0, 2)
+                    nc.sync.dma_start(
+                        out=out_v[g, :, 2 * q + rows.start : 2 * q + rows.stop, h * 512 : (h + 1) * 512],
+                        in_=result[s][:, rows, :],
+                    )
+
+        def turn_affinity(n):
+            run = turn(("a", n // 2, n % 2, 0), ("a", n // 2, n % 2, 1))
+            release(("a", n // 2, n % 2))
+            return run
 
         nc.sync.dma_start(out=gain_in[:], in_=gain.rearrange("(h p j) -> p h j", p=P, j=4))
-        load(("c", 0, 0), ("t", 0, 0), ("c", 0, 1), ("t", 0, 1), ("c", 0, 2), ("c", 1, 0), ("s", 0, 0), ("c", 1, 1), ("t", 1, 0), ("t", 1, 1))
+        pending.extend([("c", 0, 0), ("t", 0, 0), ("c", 0, 1), ("t", 0, 1), ("c", 0, 2), ("c", 1, 0), ("s", 0, 0), ("c", 1, 1), ("t", 1, 0), ("t", 1, 1)])
+        pending.extend([("s", 0, 1), ("c", 1, 2), ("a", 0, 0), ("c", 2, 0), ("s", 1, 0), ("keep",), ("a", 0, 1), ("w", 0), ("a", 1, 0), ("c", 2, 1)])
+        pending.extend([("s", 1, 1), ("a", 1, 1), ("c", 2, 2), ("s", 2, 0), ("w", 1), ("s", 2, 1), ("w", 2)])
+        load_more()
         make_identity(nc, ident[:])
         nc.scalar.copy(out=gain_f32[:], in_=gain_in[:])
         for h in range(G):
@@ -334,27 +372,20 @@ def tile_teacher_student_logits_t1_kernel(
         for h in range(G):
             fetch_gain(h)
 
-        def turn_teacher(g, q, bank_numbers, held=None):
-            first = fetch(turn(bank_numbers[:2], ("t", g, q, 0), ("t", g, q, 1)))
-            return first, fetch(turn(bank_numbers[2:], ("t", g, q, 2)), held=held)
-
-        def turn_affinity(s, bank_numbers):
-            return turn(bank_numbers, ("a", s // 2, s % 2, 0), ("a", s // 2, s % 2, 1))
+        def turn_teacher(g, q):
+            first = fetch(turn(("t", g, q, 0), ("t", g, q, 1)))
+            return first, fetch(turn(("t", g, q, 2)))
 
         interleave("vector", ("c", 0, 0))
-        runs = turn_teacher(0, 0, (2, 3, 4))
+        runs = turn_teacher(0, 0)
         quantise(("c", 0, 0))
-        load(("s", 0, 1), ("c", 1, 2))
         interleave("vector", ("c", 0, 1))
         quantise(runs[0], ("c", 0, 1), runs[1])
-        runs = turn_teacher(0, 1, (5, 6, 7))
+        runs = turn_teacher(0, 1)
         mm1(0, (0, 1))
         interleave("vector", ("c", 0, 2))
-        load(("a", 0, 0), ("c", 2, 0))
         quantise(runs[0], ("c", 0, 2))
         mm1(0, (2,))
-        load(("s", 1, 0))
-        nc.sync.dma_start(out=keep_sb[:], in_=keep.rearrange("(g p t) -> p g t", p=P, t=4))
         quantise(runs[1])
         mm1(1)
         interleave("scalar", ("c", 1, 0))
@@ -362,107 +393,108 @@ def tile_teacher_student_logits_t1_kernel(
         add1(0)
         quantise(("c", 1, 0))
         add1(1)
-        load(("a", 0, 1), ("w", 0), ("a", 1, 0))
-        runs = turn_teacher(1, 0, (4, 5, 6))
-        later = turn_teacher(1, 1, (7, 0, 1), held=1)
-        load(("c", 2, 1), ("s", 1, 1))
+        runs = turn_teacher(1, 0)
+        later = turn_teacher(1, 1)
+        free_loads.extend(range(6))
+        load_more()
         interleave("scalar", ("c", 1, 2))
         interleave("vector", ("z1", 0, 0))
         quantise(*runs)
         mm1(2)
         quantise(later[0], ("c", 1, 1), ("z1", 0, 0), later[1])
         mm1(3)
-        interleave("gpsimd", ("c", 2, 0), 208, 512, held=1)
+        interleave("gpsimd", ("c", 2, 0), 208, 512, True)
         interleave("scalar", ("c", 2, 0), 0, 208)
-        load(("a", 1, 1))
-        a_run = {0: fetch(turn_affinity(0, (4, 5)))}
+        a0 = fetch(turn_affinity(0))
         mm1(4, (0, 1))
         add1(2)
-        a_run[1] = turn_affinity(1, (4, 5))
+        a1 = turn_affinity(1)
         add1(3)
-        load(("c", 2, 2), ("s", 2, 0))
         quantise(("c", 1, 2))
         mm1(4, (2,))
         interleave("vector", ("z1", 0, 1), 0, 320)
         interleave("scalar", ("z1", 0, 1), 320, 512)
-        fetch(a_run[1], held=0)
+        fetch(a1)
         interleave("scalar", ("w", 0))
-        quantise(a_run[0])
+        quantise(a0)
         mm2(0, (0,))
         quantise(("z1", 0, 1))
         mm2(0, (1,))
-        a_run[2] = turn_affinity(2, (4, 5))
-        mm1(5)
-        quantise(("c", 2, 0), a_run[1])
-        load(("w", 1), ("s", 2, 1))
-
-        interleave("gpsimd", ("c", 2, 1), 208, 512, held=0)
-        fetch(a_run[2])
+        a2 = turn_affinity(2)
+        quantise(("c", 2, 0), a1)
+        a3 = turn_affinity(3)
+        interleave("gpsimd", ("c", 2, 1), 208, 512, True)
+        fetch(a2)
+        fetch(a3)
         interleave("scalar", ("c", 2, 1), 0, 208)
         add1(4)
+        mm1(5)
         add2(0)
         round2(0)
         mm2(1)
         mm1(6)
-        interleave("scalar", ("c", 2, 2), 0, 320)
-        load(("w", 2))
-        quantise(("w", 0), a_run[2], ("c", 2, 1))
-        gain_mul(0)
+        interleave("scalar", ("c", 2, 2))
+        quantise(("w", 0), a2, a3, ("c", 2, 1))
+        gain_mul(0, True)
         add1(5)
-        turn2(0)
-        a_run[3] = turn_affinity(3, (4, 5))
-        fetch2(0)
-        fetch(a_run[3])
-        add2(1)
-        round2(1)
-        mm2(2)
-        interleave("scalar", ("c", 2, 2), 320, 512)
+        z0 = fetch(turn2(0))
         interleave("scalar", ("z1", 1, 0))
+        add2(1)
+        mm2(2)
         add1(6)
         mm1(7)
-        quantise(a_run[3], ("z2", 0))
+        quantise(z0)
 
+        turn_banks.extend([free_banks.pop(), free_banks.pop()])
         first_pair = {s: s + 5 for s in range(2, 7)}
-        interleaved = {2: [("z1", 1, 1)], 3: [("w", 1)], 4: [("z1", 2, 0)], 5: [("w", 2)], 6: [("z1", 2, 1)]}
-        quantised = {2: [("c", 2, 2), ("z1", 1, 0)], 3: [("z1", 1, 1)], 4: [("w", 1)], 5: [("z1", 2, 0)], 7: [("z1", 2, 1), ("w", 2)]}
+        interleaved = {2: [("z1", 1, 1)], 3: [("w", 1)], 4: [("z1", 2, 0)], 6: [("z1", 2, 1)], 8: [("w", 2)]}
+        quantised = {2: [("c", 2, 2), ("z1", 1, 0)], 3: [("z1", 1, 1)], 5: [("z1", 2, 0)], 6: [("w", 1)], 7: [("z1", 2, 1)], 9: [("w", 2)]}
+        rounds = {2: (1,), 3: (2,), 4: (3,), 5: (4, 5), 7: (6, 7), 8: (8,), 9: (9,), 10: (10,)}
+        last_tiles = {s: (s - 2,) if s < 7 else (3 * s - 16, 3 * s - 15, 3 * s - 14) for s in range(2, 12)}
+        turned = {3: (1,), 4: (2,), 5: (3,), 6: (4,), 7: (5,), 8: (6, 7), 9: (8,), 10: (9,), 11: (10,)}
         for s in range(2, 12):
-            early = s in (4, 5, 6)
-            gain_mul(s - 1)
-            mm3(s - 2)
-            turn2(s - 1)
-            fetch2(s - 1)
-            if early:
+            gain_mul(s - 1, True)
+            run = []
+            mm3(*[i for i in last_tiles[s] if ("out", i // 2, i % 2) not in banks])
+            if s in turned:
+                run = [fetch(turn2(*turned[s]))]
+            for k in rounds.get(s, ()):
+                if k < s:
+                    round2(k)
+            if s in first_pair and s > 3:
                 add1(first_pair[s])
                 if s < 6:
                     mm1(first_pair[s] + 1)
             add2(s)
-            if s < 11:
-                round2(s)
+            if s == 3:
+                add1(8)
+                mm1(9)
+            if s == 2:
+                add1(7)
+                mm1(8, (0, 1))
             if s in (3, 7):
                 mm2(s + 1, (0,))
             elif s < 11:
                 mm2(s + 1)
-            if s == 2:
-                add1(7)
-                mm1(8, (0, 1))
+            if s in rounds.get(s, ()):
+                round2(s)
             for key in interleaved.get(s, []):
                 interleave("scalar", key)
-            if s == 3:
-                add1(8)
-                mm1(9)
-            add3(s - 2)
+            add3(*last_tiles[s])
+            if s < 11:
+                mm3(*[i for i in last_tiles[s + 1] if ("z2", i // 2) in codes and ("w", i // 8) in codes])
             for key in quantised.get(s, []):
                 quantise(key)
                 if key == ("c", 2, 2):
                     mm1(8, (2,))
                 if key in (("z1", 1, 1), ("z1", 2, 1)):
                     mm2(s + 1, (1,))
-            quantise(("z2", s - 1))
-        turn2_unrounded(11)
-        mm3(10)
-        gain_mul_tile(11, 1, nc.vector, 11)
-        quantise(("z2", 11))
-        gain_mul_tile(11, 0, nc.gpsimd, 12)
-        mm3(11)
-        for s, a in ((10, 0), (10, 1), (11, 1), (11, 0)):
-            add3(s, (a,))
+            quantise(*run)
+        last = turn2_unrounded(11)
+        mm3(20, 21)
+        gain_mul_tile(11, 1, nc.vector)
+        quantise(last)
+        gain_mul_tile(11, 0, nc.gpsimd, True)
+        mm3(22, 23)
+        for i in (20, 21, 23, 22):
+            add3(i, single=True)

@@ -17,9 +17,16 @@ ADD = mybir.AluOpType.add
 
 KIB = 1024
 PLACE = 4 * KIB
-LOAD_PLACES = 7
+LOAD_PLACES = 13
 WORK_PLACES = 12
-PAIR_BYTES = 6 * KIB
+LOADS = {
+    ("c", 0, 1, 0): 0, ("t", 0, 0): 4, ("c", 0, 1, 1): 10, ("t", 0, 1): 14, ("c", 0, 1, 2): 20,
+    ("c", 1, 1, 0): 24, ("s", 0, 1, 0): 28, ("c", 1, 1, 1): 32, ("t", 1, 0): 36, ("t", 1, 1): 42,
+    ("s", 0, 1, 1): 48, ("c", 1, 1, 2): 0, ("a", 0, 0): 4, ("c", 2, 1, 0): 10, ("s", 1, 1, 0): 14,
+    ("keep",): 0, ("a", 0, 1): 20, ("w", 0): 24, ("a", 1, 0): 28, ("c", 2, 1, 1): 32,
+    ("s", 1, 1, 1): 36, ("a", 1, 1): 42, ("c", 2, 1, 2): 0, ("s", 2, 1, 0): 4, ("w", 1): 10,
+    ("s", 2, 1, 1): 20, ("w", 2): 48,
+}
 
 
 def tile_teacher_student_logits_t1_kernel(
@@ -38,8 +45,7 @@ def tile_teacher_student_logits_t1_kernel(
         free_banks = list(range(8))
         turn_banks = []
         list_of = {}
-        free_loads = list(range(6, 6 + LOAD_PLACES))
-        free_work = list(range(6 + LOAD_PLACES, 6 + LOAD_PLACES + WORK_PLACES))
+        free_work = list(range(LOAD_PLACES, LOAD_PLACES + WORK_PLACES))
         place_of = {}
 
         def label(key):
@@ -90,15 +96,15 @@ def tile_teacher_student_logits_t1_kernel(
 
         def load(key):
             name = "raw_" + label(key)
-            if key[0] == "t":
-                place = (2 * key[1] + key[2]) * PAIR_BYTES
-            else:
-                place_of["load", key] = free_loads.pop(0)
-                place = place_of["load", key] * PLACE
+            place = LOADS[key] * KIB
             if key[0] in ("c", "s"):
                 source = confusion_v if key[0] == "c" else student_v
-                loaded[key] = placed(name, place, [P, 4, 512], BF16)[:]
-                nc.sync.dma_start(out=loaded[key], in_=source[key[2], :, :, key[1] * 512 : (key[1] + 1) * 512])
+                first, count, n = key[1:]
+                t = placed(name, place, [P, 4, 512 * count], BF16)
+                nc.sync.dma_start(out=t[:], in_=source[n, :, :, first * 512 : (first + count) * 512])
+                for h in range(count):
+                    loaded[key[0], first + h, n] = t[:, :, h * 512 : (h + 1) * 512]
+                    load_of[key[0], first + h, n] = key
             if key[0] in ("t", "a"):
                 g, q = key[1:]
                 source = teacher_v if key[0] == "t" else affinity_v
@@ -113,36 +119,51 @@ def tile_teacher_student_logits_t1_kernel(
                 nc.sync.dma_start(out=t[:], in_=within_v[key[1]].rearrange("p j n -> p (j n)"))
                 loaded[key] = t[:].rearrange("p (j n) -> p j n", j=4)
             if key[0] == "keep":
-                nc.sync.dma_start(out=keep_sb[:], in_=keep.rearrange("(g p t) -> p g t", p=P, t=4))
-                free_loads.insert(0, place_of["load", key])
+                nc.sync.dma_start(out=keep_sb[:, :, 0:4], in_=keep.rearrange("(g p t) -> p g t", p=P, t=4))
 
-        pending = []
+        def kib(key):
+            return {"t": 6, "keep": 0}.get(key[0], 4 * key[2] if len(key) == 4 else 4)
+
+        pending = list(LOADS)
+        unread = {}
+        load_of = {}
 
         def load_more():
-            while pending and (pending[0][0] == "t" or free_loads):
+            while pending:
+                key = pending[0]
+                if any(LOADS[k] < LOADS[key] + kib(key) and LOADS[key] < LOADS[k] + kib(k) for k in unread):
+                    return
                 load(pending.pop(0))
+                if kib(key):
+                    unread[key] = key[2] if len(key) == 4 else 1
 
         def release(key):
-            free_loads.append(place_of["load", key])
-            load_more()
+            key = load_of.get(key, key)
+            unread[key] = unread[key] - 1
+            if unread[key] == 0:
+                unread.pop(key)
+                load_more()
 
         ident = sbuf.tile([P, P], F32, name="ident", tag="ident")
-        keep_sb = sbuf.tile([P, 2, 4], BF16, name="keep_sb", tag="keep_sb")
-        gain_in = sbuf.tile([P, G, 4], BF16, name="gain_in", tag="gain_in")
-        gain_f32 = sbuf.tile([P, G, 4], F32, name="gain_f32", tag="gain_f32")
-        gain_sb = sbuf.tile([P, G, 512], BF16, name="gain_sb", tag="gain_sb", align_bytes=64)
+        keep_sb = sbuf.tile([P, 2, 16], BF16, name="keep_sb", tag="keep_sb")
+        gain_in = sbuf.tile([P, 12], BF16, name="gain_in", tag="gain_in")
+        gain_sb = sbuf.tile([P, 2, 768], BF16, name="gain_sb", tag="gain_sb", align_bytes=64)
 
-        def spread_gain(h):
-            bank = take_bank(("gain", h), [P, 4, P])
-            for j in range(4):
-                nc.tensor.transpose(bank[:, j, :], gain_f32[:, h, j : j + 1].to_broadcast([P, P]), ident[:])
+        def spread_gain(u):
+            bank = take_bank(("gain", u), [P, 3, P])
+            for j in range(3):
+                word = gain_in[:].bitcast(F32)[:, 2 * j + u : 2 * j + u + 1]
+                nc.tensor.transpose(bank[:, j, :], word.to_broadcast([P, P]), ident[:])
 
-        def fetch_gain(h):
+        def fetch_gain(u):
             nc.scalar.copy(
-                out=gain_sb[:, h, :].rearrange("p (u m e) -> p u m e", u=2, e=2),
-                in_=banks["gain", h][:].rearrange("p (u e) m -> p u m e", u=2),
+                out=gain_sb[:, u, :].bitcast(F32).rearrange("p (n j) -> p n j", j=3),
+                in_=banks["gain", u][:].rearrange("p j n -> p n j"),
             )
-            give_bank(("gain", h))
+            give_bank(("gain", u))
+
+        def gain_of(h):
+            return gain_sb[:, :, 256 * h : 256 * (h + 1)]
 
         def copy_on(engine, o, s):
             if engine == "vector":
@@ -297,15 +318,20 @@ def tile_teacher_student_logits_t1_kernel(
             for a in range(2):
                 gained[s, a] = pair_tile[:, a, :]
             nc.gpsimd.tensor_tensor(
-                out=pair_tile[:],
-                in0=z2_of(s),
-                in1=gain_sb[:, s // 4, :].unsqueeze(1).to_broadcast([P, 2, 512]),
+                out=pair_tile[:].rearrange("p a (u n) -> p a u n", u=2),
+                in0=z2_of(s).rearrange("p a (u n) -> p a u n", u=2),
+                in1=gain_of(s // 4).unsqueeze(1).to_broadcast([P, 2, 2, 256]),
                 op=MULT,
             )
 
         def gain_mul_tile(s, a, engine, newest=False):
             gained[s, a] = work_tile(("gained", s, a), [P, 512], F32, newest)[:]
-            engine.tensor_tensor(out=gained[s, a], in0=z2_of(s)[:, a, :], in1=gain_sb[:, s // 4, :], op=MULT)
+            engine.tensor_tensor(
+                out=gained[s, a].rearrange("p (u n) -> p u n", u=2),
+                in0=z2_of(s)[:, a, :].rearrange("p (u n) -> p u n", u=2),
+                in1=gain_of(s // 4),
+                op=MULT,
+            )
 
         def round2(s):
             rounded = ring("rounded", 3, [P, 2, 512], BF16)
@@ -360,21 +386,19 @@ def tile_teacher_student_logits_t1_kernel(
             release(("a", n // 2, n % 2))
             return run
 
-        nc.sync.dma_start(out=gain_in[:], in_=gain.rearrange("(h p j) -> p h j", p=P, j=4))
-        pending.extend([("c", 0, 0), ("t", 0, 0), ("c", 0, 1), ("t", 0, 1), ("c", 0, 2), ("c", 1, 0), ("s", 0, 0), ("c", 1, 1), ("t", 1, 0), ("t", 1, 1)])
-        pending.extend([("s", 0, 1), ("c", 1, 2), ("a", 0, 0), ("c", 2, 0), ("s", 1, 0), ("keep",), ("a", 0, 1), ("w", 0), ("a", 1, 0), ("c", 2, 1)])
-        pending.extend([("s", 1, 1), ("a", 1, 1), ("c", 2, 2), ("s", 2, 0), ("w", 1), ("s", 2, 1), ("w", 2)])
+        nc.sync.dma_start(out=gain_in[:], in_=gain.rearrange("(n i) -> n i", i=12))
         load_more()
         make_identity(nc, ident[:])
-        nc.scalar.copy(out=gain_f32[:], in_=gain_in[:])
-        for h in range(G):
-            spread_gain(h)
-        for h in range(G):
-            fetch_gain(h)
+        for u in range(2):
+            spread_gain(u)
+        for u in range(2):
+            fetch_gain(u)
 
         def turn_teacher(g, q):
             first = fetch(turn(("t", g, q, 0), ("t", g, q, 1)))
-            return first, fetch(turn(("t", g, q, 2)))
+            second = fetch(turn(("t", g, q, 2)))
+            release(("t", g, q))
+            return first, second
 
         interleave("vector", ("c", 0, 0))
         runs = turn_teacher(0, 0)
@@ -395,8 +419,6 @@ def tile_teacher_student_logits_t1_kernel(
         add1(1)
         runs = turn_teacher(1, 0)
         later = turn_teacher(1, 1)
-        free_loads.extend(range(6))
-        load_more()
         interleave("scalar", ("c", 1, 2))
         interleave("vector", ("z1", 0, 0))
         quantise(*runs)
@@ -422,28 +444,29 @@ def tile_teacher_student_logits_t1_kernel(
         mm2(0, (1,))
         a2 = turn_affinity(2)
         quantise(("c", 2, 0), a1)
-        a3 = turn_affinity(3)
+        mm1(5)
         interleave("gpsimd", ("c", 2, 1), 208, 512, True)
         fetch(a2)
-        fetch(a3)
         interleave("scalar", ("c", 2, 1), 0, 208)
         add1(4)
-        mm1(5)
         add2(0)
         round2(0)
         mm2(1)
         mm1(6)
-        interleave("scalar", ("c", 2, 2))
-        quantise(("w", 0), a2, a3, ("c", 2, 1))
+        interleave("scalar", ("c", 2, 2), 320, 512)
+        quantise(("w", 0), a2, ("c", 2, 1))
         gain_mul(0, True)
         add1(5)
-        z0 = fetch(turn2(0))
+        z0 = turn2(0)
+        a3 = fetch(turn_affinity(3))
+        fetch(z0)
         interleave("scalar", ("z1", 1, 0))
         add2(1)
         mm2(2)
+        interleave("scalar", ("c", 2, 2), 0, 320)
         add1(6)
         mm1(7)
-        quantise(z0)
+        quantise(a3, z0)
 
         turn_banks.extend([free_banks.pop(), free_banks.pop()])
         first_pair = {s: s + 5 for s in range(2, 7)}
@@ -465,6 +488,9 @@ def tile_teacher_student_logits_t1_kernel(
                 add1(first_pair[s])
                 if s < 6:
                     mm1(first_pair[s] + 1)
+            tiles = list(last_tiles[s])
+            if s == 8:
+                add3(tiles.pop(0), tiles.pop(0))
             add2(s)
             if s == 3:
                 add1(8)
@@ -480,7 +506,7 @@ def tile_teacher_student_logits_t1_kernel(
                 round2(s)
             for key in interleaved.get(s, []):
                 interleave("scalar", key)
-            add3(*last_tiles[s])
+            add3(*tiles)
             if s < 11:
                 mm3(*[i for i in last_tiles[s + 1] if ("z2", i // 2) in codes and ("w", i // 8) in codes])
             for key in quantised.get(s, []):

@@ -24,7 +24,7 @@ LOADS = {
     ("c", 1, 1, 0): 24, ("s", 0, 1, 0): 28, ("c", 1, 1, 1): 32, ("t", 1, 0): 36, ("t", 1, 1): 42,
     ("s", 0, 1, 1): 48, ("c", 1, 1, 2): 0, ("a", 0, 0): 4, ("c", 2, 1, 0): 10, ("s", 1, 1, 0): 14,
     ("keep",): 0, ("a", 0, 1): 20, ("w", 0): 24, ("a", 1, 0): 28, ("c", 2, 1, 1): 32,
-    ("s", 1, 1, 1): 36, ("a", 1, 1): 42, ("c", 2, 1, 2): 0, ("s", 2, 1, 0): 4, ("w", 1): 10,
+    ("s", 1, 1, 1): 36, ("c", 2, 1, 2): 0, ("a", 1, 1): 42, ("s", 2, 1, 0): 4, ("w", 1): 10,
     ("s", 2, 1, 1): 20, ("w", 2): 48,
 }
 
@@ -65,7 +65,7 @@ def tile_teacher_student_logits_t1_kernel(
             return placed("work_" + label(key), place_of[key] * PLACE, shape, dtype)
 
         def take_bank(key, shape):
-            free = turn_banks if key[0] in ("a", "z2") and len(key) != 3 and turn_banks else free_banks
+            free = turn_banks if turn_banks and (key[0] in ("a", "z2t") or len(key) == 2) else free_banks
             bank_of[key] = free.pop(0)
             list_of[key] = free
             tag = "bank" + str(bank_of[key])
@@ -91,7 +91,6 @@ def tile_teacher_student_logits_t1_kernel(
         codes = {}
         scales = {}
         z = {}
-        result = {}
         gained = {}
 
         def load(key):
@@ -195,7 +194,7 @@ def tile_teacher_student_logits_t1_kernel(
             if done_cols[key] == 512 and key[0] != "z1":
                 release(key)
 
-        depth = {"c512": 6, "w512": 2, "z1512": 4, "t256": 4, "t512": 4, "a512": 4, "z2256": 4, "z2512": 1}
+        depth = {"c512": 6, "w512": 3, "z1512": 6, "t256": 4, "t512": 4, "a512": 4, "z2256": 11, "z2512": 2}
 
         def quantise(*keys):
             for key in keys:
@@ -361,10 +360,8 @@ def tile_teacher_student_logits_t1_kernel(
 
         def add3(*tiles, single=False):
             for s, a in [divmod(i, 2) for i in tiles]:
-                if s not in result:
-                    result[s] = ring("result", 4, [P, 2, 512], F32)
                 nc.vector.tensor_tensor(
-                    out=result[s][:, a, :].rearrange("p (m u e) -> p m u e", u=2, e=2),
+                    out=z2_of(s)[:, a, :].rearrange("p (m u e) -> p m u e", u=2, e=2),
                     in0=banks["out", s, a][:].rearrange("p (m u e) -> p m u e", u=2, e=2),
                     in1=gained[s, a].rearrange("p (u m e) -> p m u e", u=2, e=2),
                     op=ADD,
@@ -378,7 +375,7 @@ def tile_teacher_student_logits_t1_kernel(
                     rows = slice(a, a + 1) if single else slice(0, 2)
                     nc.sync.dma_start(
                         out=out_v[g, :, 2 * q + rows.start : 2 * q + rows.stop, h * 512 : (h + 1) * 512],
-                        in_=result[s][:, rows, :],
+                        in_=z2_of(s)[:, rows, :],
                     )
 
         def turn_affinity(n):
@@ -451,27 +448,25 @@ def tile_teacher_student_logits_t1_kernel(
         add1(4)
         add2(0)
         round2(0)
+        interleave("scalar", ("c", 2, 2))
         mm2(1)
         mm1(6)
-        interleave("scalar", ("c", 2, 2), 320, 512)
         quantise(("w", 0), a2, ("c", 2, 1))
         gain_mul(0, True)
         add1(5)
-        z0 = turn2(0)
-        a3 = fetch(turn_affinity(3))
-        fetch(z0)
+        z0 = fetch(turn2(0))
         interleave("scalar", ("z1", 1, 0))
         add2(1)
         mm2(2)
-        interleave("scalar", ("c", 2, 2), 0, 320)
         add1(6)
         mm1(7)
-        quantise(a3, z0)
+        a3 = fetch(turn_affinity(3))
+        quantise(z0)
 
         turn_banks.extend([free_banks.pop(), free_banks.pop()])
         first_pair = {s: s + 5 for s in range(2, 7)}
         interleaved = {2: [("z1", 1, 1)], 3: [("w", 1)], 4: [("z1", 2, 0)], 6: [("z1", 2, 1)], 8: [("w", 2)]}
-        quantised = {2: [("c", 2, 2), ("z1", 1, 0)], 3: [("z1", 1, 1)], 5: [("z1", 2, 0)], 6: [("w", 1)], 7: [("z1", 2, 1)], 9: [("w", 2)]}
+        quantised = {2: [a3, ("c", 2, 2), ("z1", 1, 0)], 3: [("z1", 1, 1)], 5: [("z1", 2, 0)], 6: [("w", 1)], 7: [("z1", 2, 1)], 9: [("w", 2)]}
         rounds = {2: (1,), 3: (2,), 4: (3,), 5: (4, 5), 7: (6, 7), 8: (8,), 9: (9,), 10: (10,)}
         last_tiles = {s: (s - 2,) if s < 7 else (3 * s - 16, 3 * s - 15, 3 * s - 14) for s in range(2, 12)}
         turned = {3: (1,), 4: (2,), 5: (3,), 6: (4,), 7: (5,), 8: (6, 7), 9: (8,), 10: (9,), 11: (10,)}
@@ -484,11 +479,13 @@ def tile_teacher_student_logits_t1_kernel(
             for k in rounds.get(s, ()):
                 if k < s:
                     round2(k)
+            tiles = list(last_tiles[s])
+            if s == 3:
+                add3(tiles.pop(0))
             if s in first_pair and s > 3:
                 add1(first_pair[s])
                 if s < 6:
                     mm1(first_pair[s] + 1)
-            tiles = list(last_tiles[s])
             if s == 8:
                 add3(tiles.pop(0), tiles.pop(0))
             add2(s)
@@ -500,7 +497,7 @@ def tile_teacher_student_logits_t1_kernel(
                 mm1(8, (0, 1))
             if s in (3, 7):
                 mm2(s + 1, (0,))
-            elif s < 11:
+            elif 2 < s < 11:
                 mm2(s + 1)
             if s in rounds.get(s, ()):
                 round2(s)
@@ -511,6 +508,8 @@ def tile_teacher_student_logits_t1_kernel(
                 mm3(*[i for i in last_tiles[s + 1] if ("z2", i // 2) in codes and ("w", i // 8) in codes])
             for key in quantised.get(s, []):
                 quantise(key)
+                if key == a3:
+                    mm2(3)
                 if key == ("c", 2, 2):
                     mm1(8, (2,))
                 if key in (("z1", 1, 1), ("z1", 2, 1)):

@@ -21,10 +21,10 @@ LOAD_PLACES = 13
 WORK_PLACES = 12
 LOADS = {
     ("c", 0, 1, 0): 0, ("t", 0, 0): 4, ("c", 0, 1, 1): 10, ("t", 0, 1): 14, ("c", 0, 1, 2): 20,
-    ("c", 1, 1, 0): 24, ("s", 0, 1, 0): 28, ("c", 1, 1, 1): 32, ("t", 1, 0): 36, ("t", 1, 1): 42,
+    ("c", 1, 1, 0): 24, ("c", 1, 1, 1): 32, ("t", 1, 0): 36, ("t", 1, 1): 42, ("s", 0, 1, 0): 28,
     ("s", 0, 1, 1): 48, ("c", 1, 1, 2): 0, ("a", 0, 0): 4, ("c", 2, 1, 0): 10, ("s", 1, 1, 0): 14,
-    ("keep",): 0, ("a", 0, 1): 20, ("w", 0): 24, ("a", 1, 0): 28, ("c", 2, 1, 1): 32,
-    ("s", 1, 1, 1): 36, ("c", 2, 1, 2): 0, ("a", 1, 1): 42, ("s", 2, 1, 0): 4, ("w", 1): 10,
+    ("keep",): 0, ("a", 0, 1): 20, ("w", 0): 24, ("a", 1, 0): 32, ("c", 2, 1, 1): 36,
+    ("s", 1, 1, 1): 42, ("c", 2, 1, 2): 0, ("a", 1, 1): 28, ("s", 2, 1, 0): 4, ("w", 1): 10,
     ("s", 2, 1, 1): 20, ("w", 2): 48,
 }
 
@@ -411,17 +411,17 @@ def tile_teacher_student_logits_t1_kernel(
         mm1(1)
         interleave("scalar", ("c", 1, 0))
         interleave("scalar", ("c", 1, 1))
-        add1(0)
-        quantise(("c", 1, 0))
-        add1(1)
         runs = turn_teacher(1, 0)
         later = turn_teacher(1, 1)
-        interleave("scalar", ("c", 1, 2))
-        interleave("vector", ("z1", 0, 0))
-        quantise(*runs)
+        quantise(("c", 1, 0), ("c", 1, 1), *runs)
         mm1(2)
-        quantise(later[0], ("c", 1, 1), ("z1", 0, 0), later[1])
+        add1(0)
+        add1(1)
+        interleave("vector", ("z1", 0, 0))
+        interleave("scalar", ("c", 1, 2))
+        quantise(*later)
         mm1(3)
+        quantise(("z1", 0, 0))
         interleave("gpsimd", ("c", 2, 0), 208, 512, True)
         interleave("scalar", ("c", 2, 0), 0, 208)
         a0 = fetch(turn_affinity(0))

@@ -20,12 +20,12 @@ PLACE = 4 * KIB
 LOAD_PLACES = 13
 WORK_PLACES = 12
 LOADS = {
-    ("c", 0, 1, 0): 0, ("t", 0, 0): 4, ("c", 0, 1, 1): 10, ("t", 0, 1): 14, ("c", 0, 1, 2): 20,
-    ("c", 1, 1, 0): 24, ("c", 1, 1, 1): 32, ("t", 1, 0): 36, ("t", 1, 1): 42, ("s", 0, 1, 0): 28,
-    ("s", 0, 1, 1): 48, ("c", 1, 1, 2): 0, ("a", 0, 0): 4, ("c", 2, 1, 0): 10, ("s", 1, 1, 0): 14,
-    ("keep",): 0, ("a", 0, 1): 20, ("w", 0): 24, ("a", 1, 0): 32, ("c", 2, 1, 1): 36,
-    ("s", 1, 1, 1): 42, ("c", 2, 1, 2): 0, ("a", 1, 1): 28, ("s", 2, 1, 0): 4, ("w", 1): 10,
-    ("s", 2, 1, 1): 20, ("w", 2): 48,
+    ("c", 0, 2, 0): 0, ("t", 0, 0): 8, ("c", 0, 2, 1): 14, ("t", 0, 1): 22, ("c", 0, 1, 2): 28,
+    ("t", 1, 0): 32, ("t", 1, 1): 38, ("s", 0, 1, 0): 44, ("s", 0, 1, 1): 48, ("c", 1, 1, 2): 0,
+    ("a", 0, 0): 4, ("c", 2, 1, 0): 8, ("s", 1, 1, 0): 14, ("keep",): 0, ("a", 0, 1): 18,
+    ("w", 0): 22, ("a", 1, 0): 28, ("c", 2, 1, 1): 32, ("s", 1, 1, 1): 38, ("c", 2, 1, 2): 0,
+    ("a", 1, 1): 44, ("s", 2, 1, 0): 4, ("w", 1): 8, ("s", 2, 1, 1): 18, ("w", 2): 48,
+
 }
 
 
@@ -194,7 +194,7 @@ def tile_teacher_student_logits_t1_kernel(
             if done_cols[key] == 512 and key[0] != "z1":
                 release(key)
 
-        depth = {"c512": 6, "w512": 3, "z1512": 6, "t256": 4, "t512": 4, "a512": 4, "z2256": 11, "z2512": 2}
+        depth = {"c512": 7, "w512": 3, "z1512": 6, "t256": 4, "t512": 4, "a512": 4, "z2256": 9, "z2512": 2}
 
         def quantise(*keys):
             for key in keys:
@@ -398,22 +398,23 @@ def tile_teacher_student_logits_t1_kernel(
             return first, second
 
         interleave("vector", ("c", 0, 0))
-        runs = turn_teacher(0, 0)
-        quantise(("c", 0, 0))
-        interleave("vector", ("c", 0, 1))
-        quantise(runs[0], ("c", 0, 1), runs[1])
-        runs = turn_teacher(0, 1)
-        mm1(0, (0, 1))
-        interleave("vector", ("c", 0, 2))
-        quantise(runs[0], ("c", 0, 2))
-        mm1(0, (2,))
-        quantise(runs[1])
-        mm1(1)
         interleave("scalar", ("c", 1, 0))
+        runs = turn_teacher(0, 0)
+        quantise(("c", 0, 0), ("c", 1, 0), *runs)
+        mm1(0, (0,))
+        interleave("vector", ("c", 0, 1))
         interleave("scalar", ("c", 1, 1))
+        quantise(("c", 0, 1))
+        runs = turn_teacher(0, 1)
+        mm1(0, (1,))
+        quantise(("c", 1, 1))
+        interleave("vector", ("c", 0, 2))
+        quantise(runs[0], ("c", 0, 2), runs[1])
         runs = turn_teacher(1, 0)
+        mm1(0, (2,))
+        mm1(1)
         later = turn_teacher(1, 1)
-        quantise(("c", 1, 0), ("c", 1, 1), *runs)
+        quantise(*runs)
         mm1(2)
         add1(0)
         add1(1)

from contextlib import ExitStack

import concourse.mybir as mybir
from concourse.masks import make_identity

B, C, G, J = 1024, 1536, 3, 512
P = 128
FLOPS = 2 * B * C * C + 2 * B * B * C + 2 * B * C * J

F32 = mybir.dt.float32
BF16 = mybir.dt.bfloat16
U32 = mybir.dt.uint32
U8 = mybir.dt.uint8
FP8X4 = mybir.dt.float8_e4m3fn_x4
MULT = mybir.AluOpType.mult
ADD = mybir.AluOpType.add

KIB = 1024
PLACE = 4 * KIB
LOAD_PLACES = 13
WORK_PLACES = 12
LOADS = {
    ("c", 0, 2, 0): 0, ("t", 0, 0): 8, ("c", 0, 2, 1): 14, ("t", 0, 1): 22, ("c", 0, 1, 2): 28,
    ("t", 1, 0): 32, ("t", 1, 1): 38, ("s", 0, 1, 0): 44, ("s", 0, 1, 1): 48, ("c", 1, 1, 2): 0,
    ("a", 0, 0): 4, ("c", 2, 1, 0): 8, ("s", 1, 1, 0): 14, ("keep",): 0, ("a", 0, 1): 18,
    ("w", 0): 22, ("a", 1, 0): 28, ("c", 2, 1, 1): 32, ("s", 1, 1, 1): 38, ("c", 2, 1, 2): 0,
    ("a", 1, 1): 44, ("s", 2, 1, 0): 4, ("w", 1): 8, ("s", 2, 1, 1): 18, ("w", 2): 48,

}


def tile_teacher_student_logits_t1_kernel(
    tc, student, teacher, confusion, affinity, keep, within, gain, out
):
    nc = tc.nc
    with ExitStack() as ctx:
        raw = ctx.enter_context(tc.tile_pool(name="raw", bufs=1))
        sbuf = ctx.enter_context(tc.tile_pool(name="sbuf", bufs=1))
        psum = ctx.enter_context(tc.psum_pool(name="psum", bufs=1))
        ctx.enter_context(tc.manual_schedule())

        counts = {}
        banks = {}
        bank_of = {}
        free_banks = list(range(8))
        turn_banks = []
        list_of = {}
        free_work = list(range(LOAD_PLACES, LOAD_PLACES + WORK_PLACES))
        place_of = {}

        def label(key):
            return "_".join(str(x) for x in key)

        def ring(name, depth, shape, dtype):
            n = counts.get(name, 0)
            counts[name] = n + 1
            tag = name + str(n % depth)
            return sbuf.tile(shape, dtype, name=tag, tag=tag, align_bytes=64)

        def placed(name, place, shape, dtype):
            return raw.tile(shape, dtype, name=name, tag=name, align_bytes=64, offset=place)

        def work_tile(key, shape, dtype, newest=False):
            place_of[key] = free_work.pop(-1 if newest else 0)
            return placed("work_" + label(key), place_of[key] * PLACE, shape, dtype)

        def take_bank(key, shape):
            free = turn_banks if turn_banks and (key[0] in ("a", "z2t") or len(key) == 2) else free_banks
            bank_of[key] = free.pop(0)
            list_of[key] = free
            tag = "bank" + str(bank_of[key])
            banks[key] = psum.tile(shape, F32, name=tag, tag=tag)
            return banks[key]

        def give_bank(key):
            list_of[key].append(bank_of[key])

        teacher_v = teacher.rearrange("(g p t) k -> g p t k", p=P, t=4)
        affinity_v = affinity.rearrange("(g p t) k -> g p t k", p=P, t=4)
        student_v = student.rearrange("(g p t) c -> g p t c", p=P, t=4)
        confusion_v = confusion.rearrange("(c p j) n -> c p j n", p=P, j=4)
        within_v = within.rearrange("(h p j) n -> h p j n", p=P, j=4)
        out_v = out.rearrange("(g p t) c -> g p t c", p=P, t=4)

        loaded = {}
        words = {}
        sorted_words = {}
        grouped = {}
        done_cols = {}
        parts = {}
        codes = {}
        scales = {}
        z = {}
        gained = {}

        def load(key):
            name = "raw_" + label(key)
            place = LOADS[key] * KIB
            if key[0] in ("c", "s"):
                source = confusion_v if key[0] == "c" else student_v
                first, count, n = key[1:]
                t = placed(name, place, [P, 4, 512 * count], BF16)
                nc.sync.dma_start(out=t[:], in_=source[n, :, :, first * 512 : (first + count) * 512])
                for h in range(count):
                    loaded[key[0], first + h, n] = t[:, :, h * 512 : (h + 1) * 512]
                    load_of[key[0], first + h, n] = key
            if key[0] in ("t", "a"):
                g, q = key[1:]
                source = teacher_v if key[0] == "t" else affinity_v
                width = source.shape[-1]
                t = placed(name, place, [P, 2 * width], BF16)
                nc.sync.dma_start(out=t[:], in_=source[g, :, 2 * q : 2 * q + 2, :].rearrange("p a k -> p (a k)"))
                loaded[key] = t[:].bitcast(F32).rearrange("p (a k) -> p a k", a=2)
                for c in range(width // 512):
                    words[key + (c,)] = loaded[key][:, :, 256 * c : 256 * (c + 1)]
            if key[0] == "w":
                t = placed(name, place, [P, 4 * 512], BF16)
                nc.sync.dma_start(out=t[:], in_=within_v[key[1]].rearrange("p j n -> p (j n)"))
                loaded[key] = t[:].rearrange("p (j n) -> p j n", j=4)
            if key[0] == "keep":
                nc.sync.dma_start(out=keep_sb[:, :, 0:4], in_=keep.rearrange("(g p t) -> p g t", p=P, t=4))

        def kib(key):
            return {"t": 6, "keep": 0}.get(key[0], 4 * key[2] if len(key) == 4 else 4)

        pending = list(LOADS)
        unread = {}
        load_of = {}

        def load_more():
            while pending:
                key = pending[0]
                if any(LOADS[k] < LOADS[key] + kib(key) and LOADS[key] < LOADS[k] + kib(k) for k in unread):
                    return
                load(pending.pop(0))
                if kib(key):
                    unread[key] = key[2] if len(key) == 4 else 1

        def release(key):
            key = load_of.get(key, key)
            unread[key] = unread[key] - 1
            if unread[key] == 0:
                unread.pop(key)
                load_more()

        ident = sbuf.tile([P, P], F32, name="ident", tag="ident")
        keep_sb = sbuf.tile([P, 2, 16], BF16, name="keep_sb", tag="keep_sb")
        gain_in = sbuf.tile([P, 12], BF16, name="gain_in", tag="gain_in")
        gain_sb = sbuf.tile([P, 2, 768], BF16, name="gain_sb", tag="gain_sb", align_bytes=64)

        def spread_gain(u):
            bank = take_bank(("gain", u), [P, 3, P])
            for j in range(3):
                word = gain_in[:].bitcast(F32)[:, 2 * j + u : 2 * j + u + 1]
                nc.tensor.transpose(bank[:, j, :], word.to_broadcast([P, P]), ident[:])

        def fetch_gain(u):
            nc.scalar.copy(
                out=gain_sb[:, u, :].bitcast(F32).rearrange("p (n j) -> p n j", j=3),
                in_=banks["gain", u][:].rearrange("p j n -> p n j"),
            )
            give_bank(("gain", u))

        def gain_of(h):
            return gain_sb[:, :, 256 * h : 256 * (h + 1)]

        def copy_on(engine, o, s):
            if engine == "vector":
                nc.vector.tensor_copy(out=o, in_=s)
            else:
                nc.scalar.copy(out=o, in_=s)

        def interleave(engine, key, start=0, stop=512, newest=False):
            cols = slice(start, stop)
            if key not in grouped:
                grouped[key] = work_tile(key, [P, 512, 4], BF16, newest)
            src = z[key[1:]] if key[0] == "z1" else loaded[key]
            if engine == "gpsimd":
                nc.gpsimd.tensor_scalar(
                    out=grouped[key][:, cols, :],
                    in0=src[:, :, cols].rearrange("p t n -> p n t"),
                    scalar1=1.0,
                    scalar2=0.0,
                    op0=MULT,
                    op1=ADD,
                )
            else:
                copy_on(
                    engine,
                    grouped[key][:, cols, :].rearrange("p (n i) t -> p n t i", i=4),
                    src[:, :, cols].rearrange("p t (n i) -> p n t i", i=4),
                )
            done_cols[key] = done_cols.get(key, 0) + stop - start
            if done_cols[key] == 512 and key[0] != "z1":
                release(key)

        depth = {"c512": 7, "w512": 3, "z1512": 6, "t256": 4, "t512": 4, "a512": 4, "z2256": 9, "z2512": 2}

        def quantise(*keys):
            for key in keys:
                width = grouped[key].shape[1]
                name = key[0] + str(width)
                codes[key] = ring(name + "codes", depth[name], [P, width], U32)
                scales[key] = ring(name + "scales", depth[name], [P, width], U8)
                share = width // len(parts.get(key, [key]))
                for n, part in enumerate(parts.get(key, [])):
                    codes[part] = codes[key][:, n * share : (n + 1) * share]
                    scales[part] = scales[key][:, n * share : (n + 1) * share]
                nc.vector.quantize_mx(
                    out=codes[key][:].bitcast(FP8X4),
                    scales=scales[key][:],
                    in_=grouped[key][:].rearrange("p n t -> p (n t)"),
                )
                free_work.append(place_of[key])

        def z_tile(h, g):
            tag = "z" + str(h) + str(g)
            return sbuf.tile([P, 4, 512], F32, name=tag, tag=tag, align_bytes=64)

        def sort_words(engine, key, h, g):
            n = loaded[key].shape[2] // 256
            tag = "z" + str(h) + str(g)
            ordered = sbuf.tile([P, 2 * n, 2, P], F32, name=tag, tag=tag, align_bytes=64)
            copy_on(engine, ordered[:], loaded[key].rearrange("p a (c m u) -> p (a c) u m", c=n, u=2))
            for c in range(n):
                sorted_words[key + (c,)] = ordered[:, c : 2 * n : n]

        def turn(*keys):
            run = (keys[0][0], "run", *keys)
            parts[run] = keys
            for key in keys:
                take_bank(key, [P, 2, 2, P])
                for a in range(2):
                    for u in range(2):
                        src = sorted_words[key][:, a, u] if key in sorted_words else words[key][:, a, u:256:2]
                        nc.tensor.transpose(banks[key][:, a, u, :], src, ident[:])
            return run

        def fetch(run, engines=("scalar", "scalar")):
            keys = parts[run]
            grouped[run] = work_tile(run, [P, 256 * len(keys), 4], BF16)
            for n, key in enumerate(keys):
                copy_on(
                    engines[n],
                    grouped[run][:, 256 * n : 256 * (n + 1), :].bitcast(F32).rearrange("p (a r) u -> p a r u", a=2),
                    banks[key][:].rearrange("p a u r -> p a r u"),
                )
                give_bank(key)
            return run

        def product(bank, left, cols, right, start, stop):
            nc.tensor.matmul_mx(
                out=bank[:],
                lhsT=codes[left][:, cols].bitcast(FP8X4),
                lhsT_scale=scales[left][:, cols],
                rhs=codes[right][:].bitcast(FP8X4),
                rhs_scale=scales[right][:],
                start=start,
                stop=stop,
            )

        def pair(s):
            return s // 4, s // 2 % 2, s % 2

        def passes(name, s, which, total, left, right, tiles):
            h, g, q = pair(s)
            for a in reversed(tiles):
                for c in which:
                    n = counts.get((name, s, a), 0)
                    counts[name, s, a] = n + 1
                    if n == 0:
                        take_bank((name, s, a), [P, 512])
                    product(banks[name, s, a], (left, g, q, c), slice(a * P, (a + 1) * P), (right, h, c), n == 0, n == total - 1)

        def mm1(s, which=(0, 1, 2), tiles=(0, 1)):
            passes("z1", s, which, 3, "t", "c", tiles)

        def add1(s, tiles=(0, 1)):
            h, g, q = pair(s)
            if (h, g) not in z:
                z[h, g] = z_tile(h, g)
            for a in tiles:
                t = 2 * q + a
                nc.vector.tensor_tensor(
                    out=z[h, g][:, t, :].rearrange("p (u m e) -> p m u e", u=2, e=2),
                    in0=banks["z1", s, a][:].rearrange("p (m u e) -> p m u e", u=2, e=2),
                    in1=loaded["s", h, g][:, t, :].rearrange("p (m u e) -> p m u e", u=2, e=2),
                    op=ADD,
                )
                give_bank(("z1", s, a))
                if t == 3:
                    release(("s", h, g))

        def mm2(s, which=(0, 1), tiles=(0, 1)):
            passes("z2", s, which, 2, "a", "z1", tiles)

        def add2(s, tiles=(0, 1)):
            h, g, q = pair(s)
            for a in tiles:
                t = 2 * q + a
                nc.vector.scalar_tensor_tensor(
                    out=z[h, g][:, t, :],
                    in0=z[h, g][:, t, :],
                    scalar=keep_sb[:, g, t : t + 1],
                    in1=banks["z2", s, a][:],
                    op0=MULT,
                    op1=ADD,
                )
                give_bank(("z2", s, a))

        def z2_of(s):
            h, g, q = pair(s)
            return z[h, g][:, 2 * q : 2 * q + 2, :]

        def gain_mul(s, newest=False):
            pair_tile = work_tile(("gained", s), [P, 2, 512], F32, newest)
            for a in range(2):
                gained[s, a] = pair_tile[:, a, :]
            nc.gpsimd.tensor_tensor(
                out=pair_tile[:].rearrange("p a (u n) -> p a u n", u=2),
                in0=z2_of(s).rearrange("p a (u n) -> p a u n", u=2),
                in1=gain_of(s // 4).unsqueeze(1).to_broadcast([P, 2, 2, 256]),
                op=MULT,
            )

        def gain_mul_tile(s, a, engine, newest=False):
            gained[s, a] = work_tile(("gained", s, a), [P, 512], F32, newest)[:]
            engine.tensor_tensor(
                out=gained[s, a].rearrange("p (u n) -> p u n", u=2),
                in0=z2_of(s)[:, a, :].rearrange("p (u n) -> p u n", u=2),
                in1=gain_of(s // 4),
                op=MULT,
            )

        def round2(s):
            rounded = ring("rounded", 3, [P, 2, 512], BF16)
            nc.scalar.copy(out=rounded[:], in_=z2_of(s))
            sorted_words["z2", s] = rounded[:].bitcast(F32).rearrange("p a (u m) -> p a u m", u=2)

        def turn2(*pairs):
            return turn(*[("z2", s) for s in pairs])

        def turn2_unrounded(s):
            grouped["z2", s] = work_tile(("z2", s), [P, 2 * P, 4], BF16)
            for a in (0, 1):
                bank = take_bank(("z2t", s, a), [P, 4, P])
                for t in range(4):
                    start = t // 2 * 256 + t % 2
                    nc.tensor.transpose(bank[:, t, :], z2_of(s)[:, a, start : t // 2 * 256 + 256 : 2], ident[:])
                nc.scalar.copy(
                    out=grouped["z2", s][:, a * P : (a + 1) * P, :], in_=bank[:].rearrange("p t n -> p n t")
                )
                give_bank(("z2t", s, a))
            return ("z2", s)

        def mm3(*tiles):
            for s, a in reversed([divmod(i, 2) for i in tiles]):
                take_bank(("out", s, a), [P, 512])
                product(banks["out", s, a], ("z2", s), slice(a * P, (a + 1) * P), ("w", s // 4), True, True)

        def add3(*tiles, single=False):
            for s, a in [divmod(i, 2) for i in tiles]:
                nc.vector.tensor_tensor(
                    out=z2_of(s)[:, a, :].rearrange("p (m u e) -> p m u e", u=2, e=2),
                    in0=banks["out", s, a][:].rearrange("p (m u e) -> p m u e", u=2, e=2),
                    in1=gained[s, a].rearrange("p (u m e) -> p m u e", u=2, e=2),
                    op=ADD,
                )
                give_bank(("out", s, a))
                counts["added", s] = counts.get(("added", s), 0) + 1
                if counts["added", s] == 2 and ("gained", s) in place_of:
                    free_work.append(place_of["gained", s])
                if single or counts["added", s] == 2:
                    h, g, q = pair(s)
                    rows = slice(a, a + 1) if single else slice(0, 2)
                    nc.sync.dma_start(
                        out=out_v[g, :, 2 * q + rows.start : 2 * q + rows.stop, h * 512 : (h + 1) * 512],
                        in_=z2_of(s)[:, rows, :],
                    )

        def turn_affinity(n):
            run = turn(("a", n // 2, n % 2, 0), ("a", n // 2, n % 2, 1))
            release(("a", n // 2, n % 2))
            return run

        nc.sync.dma_start(out=gain_in[:], in_=gain.rearrange("(n i) -> n i", i=12))
        load_more()
        make_identity(nc, ident[:])
        for u in range(2):
            spread_gain(u)
        for u in range(2):
            fetch_gain(u)

        def turn_teacher(g, q):
            first = fetch(turn(("t", g, q, 0), ("t", g, q, 1)))
            second = fetch(turn(("t", g, q, 2)))
            release(("t", g, q))
            return first, second

        interleave("vector", ("c", 0, 0))
        interleave("scalar", ("c", 1, 0))
        runs = turn_teacher(0, 0)
        quantise(("c", 0, 0), ("c", 1, 0), *runs)
        mm1(0, (0,))
        interleave("vector", ("c", 0, 1))
        interleave("scalar", ("c", 1, 1))
        quantise(("c", 0, 1))
        runs = turn_teacher(0, 1)
        mm1(0, (1,))
        quantise(("c", 1, 1))
        interleave("vector", ("c", 0, 2))
        quantise(runs[0], ("c", 0, 2), runs[1])
        runs = turn_teacher(1, 0)
        mm1(0, (2,))
        mm1(1)
        later = turn_teacher(1, 1)
        quantise(*runs)
        mm1(2)
        add1(0)
        add1(1)
        interleave("vector", ("z1", 0, 0))
        interleave("scalar", ("c", 1, 2))
        quantise(*later)
        mm1(3)
        quantise(("z1", 0, 0))
        interleave("gpsimd", ("c", 2, 0), 208, 512, True)
        interleave("scalar", ("c", 2, 0), 0, 208)
        a0 = fetch(turn_affinity(0))
        mm1(4, (0, 1))
        add1(2)
        a1 = turn_affinity(1)
        add1(3)
        quantise(("c", 1, 2))
        mm1(4, (2,))
        interleave("vector", ("z1", 0, 1), 0, 320)
        interleave("scalar", ("z1", 0, 1), 320, 512)
        fetch(a1)
        interleave("scalar", ("w", 0))
        quantise(a0)
        mm2(0, (0,))
        quantise(("z1", 0, 1))
        mm2(0, (1,))
        a2 = turn_affinity(2)
        quantise(("c", 2, 0), a1)
        mm1(5)
        interleave("gpsimd", ("c", 2, 1), 208, 512, True)
        fetch(a2)
        interleave("scalar", ("c", 2, 1), 0, 208)
        add1(4)
        add2(0)
        round2(0)
        interleave("scalar", ("c", 2, 2))
        mm2(1)
        mm1(6)
        quantise(("w", 0), a2, ("c", 2, 1))
        gain_mul(0, True)
        add1(5)
        z0 = fetch(turn2(0))
        interleave("scalar", ("z1", 1, 0))
        add2(1)
        mm2(2)
        add1(6)
        mm1(7)
        a3 = fetch(turn_affinity(3))
        quantise(z0)

        turn_banks.extend([free_banks.pop(), free_banks.pop()])
        first_pair = {s: s + 5 for s in range(2, 7)}
        interleaved = {2: [("z1", 1, 1)], 3: [("w", 1)], 4: [("z1", 2, 0)], 6: [("z1", 2, 1)], 8: [("w", 2)]}
        quantised = {2: [a3, ("c", 2, 2), ("z1", 1, 0)], 3: [("z1", 1, 1)], 5: [("z1", 2, 0)], 6: [("w", 1)], 7: [("z1", 2, 1)], 9: [("w", 2)]}
        rounds = {2: (1,), 3: (2,), 4: (3,), 5: (4, 5), 7: (6, 7), 8: (8,), 9: (9,), 10: (10,)}
        last_tiles = {s: (s - 2,) if s < 7 else (3 * s - 16, 3 * s - 15, 3 * s - 14) for s in range(2, 12)}
        turned = {3: (1,), 4: (2,), 5: (3,), 6: (4,), 7: (5,), 8: (6, 7), 9: (8,), 10: (9,), 11: (10,)}
        for s in range(2, 12):
            gain_mul(s - 1, True)
            run = []
            mm3(*[i for i in last_tiles[s] if ("out", i // 2, i % 2) not in banks])
            if s in turned:
                run = [fetch(turn2(*turned[s]))]
            for k in rounds.get(s, ()):
                if k < s:
                    round2(k)
            tiles = list(last_tiles[s])
            if s == 3:
                add3(tiles.pop(0))
            if s in first_pair and s > 3:
                add1(first_pair[s])
                if s < 6:
                    mm1(first_pair[s] + 1)
            if s == 8:
                add3(tiles.pop(0), tiles.pop(0))
            add2(s)
            if s == 3:
                add1(8)
                mm1(9)
            if s == 2:
                add1(7)
                mm1(8, (0, 1))
            if s in (3, 7):
                mm2(s + 1, (0,))
            elif 2 < s < 11:
                mm2(s + 1)
            if s in rounds.get(s, ()):
                round2(s)
            for key in interleaved.get(s, []):
                interleave("scalar", key)
            add3(*tiles)
            if s < 11:
                mm3(*[i for i in last_tiles[s + 1] if ("z2", i // 2) in codes and ("w", i // 8) in codes])
            for key in quantised.get(s, []):
                quantise(key)
                if key == a3:
                    mm2(3)
                if key == ("c", 2, 2):
                    mm1(8, (2,))
                if key in (("z1", 1, 1), ("z1", 2, 1)):
                    mm2(s + 1, (1,))
            quantise(*run)
        last = turn2_unrounded(11)
        mm3(20, 21)
        gain_mul_tile(11, 1, nc.vector)
        quantise(last)
        gain_mul_tile(11, 0, nc.gpsimd, True)
        mm3(22, 23)
        for i in (20, 21, 23, 22):
            add3(i, single=True)
